import numpy as np
import ml_dtypes


def mxq(x, axis, fmt="e4m3"):
    dtype, down = {"e4m3": (ml_dtypes.float8_e4m3fn, 7), "e5m2": (ml_dtypes.float8_e5m2, 14)}[fmt]
    v = np.moveaxis(np.asarray(x, np.float32).astype(ml_dtypes.bfloat16).astype(np.float64), axis, -1)
    blocks = v.reshape(v.shape[:-1] + (-1, 32))
    amax = np.abs(blocks).max(-1, keepdims=True)
    byte = np.maximum(np.where(amax > 0, np.frexp(amax)[1] - 1 + 127, 0) - down, 1)
    scale = np.exp2(byte - 127.0)
    codes = (blocks / scale).astype(np.float32).astype(dtype).astype(np.float64)
    return np.moveaxis((codes * scale).reshape(v.shape), -1, axis)


WIDE = False


def mx_kscale(k):
    if not WIDE:
        return np.ones(k)
    levels = np.array([10, -10, 5, -5, 0])
    if k % 512:
        return np.exp2(np.random.permutation(np.resize(levels, k // 32))).repeat(32)
    a = np.empty((k // 512, 16))
    for p in range(k // 512):
        a[p, :8] = np.random.permutation(np.resize(levels, 8))
        for g in range(8):
            far = levels[np.abs(levels - a[p, g]) >= 10]
            a[p, g + 8] = far[np.random.randint(len(far))]
    return np.exp2(a.ravel()).repeat(32)


def f64(x):
    return np.asarray(x).astype(np.float64)


def striped(idx):
    return np.tile(idx.reshape(-1, 16).T, (8, 1)).astype(np.uint16)


def unstriped(offs):
    return offs[:16].T.reshape(-1).astype(np.int64)


E2M1 = np.array([0.0, 0.5, 1.0, 1.5, 2.0, 3.0, 4.0, 6.0, -0.0, -0.5, -1.0, -1.5, -2.0, -3.0, -4.0, -6.0])


def pack_weight(w, fmt):
    k, n = w.shape
    w = f64(np.asarray(w, np.float32).astype(ml_dtypes.bfloat16)).reshape(k // 32, 32, n)
    amax = np.abs(w).max(1)
    if fmt == "e4m3":
        byte = np.frexp(amax)[1] - 1 + 127 - 7
    else:
        mant, ex = np.frexp(amax / 6.0)
        byte = np.where(mant > 0.5, ex, ex - 1) + 127
    byte = np.clip(np.where(amax > 0, byte, 1), 1, 254)
    scaled = (w * np.exp2(127.0 - byte)[:, None, :]).reshape(k, n).astype(np.float32)
    by_word = np.ascontiguousarray(scaled.reshape(k // 512, 128, 4, n).transpose(0, 1, 3, 2))
    if fmt == "e4m3":
        words = by_word.astype(ml_dtypes.float8_e4m3fn).view(np.uint8)
    else:
        c = by_word.astype(ml_dtypes.float4_e2m1fn).view(np.uint8) & 0xF
        words = (c[..., 0::2] | (c[..., 1::2] << 4)).reshape(k // 512, 128, 2 * n)
    return np.ascontiguousarray(words), np.ascontiguousarray(byte.astype(np.uint8).reshape(k // 512, 16, n))


def unpack_weight(words, scales, fmt):
    g, _, n = scales.shape
    words = np.ascontiguousarray(words).reshape(g, 128, n, -1)
    if fmt == "e4m3":
        vals = words.view(ml_dtypes.float8_e4m3fn).astype(np.float64)
    else:
        nib = np.empty((g, 128, n, 4), np.uint8)
        nib[..., 0::2] = words & 0xF
        nib[..., 1::2] = words >> 4
        vals = E2M1[nib]
    vals = vals * np.repeat(np.exp2(scales.astype(np.float64) - 127.0), 8, axis=1)[..., None]
    return vals.transpose(0, 1, 3, 2).reshape(g * 512, n)


def d_silu(v):
    s = 1.0 / (1.0 + np.exp(-np.maximum(v, -700.0)))
    return s * (1.0 + v * (1.0 - s))


K, T, G, C1, E, C2, H = 256, 768, 3, 256, 6, 128, 512
N = 512


def by_expert(wq, xq, E, C):
    return np.concatenate([wq[e].T @ xq[:, e * C:(e + 1) * C] for e in range(E)], axis=1)


def setup_inputs():
    n = np.random.standard_normal
    v = mx_kscale(N)
    u = mx_kscale(H)
    slots1 = np.random.permutation(T)
    slots2 = np.concatenate([q * C1 + np.random.permutation(C1) for q in range(G)])
    dy = pack_weight(n((N, T)) * v[:, None], "e4m3")
    wet = [pack_weight(m, "e2m1") for m in n((E, N, H)) / np.sqrt(N) / v[None, :, None] * u]
    return {
        "dy_words": dy[0],
        "dy_scales": dy[1],
        "wet_words": np.stack([m[0] for m in wet]),
        "wet_scales": np.stack([m[1] for m in wet]),
        "wgt": (n((G, H, K)) / np.sqrt(H) / u[None, :, None]).astype(np.float32),
        "a": (n((H, T))).astype(np.float32),
        "gate": (np.tile(np.random.uniform(0.2, 1.0, T), (128, 1))).astype(np.float32),
        "offs": striped(slots1),
        "offs2": striped(slots2),
        "dst": striped(slots1[slots2]),
    }


def reference(dy_words, dy_scales, wet_words, wet_scales, wgt, a, gate, offs, offs2, dst):
    wet = np.stack([unpack_weight(wet_words[e], wet_scales[e], "e2m1") for e in range(E)])
    wgtq = mxq(f64(wgt), 1, "e4m3")
    gq = unpack_weight(dy_words, dy_scales, "e4m3")[:, unstriped(dst)]
    z = f64(gate[:1]) * by_expert(wet, gq, E, C2)
    da = np.zeros((H, T))
    da[:, unstriped(offs2)] = z
    dx = by_expert(wgtq, mxq(da * d_silu(f64(a)), 0, "e4m3"), G, C1)
    out = np.zeros((K, T))
    out[:, unstriped(offs)] = dx
    return out

@@ -1,0 +1,195 @@
+from contextlib import ExitStack
+
+import concourse.mybir as mybir
+from concourse.masks import make_identity
+
+K, T, G, C1, E, C2, H, N = 256, 768, 3, 256, 6, 128, 512, 512
+FLOPS = 2 * T * N * H + 2 * T * H * K
+P = 128
+F32 = mybir.dt.float32
+BF16 = mybir.dt.bfloat16
+I32 = mybir.dt.int32
+U32 = mybir.dt.uint32
+U16 = mybir.dt.uint16
+U8 = mybir.dt.uint8
+FP8X4 = mybir.dt.float8_e4m3fn_x4
+FP4X4 = mybir.dt.float4_e2m1fn_x4
+ACT = mybir.ActivationFunctionType
+ALU = mybir.AluOpType
+D_ENG = "vector"
+M_ENG = "vector"
+W_ENG = "scalar"
+
+
+def tile_moe_hib_silu_kernel(tc, dy_words, dy_scales, wet_words, wet_scales, wgt, a, gate, offs, offs2, dst, out):
+    nc = tc.nc
+    with ExitStack() as ctx:
+        held = ctx.enter_context(tc.tile_pool(name="held", bufs=1))
+        ring = ctx.enter_context(tc.tile_pool(name="ring", bufs=2))
+        psum = ctx.enter_context(tc.psum_pool(name="psum", bufs=2))
+
+        dst_t = held.tile([P, T // 16], U16, name="dst_t")
+        offs2_t = held.tile([P, T // 16], U16, name="offs2_t")
+        offs_t = held.tile([P, T // 16], U16, name="offs_t")
+        dyw = held.tile([P, T], I32, name="dyw", align_bytes=64)
+        dys = held.tile([P, T], U8, name="dys", align_bytes=64)
+        wetw = held.tile([P, E, 2 * H], U8, name="wetw", align_bytes=64)
+        wets = held.tile([P, E, H], U8, name="wets", align_bytes=64)
+        gcol = held.tile([P, E], F32, name="gcol")
+        a_t = held.tile([P, 4, T], F32, name="a_t")
+        wraw = held.tile([P, G, 4, K], F32, name="wraw")
+        ident = held.tile([P, P], F32, name="ident")
+
+        nc.vector.memset(dys[:].bitcast(I32), 0)
+        nc.vector.memset(wets[:].rearrange("p e h -> p (e h)").bitcast(I32), 0)
+        warm = held.tile([P, 2], F32, name="warm")
+        nc.vector.memset(warm[:, 0:1], 0.0)
+        nc.scalar.activation(warm[:, 1:2], warm[:, 0:1], ACT.Silu)
+        make_identity(nc, ident[:])
+
+        nc.sync.dma_start(dst_t[:], dst)
+        nc.sync.dma_start(dyw[:], dy_words[0].rearrange("p t d -> p (t d)").bitcast(I32))
+        for r in range(4):
+            nc.sync.dma_start(dys[r:P:32, :].bitcast(I32), dy_scales[0, r:16:4, :].bitcast(I32))
+        nc.sync.dma_start(wetw[:, 0:2, :].bitcast(I32), wet_words[0:2, 0].rearrange("e p b -> p e b").bitcast(I32))
+        for r in range(4):
+            nc.sync.dma_start(wets[r:P:32, :, :].bitcast(I32), wet_scales[:, 0, r:16:4, :].rearrange("e q h -> q e h").bitcast(I32))
+        with nc.allow_non_contiguous_dma(reason="one gate value a partition"):
+            nc.sync.dma_start(gcol[:], gate[0].rearrange("(e p) -> p e", p=P))
+        nc.sync.dma_start(offs2_t[:], offs2)
+        nc.sync.dma_start(wetw[:, 2:E, :].bitcast(I32), wet_words[2:E, 0].rearrange("e p b -> p e b").bitcast(I32))
+        nc.sync.dma_start(a_t[:], a.rearrange("(p t) j -> p t j", t=4))
+        for g in range(G):
+            nc.sync.dma_start(wraw[:, g], wgt[g].rearrange("(p t) k -> p t k", t=4))
+        nc.sync.dma_start(offs_t[:], offs)
+
+        pieces = [(0, 128), (128, 256), (256, 768)]
+        gw, gs = {}, {}
+        for lo, hi in pieces:
+            w = held.tile([P, hi - lo], U32, name="gw%d" % lo, align_bytes=64)
+            s = held.tile([P, hi - lo], U8, name="gs%d" % lo, align_bytes=64)
+            o = dst_t[:, lo // 16 : hi // 16]
+            nc.vector.tensor_copy(w[:], dyw[:].bitcast(U32).indirect(o))
+            nc.vector.tensor_copy(s[:], dys[:].indirect(o))
+            for e in range(lo // C2, hi // C2):
+                gw[e] = w[:, e * C2 - lo : (e + 1) * C2 - lo]
+                gs[e] = s[:, e * C2 - lo : (e + 1) * C2 - lo]
+
+        zt = [held.tile([P, 4, C1], F32, name="zt%d" % g) for g in range(G)]
+
+        def expert(e):
+            acc = psum.tile([P, H], F32, name="acc1")
+            nc.tensor.matmul_mx(out=acc[:], lhsT=gw[e].bitcast(FP8X4), lhsT_scale=gs[e],
+                                rhs=wetw[:, e, :].bitcast(FP4X4), rhs_scale=wets[:, e, :], start=True, stop=True)
+            y = ring.tile([P, 4, P], F32, name="y")
+            nc.scalar.activation(y[:], acc[:].rearrange("s (m t) -> s t m", t=4), ACT.Copy, scale=gcol[:, e : e + 1])
+            turned = psum.tile([P, 4, P], F32, name="turned")
+            for t in range(4):
+                nc.tensor.transpose(turned[:, t, :], y[:, t, :], ident[:])
+            h = e % 2
+            nc.scalar.copy(zt[e // 2][:, :, h * C2 : (h + 1) * C2], turned[:])
+
+        zs = [[held.tile([P, T], F32, name="zs%d_%d" % (g, t)) for t in range(4)] for g in range(G)]
+
+        def scatter_z(g, t, lo, hi):
+            o = offs2_t[:, (g * C1 + lo) // 16 : (g * C1 + hi) // 16]
+            nc.vector.tensor_copy(zs[g][t][:].indirect(o), zt[g][:, t, lo:hi])
+
+        q_t = held.tile([P, G, 4, C1], F32, name="q_t")
+        sg_t = held.tile([P, G, 4, C1], F32, name="sg_t")
+        d_t = held.tile([P, G, 4, C1], F32, name="d_t")
+        planes = [held.tile([P, 4, C1], BF16, name="planes%d" % g) for g in range(G)]
+        qin = [held.tile([P, K + C1, 4], BF16, name="qin%d" % g, align_bytes=64) for g in range(G)]
+        codes = [held.tile([P, K + C1], U32, name="codes%d" % g, align_bytes=64) for g in range(G)]
+        scales = [held.tile([P, K + C1], U8, name="scales%d" % g, align_bytes=64) for g in range(G)]
+        dx = [held.tile([P, 2, C1], F32, name="dx%d" % g) for g in range(G)]
+        outw = [held.tile([P, T], F32, name="outw%d" % k) for k in range(2)]
+
+        def silu(g):
+            nc.scalar.activation(q_t[:, g], a_t[:, :, g * C1 : (g + 1) * C1], ACT.Silu, scale=-1.0)
+            if D_ENG != "vector":
+                nc.scalar.activation(q_t[:, g], q_t[:, g], ACT.Identity, scale=-1.0, bias=1.0)
+
+        def sigmoid(g):
+            nc.scalar.activation(sg_t[:, g], a_t[:, :, g * C1 : (g + 1) * C1], ACT.Sigmoid)
+
+        def dsilu(g):
+            if D_ENG == "vector":
+                nc.vector.scalar_tensor_tensor(d_t[:, g], q_t[:, g], 1.0, sg_t[:, g], ALU.subtract, ALU.mult)
+            else:
+                for t in range(4):
+                    nc.gpsimd.tensor_tensor(d_t[:, g, t], q_t[:, g, t], sg_t[:, g, t], ALU.mult)
+
+        def mult(g, t):
+            src = zs[g][t][:, g * C1 : (g + 1) * C1]
+            if M_ENG == "vector":
+                nc.vector.scalar_tensor_tensor(planes[g][:, t, :], src, -1.0 if D_ENG == "vector" else 1.0, d_t[:, g, t], ALU.mult, ALU.mult)
+            else:
+                nc.gpsimd.tensor_tensor(planes[g][:, t, :], src, d_t[:, g, t], ALU.mult)
+
+        def weave(dst_ap, src_ap, eng):
+            o = dst_ap.rearrange("p (c i) t -> p c t i", i=4)
+            s = src_ap.rearrange("p t (c i) -> p c t i", i=4)
+            if eng == "scalar":
+                nc.scalar.copy(o, s)
+            else:
+                nc.gpsimd.tensor_scalar(o, s, 1.0, 0.0, ALU.mult, ALU.add)
+
+        def weave_w(g):
+            weave(qin[g][:, 0:K, :], wraw[:, g], W_ENG)
+
+        def weave_da(g):
+            weave(qin[g][:, K:, :], planes[g][:], "scalar")
+
+        def second(g):
+            nc.vector.quantize_mx(out=codes[g][:].bitcast(FP8X4), scales=scales[g][:], in_=qin[g][:].rearrange("p c t -> p (c t)"))
+            acc = psum.tile([P, 2, C1], F32, name="acc2")
+            for k in range(2):
+                nc.tensor.matmul_mx(out=acc[:, k, :], lhsT=codes[g][:, k * P : (k + 1) * P].bitcast(FP8X4), lhsT_scale=scales[g][:, k * P : (k + 1) * P],
+                                    rhs=codes[g][:, K:].bitcast(FP8X4), rhs_scale=scales[g][:, K:], start=True, stop=True)
+            nc.scalar.copy(dx[g][:], acc[:])
+
+        def scatter_dx(g, k):
+            o = offs_t[:, g * C1 // 16 : (g + 1) * C1 // 16]
+            nc.vector.tensor_copy(outw[k][:].indirect(o), dx[g][:, k, :])
+
+        expert(0)
+        expert(1)
+        for h in range(2):
+            for t in range(4):
+                scatter_z(0, t, h * C2, (h + 1) * C2)
+        expert(2)
+        expert(3)
+        for g in range(G):
+            silu(g)
+        expert(4)
+        expert(5)
+        for t in range(4):
+            scatter_z(1, t, 0, C1)
+        for g in range(G):
+            sigmoid(g)
+            dsilu(g)
+        for g in range(2):
+            weave_w(g)
+            for t in range(4):
+                mult(g, t)
+            weave_da(g)
+        weave_w(2)
+        scatter_z(2, 0, 0, C1)
+        second(0)
+        scatter_z(2, 1, 0, C1)
+        second(1)
+        scatter_z(2, 2, 0, C1)
+        scatter_z(2, 3, 0, C1)
+        for t in range(4):
+            mult(2, t)
+        weave_da(2)
+        second(2)
+        scatter_dx(0, 0)
+        scatter_dx(1, 0)
+        scatter_dx(0, 1)
+        scatter_dx(1, 1)
+        scatter_dx(2, 0)
+        nc.sync.dma_start(out[0:P, :], outw[0][:])
+        scatter_dx(2, 1)
+        nc.sync.dma_start(out[P:K, :], outw[1][:])

@@ -3,9 +3,22 @@ from contextlib import ExitStack
 import concourse.mybir as mybir
 from concourse.masks import make_identity
 
-K, T, G, C1, E, C2, H, N = 256, 768, 3, 256, 6, 128, 512, 512
+K, T, H, N = 256, 768, 512, 512
+G, C1 = 3, 256
+E, C2 = 6, 128
 FLOPS = 2 * T * N * H + 2 * T * H * K
+
 P = 128
+PACK = 4
+QUAD = 32
+SCALE_ROWS = 4
+PER_COL = 16
+K_TILES = K // P
+
+GATHER_CUTS = [(0, C2), (C2, 2 * C2), (2 * C2, T)]
+FIRST_EXPERT_CUTS = [(0, 1), (1, PACK)]
+WHOLE = [(0, PACK)]
+
 F32 = mybir.dt.float32
 BF16 = mybir.dt.bfloat16
 I32 = mybir.dt.int32
@@ -16,180 +29,184 @@ FP8X4 = mybir.dt.float8_e4m3fn_x4
 FP4X4 = mybir.dt.float4_e2m1fn_x4
 ACT = mybir.ActivationFunctionType
 ALU = mybir.AluOpType
-D_ENG = "vector"
-M_ENG = "vector"
-W_ENG = "scalar"
 
 
-def tile_moe_hib_silu_kernel(tc, dy_words, dy_scales, wet_words, wet_scales, wgt, a, gate, offs, offs2, dst, out):
+def tile_moe_hib_silu_kernel(
+    tc, dy_words, dy_scales, wet_words, wet_scales, wgt, a, gate, offs, offs2, dst, out
+):
     nc = tc.nc
     with ExitStack() as ctx:
         held = ctx.enter_context(tc.tile_pool(name="held", bufs=1))
         ring = ctx.enter_context(tc.tile_pool(name="ring", bufs=2))
         psum = ctx.enter_context(tc.psum_pool(name="psum", bufs=2))
 
-        dst_t = held.tile([P, T // 16], U16, name="dst_t")
-        offs2_t = held.tile([P, T // 16], U16, name="offs2_t")
-        offs_t = held.tile([P, T // 16], U16, name="offs_t")
-        dyw = held.tile([P, T], I32, name="dyw", align_bytes=64)
-        dys = held.tile([P, T], U8, name="dys", align_bytes=64)
-        wetw = held.tile([P, E, 2 * H], U8, name="wetw", align_bytes=64)
-        wets = held.tile([P, E, H], U8, name="wets", align_bytes=64)
-        gcol = held.tile([P, E], F32, name="gcol")
-        a_t = held.tile([P, 4, T], F32, name="a_t")
-        wraw = held.tile([P, G, 4, K], F32, name="wraw")
+        dst_list = held.tile([P, T // PER_COL], U16, name="dst_list")
+        offs2_list = held.tile([P, T // PER_COL], U16, name="offs2_list")
+        offs_list = held.tile([P, T // PER_COL], U16, name="offs_list")
+        dy_w = held.tile([P, T], I32, name="dy_w", align_bytes=64)
+        dy_s = held.tile([P, T], U8, name="dy_s", align_bytes=64)
+        wet_w = held.tile([P, E, 2 * H], U8, name="wet_w", align_bytes=64)
+        wet_s = held.tile([P, E, H], U8, name="wet_s", align_bytes=64)
+        gate_col = held.tile([P, E], F32, name="gate_col")
+        a_planes = held.tile([P, PACK, T], F32, name="a_planes")
+        wgt_planes = held.tile([P, G, PACK, K], F32, name="wgt_planes")
         ident = held.tile([P, P], F32, name="ident")
 
-        nc.vector.memset(dys[:].bitcast(I32), 0)
-        nc.vector.memset(wets[:].rearrange("p e h -> p (e h)").bitcast(I32), 0)
-        warm = held.tile([P, 2], F32, name="warm")
-        nc.vector.memset(warm[:, 0:1], 0.0)
-        nc.scalar.activation(warm[:, 1:2], warm[:, 0:1], ACT.Silu)
+        nc.vector.memset(wet_s[:].rearrange("p e h -> p (e h)").bitcast(I32), 0)
+        zero = held.tile([P, 2], F32, name="zero")
+        nc.vector.memset(zero[:, 0:1], 0.0)
+        nc.scalar.activation(zero[:, 1:2], zero[:, 0:1], ACT.Silu)
+        silu_bias = zero[:, 1:2]
         make_identity(nc, ident[:])
 
-        nc.sync.dma_start(dst_t[:], dst)
-        nc.sync.dma_start(dyw[:], dy_words[0].rearrange("p t d -> p (t d)").bitcast(I32))
-        for r in range(4):
-            nc.sync.dma_start(dys[r:P:32, :].bitcast(I32), dy_scales[0, r:16:4, :].bitcast(I32))
-        nc.sync.dma_start(wetw[:, 0:2, :].bitcast(I32), wet_words[0:2, 0].rearrange("e p b -> p e b").bitcast(I32))
-        for r in range(4):
-            nc.sync.dma_start(wets[r:P:32, :, :].bitcast(I32), wet_scales[:, 0, r:16:4, :].rearrange("e q h -> q e h").bitcast(I32))
-        with nc.allow_non_contiguous_dma(reason="one gate value a partition"):
-            nc.sync.dma_start(gcol[:], gate[0].rearrange("(e p) -> p e", p=P))
-        nc.sync.dma_start(offs2_t[:], offs2)
-        nc.sync.dma_start(wetw[:, 2:E, :].bitcast(I32), wet_words[2:E, 0].rearrange("e p b -> p e b").bitcast(I32))
-        nc.sync.dma_start(a_t[:], a.rearrange("(p t) j -> p t j", t=4))
+        def load_wet_words(lo, hi):
+            source = wet_words[lo:hi, 0].rearrange("e p b -> p e b")
+            nc.sync.dma_start(wet_w[:, lo:hi, :].bitcast(I32), source.bitcast(I32))
+
+        nc.sync.dma_start(dst_list[:], dst)
+        for q in range(P // QUAD):
+            rows = dy_scales[0, SCALE_ROWS * q : SCALE_ROWS * (q + 1), :].bitcast(I32)
+            repeated = rows.unsqueeze(0).to_broadcast([QUAD // SCALE_ROWS, SCALE_ROWS, T // 4])
+            nc.sync.dma_start(dy_s[QUAD * q : QUAD * (q + 1), :].bitcast(I32), repeated)
+        nc.sync.dma_start(dy_w[:], dy_words[0].rearrange("p t d -> p (t d)").bitcast(I32))
+        load_wet_words(0, 2)
+        nc.sync.dma_start(offs2_list[:], offs2)
+        for r in range(SCALE_ROWS):
+            rows = wet_scales[:, 0, r : N // 32 : SCALE_ROWS, :].rearrange("e q h -> q e h")
+            nc.sync.dma_start(wet_s[r:P:QUAD, :, :].bitcast(I32), rows.bitcast(I32))
+        with nc.allow_non_contiguous_dma(reason="one gate value a partition and expert"):
+            nc.sync.dma_start(gate_col[:], gate[0].rearrange("(e p) -> p e", p=P))
+        load_wet_words(2, E)
+        nc.sync.dma_start(a_planes[:], a.rearrange("(p t) j -> p t j", t=PACK))
         for g in range(G):
-            nc.sync.dma_start(wraw[:, g], wgt[g].rearrange("(p t) k -> p t k", t=4))
-        nc.sync.dma_start(offs_t[:], offs)
+            nc.sync.dma_start(wgt_planes[:, g], wgt[g].rearrange("(p t) k -> p t k", t=PACK))
+        nc.sync.dma_start(offs_list[:], offs)
 
-        pieces = [(0, 128), (128, 256), (256, 768)]
-        gw, gs = {}, {}
-        for lo, hi in pieces:
-            w = held.tile([P, hi - lo], U32, name="gw%d" % lo, align_bytes=64)
-            s = held.tile([P, hi - lo], U8, name="gs%d" % lo, align_bytes=64)
-            o = dst_t[:, lo // 16 : hi // 16]
-            nc.vector.tensor_copy(w[:], dyw[:].bitcast(U32).indirect(o))
-            nc.vector.tensor_copy(s[:], dys[:].indirect(o))
+        def entries(list_tile, lo, hi):
+            return list_tile[:, lo // PER_COL : hi // PER_COL]
+
+        slot_words, slot_scales = {}, {}
+        for lo, hi in GATHER_CUTS:
+            words = held.tile([P, hi - lo], U32, name="words%d" % lo, align_bytes=64)
+            scale_bytes = held.tile([P, hi - lo], U8, name="scale_bytes%d" % lo, align_bytes=64)
+            nc.vector.tensor_copy(words[:], dy_w[:].bitcast(U32).indirect(entries(dst_list, lo, hi)))
+            nc.vector.tensor_copy(scale_bytes[:], dy_s[:].indirect(entries(dst_list, lo, hi)))
             for e in range(lo // C2, hi // C2):
-                gw[e] = w[:, e * C2 - lo : (e + 1) * C2 - lo]
-                gs[e] = s[:, e * C2 - lo : (e + 1) * C2 - lo]
+                slot_words[e] = words[:, e * C2 - lo : (e + 1) * C2 - lo]
+                slot_scales[e] = scale_bytes[:, e * C2 - lo : (e + 1) * C2 - lo]
 
-        zt = [held.tile([P, 4, C1], F32, name="zt%d" % g) for g in range(G)]
+        z_slots = [held.tile([P, PACK, C1], F32, name="z_slots%d" % g) for g in range(G)]
 
-        def expert(e):
-            acc = psum.tile([P, H], F32, name="acc1")
-            nc.tensor.matmul_mx(out=acc[:], lhsT=gw[e].bitcast(FP8X4), lhsT_scale=gs[e],
-                                rhs=wetw[:, e, :].bitcast(FP4X4), rhs_scale=wets[:, e, :], start=True, stop=True)
-            y = ring.tile([P, 4, P], F32, name="y")
-            nc.scalar.activation(y[:], acc[:].rearrange("s (m t) -> s t m", t=4), ACT.Copy, scale=gcol[:, e : e + 1])
-            turned = psum.tile([P, 4, P], F32, name="turned")
-            for t in range(4):
-                nc.tensor.transpose(turned[:, t, :], y[:, t, :], ident[:])
-            h = e % 2
-            nc.scalar.copy(zt[e // 2][:, :, h * C2 : (h + 1) * C2], turned[:])
+        def first_product(e, cuts):
+            sums = psum.tile([P, H], F32, name="sums")
+            nc.tensor.matmul_mx(
+                out=sums[:],
+                lhsT=slot_words[e].bitcast(FP8X4),
+                lhsT_scale=slot_scales[e],
+                rhs=wet_w[:, e, :].bitcast(FP4X4),
+                rhs_scale=wet_s[:, e, :],
+                start=True,
+                stop=True,
+            )
+            gated = ring.tile([P, PACK, P], F32, name="gated")
+            by_plane = sums[:].rearrange("s (p t) -> s t p", t=PACK)
+            slots = slice(e % 2 * C2, (e % 2 + 1) * C2)
+            for lo, hi in cuts:
+                turned = psum.tile([P, hi - lo, P], F32, name="turned")
+                nc.scalar.activation(gated[:, lo:hi], by_plane[:, lo:hi], ACT.Copy, scale=gate_col[:, e : e + 1])
+                for t in range(lo, hi):
+                    nc.tensor.transpose(turned[:, t - lo, :], gated[:, t, :], ident[:])
+                nc.scalar.copy(z_slots[e // 2][:, lo:hi, slots], turned[:])
 
-        zs = [[held.tile([P, T], F32, name="zs%d_%d" % (g, t)) for t in range(4)] for g in range(G)]
+        z_back = [[held.tile([P, T], F32, name="z_back%d_%d" % (g, t)) for t in range(PACK)] for g in range(G)]
 
         def scatter_z(g, t, lo, hi):
-            o = offs2_t[:, (g * C1 + lo) // 16 : (g * C1 + hi) // 16]
-            nc.vector.tensor_copy(zs[g][t][:].indirect(o), zt[g][:, t, lo:hi])
+            window = z_back[g][t][:].indirect(entries(offs2_list, g * C1 + lo, g * C1 + hi))
+            nc.vector.tensor_copy(window, z_slots[g][:, t, lo:hi])
 
-        q_t = held.tile([P, G, 4, C1], F32, name="q_t")
-        sg_t = held.tile([P, G, 4, C1], F32, name="sg_t")
-        d_t = held.tile([P, G, 4, C1], F32, name="d_t")
-        planes = [held.tile([P, 4, C1], BF16, name="planes%d" % g) for g in range(G)]
-        qin = [held.tile([P, K + C1, 4], BF16, name="qin%d" % g, align_bytes=64) for g in range(G)]
+        silu_neg = held.tile([P, G, PACK, C1], F32, name="silu_neg")
+        sigmoid = held.tile([P, G, PACK, C1], F32, name="sigmoid")
+        minus_d = held.tile([P, G, PACK, C1], F32, name="minus_d")
+        da_planes = [held.tile([P, PACK, C1], BF16, name="da_planes%d" % g) for g in range(G)]
+        woven = [held.tile([P, K + C1, PACK], BF16, name="woven%d" % g, align_bytes=64) for g in range(G)]
         codes = [held.tile([P, K + C1], U32, name="codes%d" % g, align_bytes=64) for g in range(G)]
         scales = [held.tile([P, K + C1], U8, name="scales%d" % g, align_bytes=64) for g in range(G)]
-        dx = [held.tile([P, 2, C1], F32, name="dx%d" % g) for g in range(G)]
-        outw = [held.tile([P, T], F32, name="outw%d" % k) for k in range(2)]
+        dx = [held.tile([P, K_TILES, C1], F32, name="dx%d" % g) for g in range(G)]
+        out_rows = [held.tile([P, T], F32, name="out_rows%d" % k) for k in range(K_TILES)]
 
-        def silu(g):
-            nc.scalar.activation(q_t[:, g], a_t[:, :, g * C1 : (g + 1) * C1], ACT.Silu, scale=-1.0)
-            if D_ENG != "vector":
-                nc.scalar.activation(q_t[:, g], q_t[:, g], ACT.Identity, scale=-1.0, bias=1.0)
+        def group_slots(g):
+            return slice(g * C1, (g + 1) * C1)
 
-        def sigmoid(g):
-            nc.scalar.activation(sg_t[:, g], a_t[:, :, g * C1 : (g + 1) * C1], ACT.Sigmoid)
+        def make_silu(g):
+            nc.scalar.activation(silu_neg[:, g], a_planes[:, :, group_slots(g)], ACT.Silu, scale=-1.0, bias=silu_bias)
 
-        def dsilu(g):
-            if D_ENG == "vector":
-                nc.vector.scalar_tensor_tensor(d_t[:, g], q_t[:, g], 1.0, sg_t[:, g], ALU.subtract, ALU.mult)
-            else:
-                for t in range(4):
-                    nc.gpsimd.tensor_tensor(d_t[:, g, t], q_t[:, g, t], sg_t[:, g, t], ALU.mult)
+        def make_minus_d(g):
+            nc.scalar.activation(sigmoid[:, g], a_planes[:, :, group_slots(g)], ACT.Sigmoid)
+            nc.vector.scalar_tensor_tensor(minus_d[:, g], silu_neg[:, g], 1.0, sigmoid[:, g], ALU.subtract, ALU.mult)
 
-        def mult(g, t):
-            src = zs[g][t][:, g * C1 : (g + 1) * C1]
-            if M_ENG == "vector":
-                nc.vector.scalar_tensor_tensor(planes[g][:, t, :], src, -1.0 if D_ENG == "vector" else 1.0, d_t[:, g, t], ALU.mult, ALU.mult)
-            else:
-                nc.gpsimd.tensor_tensor(planes[g][:, t, :], src, d_t[:, g, t], ALU.mult)
+        def weave(side_by_side, planes):
+            nc.scalar.copy(
+                side_by_side.rearrange("p (c i) t -> p c t i", i=4),
+                planes.rearrange("p t (c i) -> p c t i", i=4),
+            )
 
-        def weave(dst_ap, src_ap, eng):
-            o = dst_ap.rearrange("p (c i) t -> p c t i", i=4)
-            s = src_ap.rearrange("p t (c i) -> p c t i", i=4)
-            if eng == "scalar":
-                nc.scalar.copy(o, s)
-            else:
-                nc.gpsimd.tensor_scalar(o, s, 1.0, 0.0, ALU.mult, ALU.add)
+        def weave_wgt(g):
+            weave(woven[g][:, 0:K, :], wgt_planes[:, g])
 
-        def weave_w(g):
-            weave(qin[g][:, 0:K, :], wraw[:, g], W_ENG)
+        def make_da(g):
+            for t in range(PACK):
+                z = z_back[g][t][:, group_slots(g)]
+                nc.vector.scalar_tensor_tensor(da_planes[g][:, t, :], z, -1.0, minus_d[:, g, t], ALU.mult, ALU.mult)
+            weave(woven[g][:, K:, :], da_planes[g][:])
 
-        def weave_da(g):
-            weave(qin[g][:, K:, :], planes[g][:], "scalar")
-
-        def second(g):
-            nc.vector.quantize_mx(out=codes[g][:].bitcast(FP8X4), scales=scales[g][:], in_=qin[g][:].rearrange("p c t -> p (c t)"))
-            acc = psum.tile([P, 2, C1], F32, name="acc2")
-            for k in range(2):
-                nc.tensor.matmul_mx(out=acc[:, k, :], lhsT=codes[g][:, k * P : (k + 1) * P].bitcast(FP8X4), lhsT_scale=scales[g][:, k * P : (k + 1) * P],
-                                    rhs=codes[g][:, K:].bitcast(FP8X4), rhs_scale=scales[g][:, K:], start=True, stop=True)
-            nc.scalar.copy(dx[g][:], acc[:])
+        def second_product(g):
+            nc.vector.quantize_mx(
+                out=codes[g][:].bitcast(FP8X4), scales=scales[g][:], in_=woven[g][:].rearrange("p c t -> p (c t)")
+            )
+            dx_sums = psum.tile([P, K_TILES, C1], F32, name="dx_sums")
+            for k in range(K_TILES):
+                nc.tensor.matmul_mx(
+                    out=dx_sums[:, k, :],
+                    lhsT=codes[g][:, k * P : (k + 1) * P].bitcast(FP8X4),
+                    lhsT_scale=scales[g][:, k * P : (k + 1) * P],
+                    rhs=codes[g][:, K:].bitcast(FP8X4),
+                    rhs_scale=scales[g][:, K:],
+                    start=True,
+                    stop=True,
+                )
+            nc.scalar.copy(dx[g][:], dx_sums[:])
 
         def scatter_dx(g, k):
-            o = offs_t[:, g * C1 // 16 : (g + 1) * C1 // 16]
-            nc.vector.tensor_copy(outw[k][:].indirect(o), dx[g][:, k, :])
+            window = out_rows[k][:].indirect(entries(offs_list, g * C1, (g + 1) * C1))
+            nc.vector.tensor_copy(window, dx[g][:, k, :])
 
-        expert(0)
-        expert(1)
-        for h in range(2):
-            for t in range(4):
-                scatter_z(0, t, h * C2, (h + 1) * C2)
-        expert(2)
-        expert(3)
+        first_product(0, FIRST_EXPERT_CUTS)
+        first_product(1, WHOLE)
+        for expert in range(2):
+            for t in range(PACK):
+                scatter_z(0, t, expert * C2, (expert + 1) * C2)
+        for e in range(2, E):
+            first_product(e, WHOLE)
         for g in range(G):
-            silu(g)
-        expert(4)
-        expert(5)
-        for t in range(4):
+            make_silu(g)
+        for t in range(PACK):
             scatter_z(1, t, 0, C1)
         for g in range(G):
-            sigmoid(g)
-            dsilu(g)
-        for g in range(2):
-            weave_w(g)
-            for t in range(4):
-                mult(g, t)
-            weave_da(g)
-        weave_w(2)
-        scatter_z(2, 0, 0, C1)
-        second(0)
-        scatter_z(2, 1, 0, C1)
-        second(1)
-        scatter_z(2, 2, 0, C1)
-        scatter_z(2, 3, 0, C1)
-        for t in range(4):
-            mult(2, t)
-        weave_da(2)
-        second(2)
-        scatter_dx(0, 0)
-        scatter_dx(1, 0)
-        scatter_dx(0, 1)
-        scatter_dx(1, 1)
-        scatter_dx(2, 0)
-        nc.sync.dma_start(out[0:P, :], outw[0][:])
-        scatter_dx(2, 1)
-        nc.sync.dma_start(out[P:K, :], outw[1][:])
+            make_minus_d(g)
+        last = G - 1
+        for g in range(last):
+            weave_wgt(g)
+            make_da(g)
+        weave_wgt(last)
+        for t in range(PACK):
+            scatter_z(last, t, 0, C1)
+            if t < last:
+                second_product(t)
+        make_da(last)
+        second_product(last)
+        for k in range(K_TILES):
+            for g in range(last):
+                scatter_dx(g, k)
+        for k in range(K_TILES):
+            scatter_dx(last, k)
+            nc.sync.dma_start(out[k * P : (k + 1) * P, :], out_rows[k][:])

@@ -14,10 +14,12 @@ QUAD = 32
 SCALE_ROWS = 4
 PER_COL = 16
 K_TILES = K // P
+I_TILES = H // P
+HALVES = C1 // P
 
 GATHER_CUTS = [(0, C2), (C2, 2 * C2), (2 * C2, T)]
-FIRST_EXPERT_CUTS = [(0, 1), (1, PACK)]
-WHOLE = [(0, PACK)]
+FIRST_EXPERT_CUTS = [(0, 1), (1, I_TILES)]
+WHOLE = [(0, I_TILES)]
 
 F32 = mybir.dt.float32
 BF16 = mybir.dt.bfloat16
@@ -37,27 +39,31 @@ def tile_moe_hib_silu_kernel(
     nc = tc.nc
     with ExitStack() as ctx:
         held = ctx.enter_context(tc.tile_pool(name="held", bufs=1))
-        ring = ctx.enter_context(tc.tile_pool(name="ring", bufs=2))
         psum = ctx.enter_context(tc.psum_pool(name="psum", bufs=2))
+
+        def keep(shape, dtype, name, on=None):
+            return held.tile(shape, dtype, name=name, tag=on or name, align_bytes=64)
 
         dst_list = held.tile([P, T // PER_COL], U16, name="dst_list")
         offs2_list = held.tile([P, T // PER_COL], U16, name="offs2_list")
         offs_list = held.tile([P, T // PER_COL], U16, name="offs_list")
-        dy_w = held.tile([P, T], I32, name="dy_w", align_bytes=64)
-        dy_s = held.tile([P, T], U8, name="dy_s", align_bytes=64)
-        wet_w = held.tile([P, E, 2 * H], U8, name="wet_w", align_bytes=64)
-        wet_s = held.tile([P, E, H], U8, name="wet_s", align_bytes=64)
-        gate_col = held.tile([P, E], F32, name="gate_col")
-        a_planes = held.tile([P, PACK, T], F32, name="a_planes")
-        wgt_planes = held.tile([P, G, PACK, K], F32, name="wgt_planes")
-        ident = held.tile([P, P], F32, name="ident")
+        dy_w = keep([P, T], I32, "dy_w")
+        dy_s = keep([P, T], U8, "dy_s")
+        wet_w = keep([P, E, 2 * H], U8, "wet_w")
+        wet_s = keep([P, E, H], U8, "wet_s")
+        gate_rows = keep([P, T], F32, "gate_rows")
+        a_tiles = keep([P, I_TILES, T], F32, "a_tiles")
+        wgt_planes = keep([P, G, PACK, K], F32, "wgt_planes")
+        ident_bf16 = keep([P, P], BF16, "ident_bf16")
+        ident_f32 = keep([P, P], F32, "ident_f32")
 
         nc.vector.memset(wet_s[:].rearrange("p e h -> p (e h)").bitcast(I32), 0)
         zero = held.tile([P, 2], F32, name="zero")
         nc.vector.memset(zero[:, 0:1], 0.0)
         nc.scalar.activation(zero[:, 1:2], zero[:, 0:1], ACT.Silu)
         silu_bias = zero[:, 1:2]
-        make_identity(nc, ident[:])
+        make_identity(nc, ident_bf16[:])
+        make_identity(nc, ident_f32[:])
 
         def load_wet_words(lo, hi):
             source = wet_words[lo:hi, 0].rearrange("e p b -> p e b")
@@ -70,14 +76,13 @@ def tile_moe_hib_silu_kernel(
             nc.sync.dma_start(dy_s[QUAD * q : QUAD * (q + 1), :].bitcast(I32), repeated)
         nc.sync.dma_start(dy_w[:], dy_words[0].rearrange("p t d -> p (t d)").bitcast(I32))
         load_wet_words(0, 2)
-        nc.sync.dma_start(offs2_list[:], offs2)
+        nc.sync.dma_start(gate_rows[:], gate)
         for r in range(SCALE_ROWS):
             rows = wet_scales[:, 0, r : N // 32 : SCALE_ROWS, :].rearrange("e q h -> q e h")
             nc.sync.dma_start(wet_s[r:P:QUAD, :, :].bitcast(I32), rows.bitcast(I32))
-        with nc.allow_non_contiguous_dma(reason="one gate value a partition and expert"):
-            nc.sync.dma_start(gate_col[:], gate[0].rearrange("(e p) -> p e", p=P))
+        nc.sync.dma_start(offs2_list[:], offs2)
         load_wet_words(2, E)
-        nc.sync.dma_start(a_planes[:], a.rearrange("(p t) j -> p t j", t=PACK))
+        nc.sync.dma_start(a_tiles[:], a.rearrange("(c p) j -> p c j", p=P))
         for g in range(G):
             nc.sync.dma_start(wgt_planes[:, g], wgt[g].rearrange("(p t) k -> p t k", t=PACK))
         nc.sync.dma_start(offs_list[:], offs)
@@ -87,77 +92,83 @@ def tile_moe_hib_silu_kernel(
 
         slot_words, slot_scales = {}, {}
         for lo, hi in GATHER_CUTS:
-            words = held.tile([P, hi - lo], U32, name="words%d" % lo, align_bytes=64)
-            scale_bytes = held.tile([P, hi - lo], U8, name="scale_bytes%d" % lo, align_bytes=64)
+            words = keep([P, hi - lo], U32, "words%d" % lo)
+            scale_bytes = keep([P, hi - lo], U8, "scale_bytes%d" % lo)
             nc.vector.tensor_copy(words[:], dy_w[:].bitcast(U32).indirect(entries(dst_list, lo, hi)))
             nc.vector.tensor_copy(scale_bytes[:], dy_s[:].indirect(entries(dst_list, lo, hi)))
             for e in range(lo // C2, hi // C2):
                 slot_words[e] = words[:, e * C2 - lo : (e + 1) * C2 - lo]
                 slot_scales[e] = scale_bytes[:, e * C2 - lo : (e + 1) * C2 - lo]
 
-        z_slots = [held.tile([P, PACK, C1], F32, name="z_slots%d" % g) for g in range(G)]
+        sums_out = keep([P, I_TILES, T], F32, "sums_out")
 
         def first_product(e, cuts):
-            sums = psum.tile([P, H], F32, name="sums")
-            nc.tensor.matmul_mx(
-                out=sums[:],
-                lhsT=slot_words[e].bitcast(FP8X4),
-                lhsT_scale=slot_scales[e],
-                rhs=wet_w[:, e, :].bitcast(FP4X4),
-                rhs_scale=wet_s[:, e, :],
-                start=True,
-                stop=True,
-            )
-            gated = ring.tile([P, PACK, P], F32, name="gated")
-            by_plane = sums[:].rearrange("s (p t) -> s t p", t=PACK)
-            slots = slice(e % 2 * C2, (e % 2 + 1) * C2)
             for lo, hi in cuts:
-                turned = psum.tile([P, hi - lo, P], F32, name="turned")
-                nc.scalar.activation(gated[:, lo:hi], by_plane[:, lo:hi], ACT.Copy, scale=gate_col[:, e : e + 1])
-                for t in range(lo, hi):
-                    nc.tensor.transpose(turned[:, t - lo, :], gated[:, t, :], ident[:])
-                nc.scalar.copy(z_slots[e // 2][:, lo:hi, slots], turned[:])
+                sums = psum.tile([P, hi - lo, C2], F32, name="sums")
+                for c in range(lo, hi):
+                    nc.tensor.matmul_mx(
+                        out=sums[:, c - lo, :],
+                        lhsT=wet_w[:, e, 2 * P * c : 2 * P * (c + 1)].bitcast(FP4X4),
+                        lhsT_scale=wet_s[:, e, P * c : P * (c + 1)],
+                        rhs=slot_words[e].bitcast(FP8X4),
+                        rhs_scale=slot_scales[e],
+                        start=True,
+                        stop=True,
+                    )
+                nc.scalar.copy(sums_out[:, lo:hi, e * C2 : (e + 1) * C2], sums[:])
 
-        z_back = [[held.tile([P, T], F32, name="z_back%d_%d" % (g, t)) for t in range(PACK)] for g in range(G)]
+        last = G - 1
+        z_back = [keep([P, T], F32, "z_back%d" % c) for c in range(I_TILES)]
 
-        def scatter_z(g, t, lo, hi):
-            window = z_back[g][t][:].indirect(entries(offs2_list, g * C1 + lo, g * C1 + hi))
-            nc.vector.tensor_copy(window, z_slots[g][:, t, lo:hi])
+        def scatter_z(window, c, first, end):
+            slots = slice(first * C2, end * C2)
+            scattered = window[:].indirect(entries(offs2_list, slots.start, slots.stop))
+            nc.vector.tensor_tensor(scattered, sums_out[:, c, slots], gate_rows[:, slots], ALU.mult)
 
-        silu_neg = held.tile([P, G, PACK, C1], F32, name="silu_neg")
-        sigmoid = held.tile([P, G, PACK, C1], F32, name="sigmoid")
-        minus_d = held.tile([P, G, PACK, C1], F32, name="minus_d")
-        da_planes = [held.tile([P, PACK, C1], BF16, name="da_planes%d" % g) for g in range(G)]
-        woven = [held.tile([P, K + C1, PACK], BF16, name="woven%d" % g, align_bytes=64) for g in range(G)]
-        codes = [held.tile([P, K + C1], U32, name="codes%d" % g, align_bytes=64) for g in range(G)]
-        scales = [held.tile([P, K + C1], U8, name="scales%d" % g, align_bytes=64) for g in range(G)]
-        dx = [held.tile([P, K_TILES, C1], F32, name="dx%d" % g) for g in range(G)]
-        out_rows = [held.tile([P, T], F32, name="out_rows%d" % k) for k in range(K_TILES)]
+        silu_neg = keep([P, I_TILES, T], F32, "silu_neg")
+        sigmoid = keep([P, I_TILES, T], F32, "sigmoid")
+        minus_d = keep([P, I_TILES, T], F32, "minus_d")
+        da = [keep([P, I_TILES, C1], BF16, "da%d" % g) for g in range(G)]
+        woven = [keep([P, K + C1, PACK], BF16, "woven%d" % g) for g in range(G)]
+        codes = [keep([P, K + C1], U32, "codes%d" % g) for g in range(G)]
+        scales = [keep([P, K + C1], U8, "scales%d" % g) for g in range(G)]
+        out_rows = [keep([P, T], F32, "out_rows%d" % k) for k in range(K_TILES)]
 
         def group_slots(g):
             return slice(g * C1, (g + 1) * C1)
 
-        def make_silu(g):
-            nc.scalar.activation(silu_neg[:, g], a_planes[:, :, group_slots(g)], ACT.Silu, scale=-1.0, bias=silu_bias)
-
         def make_minus_d(g):
-            nc.scalar.activation(sigmoid[:, g], a_planes[:, :, group_slots(g)], ACT.Sigmoid)
-            nc.vector.scalar_tensor_tensor(minus_d[:, g], silu_neg[:, g], 1.0, sigmoid[:, g], ALU.subtract, ALU.mult)
-
-        def weave(side_by_side, planes):
-            nc.scalar.copy(
-                side_by_side.rearrange("p (c i) t -> p c t i", i=4),
-                planes.rearrange("p t (c i) -> p c t i", i=4),
+            cols = group_slots(g)
+            nc.vector.scalar_tensor_tensor(
+                minus_d[:, :, cols], silu_neg[:, :, cols], 1.0, sigmoid[:, :, cols], ALU.subtract, ALU.mult
             )
 
         def weave_wgt(g):
-            weave(woven[g][:, 0:K, :], wgt_planes[:, g])
+            nc.scalar.copy(
+                woven[g][:, 0:K, :].rearrange("p (c i) t -> p c t i", i=4),
+                wgt_planes[:, g].rearrange("p t (c i) -> p c t i", i=4),
+            )
 
-        def make_da(g):
-            for t in range(PACK):
-                z = z_back[g][t][:, group_slots(g)]
-                nc.vector.scalar_tensor_tensor(da_planes[g][:, t, :], z, -1.0, minus_d[:, g, t], ALU.mult, ALU.mult)
-            weave(woven[g][:, K:, :], da_planes[g][:])
+        def make_da(g, c, window):
+            cols = group_slots(g)
+            nc.vector.scalar_tensor_tensor(
+                da[g][:, c, :], window[:, cols], -1.0, minus_d[:, c, cols], ALU.mult, ALU.mult
+            )
+
+        def regroup(g):
+            pairs = []
+            for h in range(HALVES):
+                by_slot = psum.tile([P, H], BF16, name="by_slot")
+                for c in range(I_TILES):
+                    nc.tensor.transpose(by_slot[:, c * P : (c + 1) * P], da[g][:, c, h * P : (h + 1) * P], ident_bf16[:])
+                pairs.append(keep([P, 2, P], F32, "pairs%d_%d" % (g, h)))
+                nc.scalar.copy(pairs[h][:], by_slot[:].bitcast(F32).rearrange("s (p u) -> s u p", u=2))
+            for h in range(HALVES):
+                by_word = psum.tile([P, 2, P], F32, name="by_word")
+                for u in range(2):
+                    nc.tensor.transpose(by_word[:, u, :], pairs[h][:, u, :], ident_f32[:])
+                columns = woven[g][:, K + h * P : K + (h + 1) * P, :].rearrange("p s t -> p (s t)").bitcast(F32)
+                nc.scalar.copy(columns.rearrange("p (s u) -> p s u", u=2), by_word[:].rearrange("p u s -> p s u"))
 
         def second_product(g):
             nc.vector.quantize_mx(
@@ -174,39 +185,47 @@ def tile_moe_hib_silu_kernel(
                     start=True,
                     stop=True,
                 )
-            nc.scalar.copy(dx[g][:], dx_sums[:])
+            return dx_sums
 
-        def scatter_dx(g, k):
+        def empty_dx(g, dx_sums, on=None):
+            dx = keep([P, K_TILES, C1], F32, "dx%d" % g, on)
+            nc.scalar.copy(dx[:], dx_sums[:])
+            return dx
+
+        def scatter_dx(g, k, dx):
             window = out_rows[k][:].indirect(entries(offs_list, g * C1, (g + 1) * C1))
-            nc.vector.tensor_copy(window, dx[g][:, k, :])
+            nc.vector.tensor_copy(window, dx[:, k, :])
 
         first_product(0, FIRST_EXPERT_CUTS)
-        first_product(1, WHOLE)
-        for expert in range(2):
-            for t in range(PACK):
-                scatter_z(0, t, expert * C2, (expert + 1) * C2)
-        for e in range(2, E):
+        for c in range(I_TILES):
+            scatter_z(z_back[c], c, 0, 1)
+        for e in range(1, E):
             first_product(e, WHOLE)
-        for g in range(G):
-            make_silu(g)
-        for t in range(PACK):
-            scatter_z(1, t, 0, C1)
+        for c in range(I_TILES):
+            scatter_z(z_back[c], c, 1, 4)
+        nc.scalar.activation(silu_neg[:], a_tiles[:], ACT.Silu, scale=-1.0, bias=silu_bias)
+        nc.scalar.activation(sigmoid[:], a_tiles[:], ACT.Sigmoid)
         for g in range(G):
             make_minus_d(g)
-        last = G - 1
-        for g in range(last):
+        for g in range(G):
             weave_wgt(g)
-            make_da(g)
-        weave_wgt(last)
-        for t in range(PACK):
-            scatter_z(last, t, 0, C1)
-            if t < last:
-                second_product(t)
-        make_da(last)
-        second_product(last)
-        for k in range(K_TILES):
-            for g in range(last):
-                scatter_dx(g, k)
-        for k in range(K_TILES):
-            scatter_dx(last, k)
-            nc.sync.dma_start(out[k * P : (k + 1) * P, :], out_rows[k][:])
+        for g in range(last):
+            for c in range(I_TILES):
+                make_da(g, c, z_back[c])
+            regroup(g)
+        dx_sums = [second_product(g) for g in range(last)]
+        last_windows = z_back[:-1] + [keep([P, T], F32, "z_back_last", "pairs1_0")]
+        for c in range(I_TILES):
+            scatter_z(last_windows[c], c, 4, E)
+        for c in range(I_TILES):
+            make_da(last, c, last_windows[c])
+        dx = [empty_dx(0, dx_sums[0], "pairs1_1")]
+        regroup(last)
+        last_sums = second_product(last)
+        dx.append(empty_dx(1, dx_sums[1], "pairs2_1"))
+        dx.append(empty_dx(last, last_sums))
+        for g in range(G):
+            for k in range(K_TILES):
+                scatter_dx(g, k, dx[g])
+                if g == last:
+                    nc.sync.dma_start(out[k * P : (k + 1) * P, :], out_rows[k][:])

@@ -17,7 +17,11 @@ K_TILES = K // P
 I_TILES = H // P
 HALVES = C1 // P
 
-GATHER_CUTS = [(0, C2), (C2, 2 * C2), (2 * C2, T)]
+WINDOW = 1024
+WORD_CUTS = [(0, C2), (C2, T)]
+Z_CUTS = [(0, 1), (1, 4), (4, E)]
+BLOCKS = T // P
+ON_VECTOR = 3
 FIRST_EXPERT_CUTS = [(0, 1), (1, I_TILES)]
 WHOLE = [(0, I_TILES)]
 
@@ -39,79 +43,99 @@ def tile_moe_hib_silu_kernel(
     nc = tc.nc
     with ExitStack() as ctx:
         held = ctx.enter_context(tc.tile_pool(name="held", bufs=1))
-        psum = ctx.enter_context(tc.psum_pool(name="psum", bufs=2))
+        psum = ctx.enter_context(tc.psum_pool(name="psum", bufs=1))
 
         def keep(shape, dtype, name, on=None):
             return held.tile(shape, dtype, name=name, tag=on or name, align_bytes=64)
 
+        def bank(number, shape, name):
+            return psum.tile(shape, F32, name=name, tag="bank%d" % number)
+
+        taken = []
+
+        def next_turn():
+            taken.append(len(taken) % 2)
+            return taken[-1]
+
         dst_list = held.tile([P, T // PER_COL], U16, name="dst_list")
         offs2_list = held.tile([P, T // PER_COL], U16, name="offs2_list")
         offs_list = held.tile([P, T // PER_COL], U16, name="offs_list")
-        dy_w = keep([P, T], I32, "dy_w")
-        dy_s = keep([P, T], U8, "dy_s")
+        dy_w = keep([P, WINDOW], I32, "dy_w")
+        dy_s = keep([P, WINDOW], U8, "dy_s")
         wet_w = keep([P, E, 2 * H], U8, "wet_w")
         wet_s = keep([P, E, H], U8, "wet_s")
-        gate_rows = keep([P, T], F32, "gate_rows")
-        a_tiles = keep([P, I_TILES, T], F32, "a_tiles")
-        wgt_planes = keep([P, G, PACK, K], F32, "wgt_planes")
-        ident_bf16 = keep([P, P], BF16, "ident_bf16")
-        ident_f32 = keep([P, P], F32, "ident_f32")
+        gates = [keep([P, (end - first) * C2], F32, "gate%d" % first) for first, end in Z_CUTS]
+        a_halves = [keep([P, I_TILES, T // 2], F32, "a_half%d" % half) for half in range(2)]
+        wgt_planes = [keep([P, PACK, K], F32, "wgt_planes%d" % g) for g in range(G)]
+        ident = keep([P, P], F32, "ident")
 
         nc.vector.memset(wet_s[:].rearrange("p e h -> p (e h)").bitcast(I32), 0)
+        nc.vector.memset(dy_w[:, T:], 0)
+        nc.vector.memset(dy_s[:, T:].bitcast(I32), 0)
         zero = held.tile([P, 2], F32, name="zero")
-        nc.vector.memset(zero[:, 0:1], 0.0)
-        nc.scalar.activation(zero[:, 1:2], zero[:, 0:1], ACT.Silu)
-        silu_bias = zero[:, 1:2]
-        make_identity(nc, ident_bf16[:])
-        make_identity(nc, ident_f32[:])
+        nc.vector.memset(zero[:, 0:1], 64.0)
+        nc.scalar.activation(zero[:, 1:2], zero[:, 0:1], ACT.Sigmoid)
+        one = zero[:, 1:2]
+        make_identity(nc, ident[:])
 
         def load_wet_words(lo, hi):
             source = wet_words[lo:hi, 0].rearrange("e p b -> p e b")
             nc.sync.dma_start(wet_w[:, lo:hi, :].bitcast(I32), source.bitcast(I32))
 
+        def load_gate(cut):
+            first, end = Z_CUTS[cut]
+            nc.sync.dma_start(gates[cut][:], gate[:, first * C2 : end * C2])
+
+        def load_a(half):
+            columns = a[:, half * T // 2 : (half + 1) * T // 2]
+            nc.sync.dma_start(a_halves[half][:], columns.rearrange("(c p) j -> p c j", p=P))
+
         nc.sync.dma_start(dst_list[:], dst)
         for q in range(P // QUAD):
             rows = dy_scales[0, SCALE_ROWS * q : SCALE_ROWS * (q + 1), :].bitcast(I32)
             repeated = rows.unsqueeze(0).to_broadcast([QUAD // SCALE_ROWS, SCALE_ROWS, T // 4])
-            nc.sync.dma_start(dy_s[QUAD * q : QUAD * (q + 1), :].bitcast(I32), repeated)
-        nc.sync.dma_start(dy_w[:], dy_words[0].rearrange("p t d -> p (t d)").bitcast(I32))
+            nc.sync.dma_start(dy_s[QUAD * q : QUAD * (q + 1), 0:T].bitcast(I32), repeated)
+        nc.sync.dma_start(dy_w[:, 0:T], dy_words[0].rearrange("p t d -> p (t d)").bitcast(I32))
         load_wet_words(0, 2)
-        nc.sync.dma_start(gate_rows[:], gate)
+        load_gate(0)
         for r in range(SCALE_ROWS):
             rows = wet_scales[:, 0, r : N // 32 : SCALE_ROWS, :].rearrange("e q h -> q e h")
             nc.sync.dma_start(wet_s[r:P:QUAD, :, :].bitcast(I32), rows.bitcast(I32))
         nc.sync.dma_start(offs2_list[:], offs2)
-        load_wet_words(2, E)
-        nc.sync.dma_start(a_tiles[:], a.rearrange("(c p) j -> p c j", p=P))
+        load_wet_words(2, 4)
+        load_a(0)
+        load_gate(1)
+        load_a(1)
+        load_wet_words(4, E)
         for g in range(G):
-            nc.sync.dma_start(wgt_planes[:, g], wgt[g].rearrange("(p t) k -> p t k", t=PACK))
+            nc.sync.dma_start(wgt_planes[g][:], wgt[g].rearrange("(p t) k -> p t k", t=PACK))
+        load_gate(2)
         nc.sync.dma_start(offs_list[:], offs)
 
         def entries(list_tile, lo, hi):
             return list_tile[:, lo // PER_COL : hi // PER_COL]
 
-        slot_words, slot_scales = {}, {}
-        for lo, hi in GATHER_CUTS:
+        slot_words = {}
+        scale_bytes = keep([P, T], U8, "scale_bytes")
+        nc.vector.tensor_copy(scale_bytes[:], dy_s[:].indirect(dst_list[:]))
+        for lo, hi in WORD_CUTS:
             words = keep([P, hi - lo], U32, "words%d" % lo)
-            scale_bytes = keep([P, hi - lo], U8, "scale_bytes%d" % lo)
             nc.vector.tensor_copy(words[:], dy_w[:].bitcast(U32).indirect(entries(dst_list, lo, hi)))
-            nc.vector.tensor_copy(scale_bytes[:], dy_s[:].indirect(entries(dst_list, lo, hi)))
             for e in range(lo // C2, hi // C2):
                 slot_words[e] = words[:, e * C2 - lo : (e + 1) * C2 - lo]
-                slot_scales[e] = scale_bytes[:, e * C2 - lo : (e + 1) * C2 - lo]
 
         sums_out = keep([P, I_TILES, T], F32, "sums_out")
 
-        def first_product(e, cuts):
+        def first_product(e, cuts, number=None):
             for lo, hi in cuts:
-                sums = psum.tile([P, hi - lo, C2], F32, name="sums")
+                sums = bank(next_turn() if number is None else number, [P, hi - lo, C2], "sums")
                 for c in range(lo, hi):
                     nc.tensor.matmul_mx(
                         out=sums[:, c - lo, :],
                         lhsT=wet_w[:, e, 2 * P * c : 2 * P * (c + 1)].bitcast(FP4X4),
                         lhsT_scale=wet_s[:, e, P * c : P * (c + 1)],
                         rhs=slot_words[e].bitcast(FP8X4),
-                        rhs_scale=slot_scales[e],
+                        rhs_scale=scale_bytes[:, e * C2 : (e + 1) * C2],
                         start=True,
                         stop=True,
                     )
@@ -120,68 +144,56 @@ def tile_moe_hib_silu_kernel(
         last = G - 1
         z_back = [keep([P, T], F32, "z_back%d" % c) for c in range(I_TILES)]
 
-        def scatter_z(window, c, first, end):
-            slots = slice(first * C2, end * C2)
-            scattered = window[:].indirect(entries(offs2_list, slots.start, slots.stop))
-            nc.vector.tensor_tensor(scattered, sums_out[:, c, slots], gate_rows[:, slots], ALU.mult)
+        def scatter_z(window, c, cut):
+            lo, hi = (e * C2 for e in Z_CUTS[cut])
+            scattered = window[:].indirect(entries(offs2_list, lo, hi))
+            nc.vector.tensor_tensor(scattered, sums_out[:, c, lo:hi], gates[cut][:], ALU.mult)
 
-        silu_neg = keep([P, I_TILES, T], F32, "silu_neg")
-        sigmoid = keep([P, I_TILES, T], F32, "sigmoid")
-        minus_d = keep([P, I_TILES, T], F32, "minus_d")
-        da = [keep([P, I_TILES, C1], BF16, "da%d" % g) for g in range(G)]
-        woven = [keep([P, K + C1, PACK], BF16, "woven%d" % g) for g in range(G)]
-        codes = [keep([P, K + C1], U32, "codes%d" % g) for g in range(G)]
-        scales = [keep([P, K + C1], U8, "scales%d" % g) for g in range(G)]
-        out_rows = [keep([P, T], F32, "out_rows%d" % k) for k in range(K_TILES)]
+        def turn(number, name, block_of):
+            turned = bank(number, [P, H], name)
+            for c in range(I_TILES):
+                nc.tensor.transpose(turned[:, c * P : (c + 1) * P], block_of(c), ident[:])
+            return turned
 
-        def group_slots(g):
-            return slice(g * C1, (g + 1) * C1)
+        def a_block(b):
+            return lambda c: a_halves[b // ON_VECTOR][:, c, b % ON_VECTOR * P : (b % ON_VECTOR + 1) * P]
 
-        def make_minus_d(g):
-            cols = group_slots(g)
-            nc.vector.scalar_tensor_tensor(
-                minus_d[:, :, cols], silu_neg[:, :, cols], 1.0, sigmoid[:, :, cols], ALU.subtract, ALU.mult
-            )
+        woven = {}
 
-        def weave_wgt(g):
+        def weave_wgt(g, on):
+            woven.setdefault(g, keep([P, K + C1, PACK], BF16, "woven%d" % g, on))
             nc.scalar.copy(
                 woven[g][:, 0:K, :].rearrange("p (c i) t -> p c t i", i=4),
-                wgt_planes[:, g].rearrange("p t (c i) -> p c t i", i=4),
+                wgt_planes[g][:].rearrange("p t (c i) -> p c t i", i=4),
             )
 
-        def make_da(g, c, window):
-            cols = group_slots(g)
-            nc.vector.scalar_tensor_tensor(
-                da[g][:, c, :], window[:, cols], -1.0, minus_d[:, c, cols], ALU.mult, ALU.mult
-            )
+        def make_da(b, z_turned, da):
+            nc.vector.scalar_tensor_tensor(da, z_turned[:], -1.0, minus_d[b][:], ALU.mult, ALU.mult)
+            return da
 
-        def regroup(g):
-            pairs = []
-            for h in range(HALVES):
-                by_slot = psum.tile([P, H], BF16, name="by_slot")
-                for c in range(I_TILES):
-                    nc.tensor.transpose(by_slot[:, c * P : (c + 1) * P], da[g][:, c, h * P : (h + 1) * P], ident_bf16[:])
-                pairs.append(keep([P, 2, P], F32, "pairs%d_%d" % (g, h)))
-                nc.scalar.copy(pairs[h][:], by_slot[:].bitcast(F32).rearrange("s (p u) -> s u p", u=2))
-            for h in range(HALVES):
-                by_word = psum.tile([P, 2, P], F32, name="by_word")
-                for u in range(2):
-                    nc.tensor.transpose(by_word[:, u, :], pairs[h][:, u, :], ident_f32[:])
-                columns = woven[g][:, K + h * P : K + (h + 1) * P, :].rearrange("p s t -> p (s t)").bitcast(F32)
-                nc.scalar.copy(columns.rearrange("p (s u) -> p s u", u=2), by_word[:].rearrange("p u s -> p s u"))
+        def regroup(b, da):
+            by_word = bank(b % 2, [P, 2, P], "by_word")
+            pairs = da.bitcast(F32)
+            for u in range(2):
+                nc.tensor.transpose(by_word[:, u, :], pairs[:, u : H // 2 : 2], ident[:])
+            first = K + b % HALVES * P
+            columns = woven[b // HALVES][:, first : first + P, :].rearrange("p s t -> p (s t)").bitcast(F32)
+            nc.scalar.copy(columns.rearrange("p (s u) -> p s u", u=2), by_word[:].rearrange("p u s -> p s u"))
 
-        def second_product(g):
+        def second_product(g, number, on=None):
+            codes = keep([P, K + C1], U32, "codes%d" % g, on)
+            scales = keep([P, K + C1], U8, "scales%d" % g)
             nc.vector.quantize_mx(
-                out=codes[g][:].bitcast(FP8X4), scales=scales[g][:], in_=woven[g][:].rearrange("p c t -> p (c t)")
+                out=codes[:].bitcast(FP8X4), scales=scales[:], in_=woven[g][:].rearrange("p c t -> p (c t)")
             )
-            dx_sums = psum.tile([P, K_TILES, C1], F32, name="dx_sums")
+            dx_sums = bank(number, [P, K_TILES, C1], "dx_sums")
             for k in range(K_TILES):
                 nc.tensor.matmul_mx(
                     out=dx_sums[:, k, :],
-                    lhsT=codes[g][:, k * P : (k + 1) * P].bitcast(FP8X4),
-                    lhsT_scale=scales[g][:, k * P : (k + 1) * P],
-                    rhs=codes[g][:, K:].bitcast(FP8X4),
-                    rhs_scale=scales[g][:, K:],
+                    lhsT=codes[:, k * P : (k + 1) * P].bitcast(FP8X4),
+                    lhsT_scale=scales[:, k * P : (k + 1) * P],
+                    rhs=codes[:, K:].bitcast(FP8X4),
+                    rhs_scale=scales[:, K:],
                     start=True,
                     stop=True,
                 )
@@ -198,31 +210,80 @@ def tile_moe_hib_silu_kernel(
 
         first_product(0, FIRST_EXPERT_CUTS)
         for c in range(I_TILES):
-            scatter_z(z_back[c], c, 0, 1)
-        for e in range(1, E):
+            scatter_z(z_back[c], c, 0)
+        for e in range(1, 4):
             first_product(e, WHOLE)
         for c in range(I_TILES):
-            scatter_z(z_back[c], c, 1, 4)
-        nc.scalar.activation(silu_neg[:], a_tiles[:], ACT.Silu, scale=-1.0, bias=silu_bias)
-        nc.scalar.activation(sigmoid[:], a_tiles[:], ACT.Sigmoid)
-        for g in range(G):
-            make_minus_d(g)
-        for g in range(G):
-            weave_wgt(g)
+            scatter_z(z_back[c], c, 1)
+
+        sigmoid_rows = keep([P, I_TILES, T // 2], F32, "sigmoid_rows")
+        nc.scalar.activation(sigmoid_rows[:], a_halves[0][:], ACT.Sigmoid, scale=one)
+        a_turned, sigmoid = {}, {}
+        for b in range(ON_VECTOR, BLOCKS):
+            a_turned.setdefault(b, turn(2 + b, "a_turned", a_block(b)))
+            sigmoid.setdefault(b, keep([P, H], F32, "sigmoid%d" % b))
+            nc.scalar.activation(sigmoid[b][:], a_turned[b][:], ACT.Sigmoid, scale=one)
+        silu_neg = keep([P, BLOCKS, H], F32, "silu_neg", "a_half1")
+        minus_d = {}
+
+        def make_silu(b):
+            nc.scalar.activation(silu_neg[:, b], a_turned[b][:], ACT.Silu, scale=-1.0)
+
+        def minus_d_on_gpsimd(b, on=None):
+            less_one = keep([P, H], F32, "less_one%d" % b)
+            nc.scalar.activation(less_one[:], silu_neg[:, b], ACT.Copy, bias=-1.0)
+            minus_d.setdefault(b, keep([P, H], F32, "minus_d%d" % b, on))
+            nc.gpsimd.tensor_tensor(minus_d[b][:], less_one[:], sigmoid[b][:], ALU.mult)
+
+        make_silu(3)
+        minus_d_on_gpsimd(3, "gate1")
+        make_silu(4)
+        make_silu(5)
+        for b, number in enumerate([0, 1, 5]):
+            a_turned.setdefault(b, turn(number, "a_turned", a_block(b)))
+            make_silu(b)
+            sigmoid_turned = turn(2 + b, "sigmoid", lambda c, b=b: sigmoid_rows[:, c, b * P : (b + 1) * P])
+            minus_d.setdefault(b, keep([P, H], F32, "minus_d%d" % b))
+            nc.vector.scalar_tensor_tensor(minus_d[b][:], silu_neg[:, b], 1.0, sigmoid_turned[:], ALU.subtract, ALU.mult)
+        minus_d_on_gpsimd(4)
+        minus_d_on_gpsimd(5)
+        first_product(4, WHOLE, 0)
+        first_product(5, WHOLE, 1)
+
+        def z_block(windows, b):
+            return lambda c: windows[c][:, b * P : (b + 1) * P]
+
+        z_turned = [bank(6, [P, H], "z_turned"), bank(7, [P, H], "z_turned")]
+        for c in range(I_TILES):
+            for b in range(HALVES):
+                nc.tensor.transpose(z_turned[b][:, c * P : (c + 1) * P], z_block(z_back, b)(c), ident[:])
+        z_turned.append(turn(2, "z_turned", z_block(z_back, 2)))
+        z_turned.append(turn(5, "z_turned", z_block(z_back, 3)))
+        da = [make_da(b, z_turned[b], keep([P, H], BF16, "da%d" % b)[:]) for b in range(last * HALVES)]
         for g in range(last):
-            for c in range(I_TILES):
-                make_da(g, c, z_back[c])
-            regroup(g)
-        dx_sums = [second_product(g) for g in range(last)]
-        last_windows = z_back[:-1] + [keep([P, T], F32, "z_back_last", "pairs1_0")]
+            weave_wgt(g, ["a_half1", "da1"][g])
+            for b in range(g * HALVES, (g + 1) * HALVES):
+                regroup(b, da[b])
+        dx = [empty_dx(0, second_product(0, 3))]
+        weave_wgt(last, "codes0")
+        last_windows = [
+            keep([P, T], F32, "z_last%d" % c, on) for c, on in enumerate(["minus_d2", "gate1", "wgt_planes1", "da3"])
+        ]
         for c in range(I_TILES):
-            scatter_z(last_windows[c], c, 4, E)
+            scatter_z(last_windows[c], c, 2)
+        da_last = keep([P, HALVES, H], BF16, "da_last", "wgt_planes2")
+        z_turned.extend([bank(6, [P, H], "z_turned"), bank(7, [P, H], "z_turned")])
         for c in range(I_TILES):
-            make_da(last, c, last_windows[c])
-        dx = [empty_dx(0, dx_sums[0], "pairs1_1")]
-        regroup(last)
-        last_sums = second_product(last)
-        dx.append(empty_dx(1, dx_sums[1], "pairs2_1"))
+            for b in range(last * HALVES, BLOCKS):
+                nc.tensor.transpose(z_turned[b][:, c * P : (c + 1) * P], z_block(last_windows, b)(c), ident[:])
+        for b in range(last * HALVES, BLOCKS):
+            da.append(make_da(b, z_turned[b], da_last[:, b % HALVES]))
+        middle_sums = second_product(1, 4, "minus_d4")
+        for b in range(last * HALVES, BLOCKS):
+            regroup(b, da[b])
+        out_rows = [keep([P, T], F32, "out_rows0"), keep([P, T], F32, "out_rows1", "minus_d5")]
+        last_sums = second_product(last, 5)
+        dx.append(empty_dx(1, middle_sums, "wgt_planes2"))
         dx.append(empty_dx(last, last_sums))
         for g in range(G):
             for k in range(K_TILES):

@@ -94,7 +94,8 @@ def tile_moe_hib_silu_kernel(
         for q in range(P // QUAD):
             rows = dy_scales[0, SCALE_ROWS * q : SCALE_ROWS * (q + 1), :].bitcast(I32)
             repeated = rows.unsqueeze(0).to_broadcast([QUAD // SCALE_ROWS, SCALE_ROWS, T // 4])
-            nc.sync.dma_start(dy_s[QUAD * q : QUAD * (q + 1), 0:T].bitcast(I32), repeated)
+            queue = nc.scalar if q % 2 else nc.sync
+            queue.dma_start(dy_s[QUAD * q : QUAD * (q + 1), 0:T].bitcast(I32), repeated)
         nc.sync.dma_start(dy_w[:, 0:T], dy_words[0].rearrange("p t d -> p (t d)").bitcast(I32))
         load_wet_words(0, 2)
         load_gate(0)
@@ -102,14 +103,13 @@ def tile_moe_hib_silu_kernel(
             rows = wet_scales[:, 0, r : N // 32 : SCALE_ROWS, :].rearrange("e q h -> q e h")
             nc.sync.dma_start(wet_s[r:P:QUAD, :, :].bitcast(I32), rows.bitcast(I32))
         nc.sync.dma_start(offs2_list[:], offs2)
-        load_wet_words(2, 4)
-        load_a(0)
+        load_wet_words(2, E)
         load_gate(1)
+        load_a(0)
         load_a(1)
-        load_wet_words(4, E)
+        load_gate(2)
         for g in range(G):
             nc.sync.dma_start(wgt_planes[g][:], wgt[g].rearrange("(p t) k -> p t k", t=PACK))
-        load_gate(2)
         nc.sync.dma_start(offs_list[:], offs)
 
         def entries(list_tile, lo, hi):
@@ -126,9 +126,11 @@ def tile_moe_hib_silu_kernel(
 
         sums_out = keep([P, I_TILES, T], F32, "sums_out")
 
-        def first_product(e, cuts, number=None):
+        last_first = keep([P, C1], F32, "last_first")
+
+        def first_product(e, cuts):
             for lo, hi in cuts:
-                sums = bank(next_turn() if number is None else number, [P, hi - lo, C2], "sums")
+                sums = bank(next_turn(), [P, hi - lo, C2], "sums")
                 for c in range(lo, hi):
                     nc.tensor.matmul_mx(
                         out=sums[:, c - lo, :],
@@ -139,7 +141,10 @@ def tile_moe_hib_silu_kernel(
                         start=True,
                         stop=True,
                     )
-                nc.scalar.copy(sums_out[:, lo:hi, e * C2 : (e + 1) * C2], sums[:])
+                if e >= 4 and lo == 0:
+                    nc.scalar.copy(last_first[:, (e - 4) * C2 : (e - 3) * C2], sums[:, 0, :])
+                else:
+                    nc.scalar.copy(sums_out[:, lo:hi, e * C2 : (e + 1) * C2], sums[:])
 
         last = G - 1
         z_back = [keep([P, T], F32, "z_back%d" % c) for c in range(I_TILES)]
@@ -147,7 +152,8 @@ def tile_moe_hib_silu_kernel(
         def scatter_z(window, c, cut):
             lo, hi = (e * C2 for e in Z_CUTS[cut])
             scattered = window[:].indirect(entries(offs2_list, lo, hi))
-            nc.vector.tensor_tensor(scattered, sums_out[:, c, lo:hi], gates[cut][:], ALU.mult)
+            source = last_first[:] if (c, cut) == (0, 2) else sums_out[:, c, lo:hi]
+            nc.vector.tensor_tensor(scattered, source, gates[cut][:], ALU.mult)
 
         def turn(number, name, block_of):
             turned = bank(number, [P, H], name)
@@ -215,6 +221,11 @@ def tile_moe_hib_silu_kernel(
             first_product(e, WHOLE)
         for c in range(I_TILES):
             scatter_z(z_back[c], c, 1)
+        for e in range(4, E):
+            first_product(e, FIRST_EXPERT_CUTS)
+        last_windows = [keep([P, T], F32, "z_last%d" % c) for c in range(2)]
+        for c in range(2):
+            scatter_z(last_windows[c], c, 2)
 
         sigmoid_rows = keep([P, I_TILES, T // 2], F32, "sigmoid_rows")
         nc.scalar.activation(sigmoid_rows[:], a_halves[0][:], ACT.Sigmoid, scale=one)
@@ -236,7 +247,7 @@ def tile_moe_hib_silu_kernel(
             nc.gpsimd.tensor_tensor(minus_d[b][:], less_one[:], sigmoid[b][:], ALU.mult)
 
         make_silu(3)
-        minus_d_on_gpsimd(3, "gate1")
+        minus_d_on_gpsimd(3, "last_first")
         make_silu(4)
         make_silu(5)
         for b, number in enumerate([0, 1, 5]):
@@ -247,8 +258,6 @@ def tile_moe_hib_silu_kernel(
             nc.vector.scalar_tensor_tensor(minus_d[b][:], silu_neg[:, b], 1.0, sigmoid_turned[:], ALU.subtract, ALU.mult)
         minus_d_on_gpsimd(4)
         minus_d_on_gpsimd(5)
-        first_product(4, WHOLE, 0)
-        first_product(5, WHOLE, 1)
 
         def z_block(windows, b):
             return lambda c: windows[c][:, b * P : (b + 1) * P]
@@ -266,10 +275,8 @@ def tile_moe_hib_silu_kernel(
                 regroup(b, da[b])
         dx = [empty_dx(0, second_product(0, 3))]
         weave_wgt(last, "codes0")
-        last_windows = [
-            keep([P, T], F32, "z_last%d" % c, on) for c, on in enumerate(["minus_d2", "gate1", "wgt_planes1", "da3"])
-        ]
-        for c in range(I_TILES):
+        for c, on in [(2, "minus_d2"), (3, "wgt_planes1")]:
+            last_windows.append(keep([P, T], F32, "z_last%d" % c, on))
             scatter_z(last_windows[c], c, 2)
         da_last = keep([P, HALVES, H], BF16, "da_last", "wgt_planes2")
         z_turned.extend([bank(6, [P, H], "z_turned"), bank(7, [P, H], "z_turned")])

@@ -15,14 +15,18 @@ SCALE_ROWS = 4
 PER_COL = 16
 K_TILES = K // P
 I_TILES = H // P
+BLOCKS = T // P
 HALVES = C1 // P
+LAST = G - 1
+LAST_EXPERTS = range(E - E // G, E)
 
 WINDOW = 1024
 WORD_CUTS = [(0, C2), (C2, T)]
-Z_CUTS = [(0, 1), (1, 4), (4, E)]
-BLOCKS = T // P
+EXPERT_CUTS = [(0, 1), (1, LAST_EXPERTS.start), (LAST_EXPERTS.start, E)]
+FIRST_CUT, MIDDLE_CUT, LAST_CUT = range(len(EXPERT_CUTS))
+EARLY_TILES = 2
 ON_VECTOR = 3
-FIRST_EXPERT_CUTS = [(0, 1), (1, I_TILES)]
+TILE_0_APART = [(0, 1), (1, I_TILES)]
 WHOLE = [(0, I_TILES)]
 
 F32 = mybir.dt.float32
@@ -51,12 +55,6 @@ def tile_moe_hib_silu_kernel(
         def bank(number, shape, name):
             return psum.tile(shape, F32, name=name, tag="bank%d" % number)
 
-        taken = []
-
-        def next_turn():
-            taken.append(len(taken) % 2)
-            return taken[-1]
-
         dst_list = held.tile([P, T // PER_COL], U16, name="dst_list")
         offs2_list = held.tile([P, T // PER_COL], U16, name="offs2_list")
         offs_list = held.tile([P, T // PER_COL], U16, name="offs_list")
@@ -64,7 +62,7 @@ def tile_moe_hib_silu_kernel(
         dy_s = keep([P, WINDOW], U8, "dy_s")
         wet_w = keep([P, E, 2 * H], U8, "wet_w")
         wet_s = keep([P, E, H], U8, "wet_s")
-        gates = [keep([P, (end - first) * C2], F32, "gate%d" % first) for first, end in Z_CUTS]
+        gate_rows = keep([P, T], F32, "gate_rows")
         a_halves = [keep([P, I_TILES, T // 2], F32, "a_half%d" % half) for half in range(2)]
         wgt_planes = [keep([P, PACK, K], F32, "wgt_planes%d" % g) for g in range(G)]
         ident = keep([P, P], F32, "ident")
@@ -72,19 +70,19 @@ def tile_moe_hib_silu_kernel(
         nc.vector.memset(wet_s[:].rearrange("p e h -> p (e h)").bitcast(I32), 0)
         nc.vector.memset(dy_w[:, T:], 0)
         nc.vector.memset(dy_s[:, T:].bitcast(I32), 0)
-        zero = held.tile([P, 2], F32, name="zero")
-        nc.vector.memset(zero[:, 0:1], 64.0)
-        nc.scalar.activation(zero[:, 1:2], zero[:, 0:1], ACT.Sigmoid)
-        one = zero[:, 1:2]
+        unit = held.tile([P, 2], F32, name="unit")
+        nc.vector.memset(unit[:, 0:1], 64.0)
+        nc.scalar.activation(unit[:, 1:2], unit[:, 0:1], ACT.Sigmoid)
+        one = unit[:, 1:2]
         make_identity(nc, ident[:])
 
-        def load_wet_words(lo, hi):
+        def load_wet_words(cut):
+            lo, hi = EXPERT_CUTS[cut]
             source = wet_words[lo:hi, 0].rearrange("e p b -> p e b")
             nc.sync.dma_start(wet_w[:, lo:hi, :].bitcast(I32), source.bitcast(I32))
 
-        def load_gate(cut):
-            first, end = Z_CUTS[cut]
-            nc.sync.dma_start(gates[cut][:], gate[:, first * C2 : end * C2])
+        def load_gate(lo, hi):
+            nc.sync.dma_start(gate_rows[:, lo:hi], gate[:, lo:hi])
 
         def load_a(half):
             columns = a[:, half * T // 2 : (half + 1) * T // 2]
@@ -97,17 +95,17 @@ def tile_moe_hib_silu_kernel(
             queue = nc.scalar if q % 2 else nc.sync
             queue.dma_start(dy_s[QUAD * q : QUAD * (q + 1), 0:T].bitcast(I32), repeated)
         nc.sync.dma_start(dy_w[:, 0:T], dy_words[0].rearrange("p t d -> p (t d)").bitcast(I32))
-        load_wet_words(0, 2)
-        load_gate(0)
+        load_wet_words(FIRST_CUT)
+        load_gate(0, C2)
         for r in range(SCALE_ROWS):
             rows = wet_scales[:, 0, r : N // 32 : SCALE_ROWS, :].rearrange("e q h -> q e h")
             nc.sync.dma_start(wet_s[r:P:QUAD, :, :].bitcast(I32), rows.bitcast(I32))
         nc.sync.dma_start(offs2_list[:], offs2)
-        load_wet_words(2, E)
-        load_gate(1)
+        load_wet_words(MIDDLE_CUT)
+        load_gate(C2, T)
+        load_wet_words(LAST_CUT)
         load_a(0)
         load_a(1)
-        load_gate(2)
         for g in range(G):
             nc.sync.dma_start(wgt_planes[g][:], wgt[g].rearrange("(p t) k -> p t k", t=PACK))
         nc.sync.dma_start(offs_list[:], offs)
@@ -125,12 +123,13 @@ def tile_moe_hib_silu_kernel(
                 slot_words[e] = words[:, e * C2 - lo : (e + 1) * C2 - lo]
 
         sums_out = keep([P, I_TILES, T], F32, "sums_out")
-
         last_first = keep([P, C1], F32, "last_first")
+        banks_filled = []
 
         def first_product(e, cuts):
             for lo, hi in cuts:
-                sums = bank(next_turn(), [P, hi - lo, C2], "sums")
+                sums = bank(len(banks_filled) % 2, [P, hi - lo, C2], "sums")
+                banks_filled.append(sums)
                 for c in range(lo, hi):
                     nc.tensor.matmul_mx(
                         out=sums[:, c - lo, :],
@@ -141,19 +140,19 @@ def tile_moe_hib_silu_kernel(
                         start=True,
                         stop=True,
                     )
-                if e >= 4 and lo == 0:
-                    nc.scalar.copy(last_first[:, (e - 4) * C2 : (e - 3) * C2], sums[:, 0, :])
+                if e in LAST_EXPERTS and lo == 0:
+                    place = e - LAST_EXPERTS.start
+                    nc.scalar.copy(last_first[:, place * C2 : (place + 1) * C2], sums[:, 0, :])
                 else:
                     nc.scalar.copy(sums_out[:, lo:hi, e * C2 : (e + 1) * C2], sums[:])
 
-        last = G - 1
         z_back = [keep([P, T], F32, "z_back%d" % c) for c in range(I_TILES)]
 
         def scatter_z(window, c, cut):
-            lo, hi = (e * C2 for e in Z_CUTS[cut])
+            lo, hi = (e * C2 for e in EXPERT_CUTS[cut])
             scattered = window[:].indirect(entries(offs2_list, lo, hi))
-            source = last_first[:] if (c, cut) == (0, 2) else sums_out[:, c, lo:hi]
-            nc.vector.tensor_tensor(scattered, source, gates[cut][:], ALU.mult)
+            source = last_first[:] if (c, cut) == (0, LAST_CUT) else sums_out[:, c, lo:hi]
+            nc.vector.tensor_tensor(scattered, source, gate_rows[:, lo:hi], ALU.mult)
 
         def turn(number, name, block_of):
             turned = bank(number, [P, H], name)
@@ -161,8 +160,19 @@ def tile_moe_hib_silu_kernel(
                 nc.tensor.transpose(turned[:, c * P : (c + 1) * P], block_of(c), ident[:])
             return turned
 
+        def turn_group(g, windows):
+            turned = [bank(6 + half, [P, H], "z_turned") for half in range(HALVES)]
+            for c in range(I_TILES):
+                for half in range(HALVES):
+                    block = z_block(windows, g * HALVES + half)(c)
+                    nc.tensor.transpose(turned[half][:, c * P : (c + 1) * P], block, ident[:])
+            return turned
+
         def a_block(b):
             return lambda c: a_halves[b // ON_VECTOR][:, c, b % ON_VECTOR * P : (b % ON_VECTOR + 1) * P]
+
+        def z_block(windows, b):
+            return lambda c: windows[c][:, b * P : (b + 1) * P]
 
         woven = {}
 
@@ -173,26 +183,27 @@ def tile_moe_hib_silu_kernel(
                 wgt_planes[g][:].rearrange("p t (c i) -> p c t i", i=4),
             )
 
-        def make_da(b, z_turned, da):
-            nc.vector.scalar_tensor_tensor(da, z_turned[:], -1.0, minus_d[b][:], ALU.mult, ALU.mult)
-            return da
+        def make_da(b, part):
+            nc.vector.scalar_tensor_tensor(
+                da[b][:, part], z_turned[b][:, part], -1.0, minus_d[b][:, part], ALU.mult, ALU.mult
+            )
 
-        def regroup(b, da):
+        def regroup(b):
             by_word = bank(b % 2, [P, 2, P], "by_word")
-            pairs = da.bitcast(F32)
+            pairs = da[b].bitcast(F32)
             for u in range(2):
                 nc.tensor.transpose(by_word[:, u, :], pairs[:, u : H // 2 : 2], ident[:])
             first = K + b % HALVES * P
             columns = woven[b // HALVES][:, first : first + P, :].rearrange("p s t -> p (s t)").bitcast(F32)
             nc.scalar.copy(columns.rearrange("p (s u) -> p s u", u=2), by_word[:].rearrange("p u s -> p s u"))
 
-        def second_product(g, number, on=None):
+        def second_product(g, on=None):
             codes = keep([P, K + C1], U32, "codes%d" % g, on)
             scales = keep([P, K + C1], U8, "scales%d" % g)
             nc.vector.quantize_mx(
                 out=codes[:].bitcast(FP8X4), scales=scales[:], in_=woven[g][:].rearrange("p c t -> p (c t)")
             )
-            dx_sums = bank(number, [P, K_TILES, C1], "dx_sums")
+            dx_sums = bank(3 + g, [P, K_TILES, C1], "dx_sums")
             for k in range(K_TILES):
                 nc.tensor.matmul_mx(
                     out=dx_sums[:, k, :],
@@ -206,26 +217,26 @@ def tile_moe_hib_silu_kernel(
             return dx_sums
 
         def empty_dx(g, dx_sums, on=None):
-            dx = keep([P, K_TILES, C1], F32, "dx%d" % g, on)
-            nc.scalar.copy(dx[:], dx_sums[:])
-            return dx
+            dx_rows = keep([P, K_TILES, C1], F32, "dx%d" % g, on)
+            nc.scalar.copy(dx_rows[:], dx_sums[:])
+            return dx_rows
 
-        def scatter_dx(g, k, dx):
+        def scatter_dx(g, k):
             window = out_rows[k][:].indirect(entries(offs_list, g * C1, (g + 1) * C1))
-            nc.vector.tensor_copy(window, dx[:, k, :])
+            nc.vector.tensor_copy(window, dx[g][:, k, :])
 
-        first_product(0, FIRST_EXPERT_CUTS)
+        first_product(0, TILE_0_APART)
         for c in range(I_TILES):
-            scatter_z(z_back[c], c, 0)
-        for e in range(1, 4):
+            scatter_z(z_back[c], c, FIRST_CUT)
+        for e in range(*EXPERT_CUTS[MIDDLE_CUT]):
             first_product(e, WHOLE)
         for c in range(I_TILES):
-            scatter_z(z_back[c], c, 1)
-        for e in range(4, E):
-            first_product(e, FIRST_EXPERT_CUTS)
-        last_windows = [keep([P, T], F32, "z_last%d" % c) for c in range(2)]
-        for c in range(2):
-            scatter_z(last_windows[c], c, 2)
+            scatter_z(z_back[c], c, MIDDLE_CUT)
+        for e in LAST_EXPERTS:
+            first_product(e, TILE_0_APART)
+        last_windows = [keep([P, T], F32, "z_last%d" % c) for c in range(EARLY_TILES)]
+        for c in range(EARLY_TILES):
+            scatter_z(last_windows[c], c, LAST_CUT)
 
         sigmoid_rows = keep([P, I_TILES, T // 2], F32, "sigmoid_rows")
         nc.scalar.activation(sigmoid_rows[:], a_halves[0][:], ACT.Sigmoid, scale=one)
@@ -246,54 +257,54 @@ def tile_moe_hib_silu_kernel(
             minus_d.setdefault(b, keep([P, H], F32, "minus_d%d" % b, on))
             nc.gpsimd.tensor_tensor(minus_d[b][:], less_one[:], sigmoid[b][:], ALU.mult)
 
-        make_silu(3)
-        minus_d_on_gpsimd(3, "last_first")
-        make_silu(4)
-        make_silu(5)
+        make_silu(ON_VECTOR)
+        minus_d_on_gpsimd(ON_VECTOR, "last_first")
+        for b in range(ON_VECTOR + 1, BLOCKS):
+            make_silu(b)
         for b, number in enumerate([0, 1, 5]):
             a_turned.setdefault(b, turn(number, "a_turned", a_block(b)))
             make_silu(b)
             sigmoid_turned = turn(2 + b, "sigmoid", lambda c, b=b: sigmoid_rows[:, c, b * P : (b + 1) * P])
             minus_d.setdefault(b, keep([P, H], F32, "minus_d%d" % b))
             nc.vector.scalar_tensor_tensor(minus_d[b][:], silu_neg[:, b], 1.0, sigmoid_turned[:], ALU.subtract, ALU.mult)
-        minus_d_on_gpsimd(4)
-        minus_d_on_gpsimd(5)
+        for b in range(ON_VECTOR + 1, BLOCKS):
+            minus_d_on_gpsimd(b)
 
-        def z_block(windows, b):
-            return lambda c: windows[c][:, b * P : (b + 1) * P]
-
-        z_turned = [bank(6, [P, H], "z_turned"), bank(7, [P, H], "z_turned")]
-        for c in range(I_TILES):
-            for b in range(HALVES):
-                nc.tensor.transpose(z_turned[b][:, c * P : (c + 1) * P], z_block(z_back, b)(c), ident[:])
+        z_turned = turn_group(0, z_back)
         z_turned.append(turn(2, "z_turned", z_block(z_back, 2)))
         z_turned.append(turn(5, "z_turned", z_block(z_back, 3)))
-        da = [make_da(b, z_turned[b], keep([P, H], BF16, "da%d" % b)[:]) for b in range(last * HALVES)]
-        for g in range(last):
-            weave_wgt(g, ["a_half1", "da1"][g])
+        da = [keep([P, H], BF16, "da%d" % b)[:] for b in range(LAST * HALVES)]
+        for b in range(LAST * HALVES):
+            make_da(b, slice(0, H))
+        for g, on in enumerate(["a_half1", "da1"]):
+            weave_wgt(g, on)
             for b in range(g * HALVES, (g + 1) * HALVES):
-                regroup(b, da[b])
-        dx = [empty_dx(0, second_product(0, 3))]
-        weave_wgt(last, "codes0")
-        for c, on in [(2, "minus_d2"), (3, "wgt_planes1")]:
+                regroup(b)
+        dx = [empty_dx(0, second_product(0))]
+        weave_wgt(LAST, "codes0")
+        for c, on in enumerate(["minus_d2", "wgt_planes1"], EARLY_TILES):
             last_windows.append(keep([P, T], F32, "z_last%d" % c, on))
-            scatter_z(last_windows[c], c, 2)
+            scatter_z(last_windows[c], c, LAST_CUT)
         da_last = keep([P, HALVES, H], BF16, "da_last", "wgt_planes2")
-        z_turned.extend([bank(6, [P, H], "z_turned"), bank(7, [P, H], "z_turned")])
-        for c in range(I_TILES):
-            for b in range(last * HALVES, BLOCKS):
-                nc.tensor.transpose(z_turned[b][:, c * P : (c + 1) * P], z_block(last_windows, b)(c), ident[:])
-        for b in range(last * HALVES, BLOCKS):
-            da.append(make_da(b, z_turned[b], da_last[:, b % HALVES]))
-        middle_sums = second_product(1, 4, "minus_d4")
-        for b in range(last * HALVES, BLOCKS):
-            regroup(b, da[b])
+        z_turned.extend(turn_group(LAST, last_windows))
+        da.extend(da_last[:, half] for half in range(HALVES))
+        end_block = BLOCKS - 1
+        lower, upper = slice(0, H // 2), slice(H // 2, H)
+        minus_z = keep([P, H // 2], F32, "minus_z")
+        nc.scalar.activation(minus_z[:], z_turned[end_block][:, upper], ACT.Copy, scale=-1.0)
+        nc.gpsimd.tensor_tensor(da[end_block][:, upper], minus_z[:], minus_d[end_block][:, upper], ALU.mult)
+        make_da(end_block - 1, slice(0, H))
+        make_da(end_block, lower)
+        middle_sums = second_product(1, "minus_d4")
+        for b in range(LAST * HALVES, BLOCKS):
+            regroup(b)
         out_rows = [keep([P, T], F32, "out_rows0"), keep([P, T], F32, "out_rows1", "minus_d5")]
-        last_sums = second_product(last, 5)
+        last_sums = second_product(LAST)
         dx.append(empty_dx(1, middle_sums, "wgt_planes2"))
-        dx.append(empty_dx(last, last_sums))
-        for g in range(G):
+        dx.append(empty_dx(LAST, last_sums))
+        for g in range(LAST):
             for k in range(K_TILES):
-                scatter_dx(g, k, dx[g])
-                if g == last:
-                    nc.sync.dma_start(out[k * P : (k + 1) * P, :], out_rows[k][:])
+                scatter_dx(g, k)
+        for k in range(K_TILES):
+            scatter_dx(LAST, k)
+            nc.sync.dma_start(out[k * P : (k + 1) * P, :], out_rows[k][:])

@@ -15,19 +15,10 @@ SCALE_ROWS = 4
 PER_COL = 16
 K_TILES = K // P
 I_TILES = H // P
-BLOCKS = T // P
 HALVES = C1 // P
-LAST = G - 1
-LAST_EXPERTS = range(E - E // G, E)
+
 
 WINDOW = 1024
-WORD_CUTS = [(0, C2), (C2, T)]
-EXPERT_CUTS = [(0, 1), (1, LAST_EXPERTS.start), (LAST_EXPERTS.start, E)]
-FIRST_CUT, MIDDLE_CUT, LAST_CUT = range(len(EXPERT_CUTS))
-EARLY_TILES = 2
-ON_VECTOR = 3
-TILE_0_APART = [(0, 1), (1, I_TILES)]
-WHOLE = [(0, I_TILES)]
 
 F32 = mybir.dt.float32
 BF16 = mybir.dt.bfloat16
@@ -60,10 +51,10 @@ def tile_moe_hib_silu_kernel(
         offs_list = held.tile([P, T // PER_COL], U16, name="offs_list")
         dy_w = keep([P, WINDOW], I32, "dy_w")
         dy_s = keep([P, WINDOW], U8, "dy_s")
-        wet_w = keep([P, E, 2 * H], U8, "wet_w")
+        wet_w = [keep([P, HALVES, 2 * H], U8, "wet_w%d" % g) for g in range(G)]
         wet_s = keep([P, E, H], U8, "wet_s")
         gate_rows = keep([P, T], F32, "gate_rows")
-        a_halves = [keep([P, I_TILES, T // 2], F32, "a_half%d" % half) for half in range(2)]
+        a_rows = [keep([P, I_TILES, C1], F32, "a_rows%d" % g) for g in range(G)]
         wgt_planes = [keep([P, PACK, K], F32, "wgt_planes%d" % g) for g in range(G)]
         ident = keep([P, P], F32, "ident")
 
@@ -76,17 +67,12 @@ def tile_moe_hib_silu_kernel(
         one = unit[:, 1:2]
         make_identity(nc, ident[:])
 
-        def load_wet_words(cut):
-            lo, hi = EXPERT_CUTS[cut]
-            source = wet_words[lo:hi, 0].rearrange("e p b -> p e b")
-            nc.sync.dma_start(wet_w[:, lo:hi, :].bitcast(I32), source.bitcast(I32))
+        def load_wet_words(g):
+            source = wet_words[g * HALVES : (g + 1) * HALVES, 0].rearrange("e p b -> p e b")
+            nc.sync.dma_start(wet_w[g][:].bitcast(I32), source.bitcast(I32))
 
         def load_gate(lo, hi):
             nc.sync.dma_start(gate_rows[:, lo:hi], gate[:, lo:hi])
-
-        def load_a(half):
-            columns = a[:, half * T // 2 : (half + 1) * T // 2]
-            nc.sync.dma_start(a_halves[half][:], columns.rearrange("(c p) j -> p c j", p=P))
 
         nc.sync.dma_start(dst_list[:], dst)
         for q in range(P // QUAD):
@@ -95,118 +81,135 @@ def tile_moe_hib_silu_kernel(
             queue = nc.scalar if q % 2 else nc.sync
             queue.dma_start(dy_s[QUAD * q : QUAD * (q + 1), 0:T].bitcast(I32), repeated)
         nc.sync.dma_start(dy_w[:, 0:T], dy_words[0].rearrange("p t d -> p (t d)").bitcast(I32))
-        load_wet_words(FIRST_CUT)
-        load_gate(0, C2)
+        load_wet_words(0)
+        load_gate(0, C1)
         for r in range(SCALE_ROWS):
             rows = wet_scales[:, 0, r : N // 32 : SCALE_ROWS, :].rearrange("e q h -> q e h")
             nc.sync.dma_start(wet_s[r:P:QUAD, :, :].bitcast(I32), rows.bitcast(I32))
         nc.sync.dma_start(offs2_list[:], offs2)
-        load_wet_words(MIDDLE_CUT)
-        load_gate(C2, T)
-        load_wet_words(LAST_CUT)
-        load_a(0)
-        load_a(1)
+        load_wet_words(1)
+        load_gate(C1, T)
+        load_wet_words(2)
         for g in range(G):
+            columns = a[:, g * C1 : (g + 1) * C1]
+            nc.sync.dma_start(a_rows[g][:], columns.rearrange("(c p) j -> p c j", p=P))
             nc.sync.dma_start(wgt_planes[g][:], wgt[g].rearrange("(p t) k -> p t k", t=PACK))
         nc.sync.dma_start(offs_list[:], offs)
 
         def entries(list_tile, lo, hi):
             return list_tile[:, lo // PER_COL : hi // PER_COL]
 
-        slot_words = {}
         scale_bytes = keep([P, T], U8, "scale_bytes")
         nc.vector.tensor_copy(scale_bytes[:], dy_s[:].indirect(dst_list[:]))
-        for lo, hi in WORD_CUTS:
-            words = keep([P, hi - lo], U32, "words%d" % lo)
-            nc.vector.tensor_copy(words[:], dy_w[:].bitcast(U32).indirect(entries(dst_list, lo, hi)))
-            for e in range(lo // C2, hi // C2):
-                slot_words[e] = words[:, e * C2 - lo : (e + 1) * C2 - lo]
 
-        sums_out = keep([P, I_TILES, T], F32, "sums_out")
-        last_first = keep([P, C1], F32, "last_first")
-        banks_filled = []
+        def gather_words(g, on=None):
+            words = keep([P, C1], U32, "words%d" % g, on)
+            nc.vector.tensor_copy(words[:], dy_w[:].bitcast(U32).indirect(entries(dst_list, g * C1, (g + 1) * C1)))
+            return words
 
-        def first_product(e, cuts):
-            for lo, hi in cuts:
-                sums = bank(len(banks_filled) % 2, [P, hi - lo, C2], "sums")
-                banks_filled.append(sums)
-                for c in range(lo, hi):
+        def first_product(g, words, places):
+            for c in range(I_TILES):
+                for half in range(HALVES):
+                    e = g * HALVES + half
                     nc.tensor.matmul_mx(
-                        out=sums[:, c - lo, :],
-                        lhsT=wet_w[:, e, 2 * P * c : 2 * P * (c + 1)].bitcast(FP4X4),
+                        out=places[c][:, half * C2 : (half + 1) * C2],
+                        lhsT=wet_w[g][:, half, 2 * P * c : 2 * P * (c + 1)].bitcast(FP4X4),
                         lhsT_scale=wet_s[:, e, P * c : P * (c + 1)],
-                        rhs=slot_words[e].bitcast(FP8X4),
+                        rhs=words[:, half * C2 : (half + 1) * C2].bitcast(FP8X4),
                         rhs_scale=scale_bytes[:, e * C2 : (e + 1) * C2],
                         start=True,
                         stop=True,
                     )
-                if e in LAST_EXPERTS and lo == 0:
-                    place = e - LAST_EXPERTS.start
-                    nc.scalar.copy(last_first[:, place * C2 : (place + 1) * C2], sums[:, 0, :])
-                else:
-                    nc.scalar.copy(sums_out[:, lo:hi, e * C2 : (e + 1) * C2], sums[:])
 
-        z_back = [keep([P, T], F32, "z_back%d" % c) for c in range(I_TILES)]
+        def empty_gated(g, sums, tiles, name):
+            rows = keep([P, tiles, C1], F32, name)
+            gates = gate_rows[:, g * C1 : (g + 1) * C1].unsqueeze(1).to_broadcast([P, tiles, C1])
+            nc.vector.tensor_tensor(rows[:], sums[:], gates, ALU.mult)
+            return rows
 
-        def scatter_z(window, c, cut):
-            lo, hi = (e * C2 for e in EXPERT_CUTS[cut])
-            scattered = window[:].indirect(entries(offs2_list, lo, hi))
-            source = last_first[:] if (c, cut) == (0, LAST_CUT) else sums_out[:, c, lo:hi]
-            nc.vector.tensor_tensor(scattered, source, gate_rows[:, lo:hi], ALU.mult)
+        def empty_plain(sums, tiles, name):
+            rows = keep([P, tiles, C1], F32, name)
+            nc.scalar.copy(rows[:], sums[:])
+            return rows
 
-        def turn(number, name, block_of):
-            turned = bank(number, [P, H], name)
-            for c in range(I_TILES):
-                nc.tensor.transpose(turned[:, c * P : (c + 1) * P], block_of(c), ident[:])
-            return turned
+        z_back = {}
 
-        def turn_group(g, windows):
-            turned = [bank(6 + half, [P, H], "z_turned") for half in range(HALVES)]
+        def scatter_on_scalar(c, g, source, on=None):
+            z_back.setdefault((c, g), keep([P, T], F32, "z_back%d_%d" % (c, g), on))
+            nc.scalar.activation(z_back[c, g][:].indirect(entries(offs2_list, g * C1, (g + 1) * C1)), source, ACT.Copy)
+
+        def scatter_on_vector(c, g, source, on=None):
+            z_back.setdefault((c, g), keep([P, T], F32, "z_back%d_%d" % (c, g), on))
+            scattered = z_back[c, g][:].indirect(entries(offs2_list, g * C1, (g + 1) * C1))
+            nc.vector.tensor_tensor(scattered, source, gate_rows[:, g * C1 : (g + 1) * C1], ALU.mult)
+
+        def turn(numbers, name, block_of):
+            turned = [bank(number, [P, H], name) for number in numbers]
             for c in range(I_TILES):
                 for half in range(HALVES):
-                    block = z_block(windows, g * HALVES + half)(c)
-                    nc.tensor.transpose(turned[half][:, c * P : (c + 1) * P], block, ident[:])
+                    nc.tensor.transpose(turned[half][:, c * P : (c + 1) * P], block_of(c, half), ident[:])
             return turned
 
-        def a_block(b):
-            return lambda c: a_halves[b // ON_VECTOR][:, c, b % ON_VECTOR * P : (b % ON_VECTOR + 1) * P]
+        def turn_a(g, numbers):
+            return turn(numbers, "a_turned", lambda c, half: a_rows[g][:, c, half * P : (half + 1) * P])
 
-        def z_block(windows, b):
-            return lambda c: windows[c][:, b * P : (b + 1) * P]
+        def turn_z(g, numbers):
+            return turn(
+                numbers, "z_turned", lambda c, half: z_back[c, g][:, g * C1 + half * P : g * C1 + (half + 1) * P]
+            )
+
+        def make_sigmoid(g, a_turned, on=None):
+            sigmoid = keep([P, HALVES, H], F32, "sigmoid%d" % g, on)
+            for half in range(HALVES):
+                nc.scalar.activation(sigmoid[:, half], a_turned[half][:], ACT.Sigmoid, scale=one)
+            return sigmoid
+
+        def make_minus_d(g, a_turned, sigmoid, on=(None, None)):
+            inner = [keep([P, H], F32, "inner%d_%d" % (g, half), on[half]) for half in range(HALVES)]
+            minus_d = [keep([P, H], F32, "minus_d%d_%d" % (g, half)) for half in range(HALVES)]
+            for half in range(HALVES):
+                nc.vector.scalar_tensor_tensor(
+                    inner[half][:], sigmoid[:, half], 1.0, a_turned[half][:], ALU.subtract, ALU.mult
+                )
+            for half in range(HALVES):
+                nc.vector.scalar_tensor_tensor(
+                    minus_d[half][:], inner[half][:], 1.0, sigmoid[:, half], ALU.subtract, ALU.mult
+                )
+            return minus_d
+
+        def make_da(g, z_turned, minus_d):
+            da = [keep([P, H], BF16, "da%d_%d" % (g, half)) for half in range(HALVES)]
+            for half in range(HALVES):
+                nc.vector.scalar_tensor_tensor(da[half][:], z_turned[half][:], -1.0, minus_d[half][:], ALU.mult, ALU.mult)
+            return da
 
         woven = {}
 
-        def weave_wgt(g, on):
+        def weave_wgt(g, copy, on=None):
             woven.setdefault(g, keep([P, K + C1, PACK], BF16, "woven%d" % g, on))
-            nc.scalar.copy(
+            copy(
                 woven[g][:, 0:K, :].rearrange("p (c i) t -> p c t i", i=4),
                 wgt_planes[g][:].rearrange("p t (c i) -> p c t i", i=4),
             )
 
-        def make_da(b, part):
-            nc.vector.scalar_tensor_tensor(
-                da[b][:, part], z_turned[b][:, part], -1.0, minus_d[b][:, part], ALU.mult, ALU.mult
-            )
+        def regroup(g, da, number, copy):
+            by_word = bank(number, [P, HALVES, 2, P], "by_word")
+            for half in range(HALVES):
+                pairs = da[half][:].bitcast(F32)
+                for u in range(2):
+                    nc.tensor.transpose(by_word[:, half, u, :], pairs[:, u : H // 2 : 2], ident[:])
+            columns = woven[g][:, K:, :].rearrange("p s t -> p (s t)").bitcast(F32)
+            copy(columns.rearrange("p (b s u) -> p b s u", b=HALVES, u=2), by_word[:].rearrange("p b u s -> p b s u"))
 
-        def regroup(b):
-            by_word = bank(b % 2, [P, 2, P], "by_word")
-            pairs = da[b].bitcast(F32)
-            for u in range(2):
-                nc.tensor.transpose(by_word[:, u, :], pairs[:, u : H // 2 : 2], ident[:])
-            first = K + b % HALVES * P
-            columns = woven[b // HALVES][:, first : first + P, :].rearrange("p s t -> p (s t)").bitcast(F32)
-            nc.scalar.copy(columns.rearrange("p (s u) -> p s u", u=2), by_word[:].rearrange("p u s -> p s u"))
-
-        def second_product(g, on=None):
+        def second_product(g, places, on=None):
             codes = keep([P, K + C1], U32, "codes%d" % g, on)
             scales = keep([P, K + C1], U8, "scales%d" % g)
             nc.vector.quantize_mx(
                 out=codes[:].bitcast(FP8X4), scales=scales[:], in_=woven[g][:].rearrange("p c t -> p (c t)")
             )
-            dx_sums = bank(3 + g, [P, K_TILES, C1], "dx_sums")
             for k in range(K_TILES):
                 nc.tensor.matmul_mx(
-                    out=dx_sums[:, k, :],
+                    out=places[k],
                     lhsT=codes[:, k * P : (k + 1) * P].bitcast(FP8X4),
                     lhsT_scale=scales[:, k * P : (k + 1) * P],
                     rhs=codes[:, K:].bitcast(FP8X4),
@@ -214,97 +217,88 @@ def tile_moe_hib_silu_kernel(
                     start=True,
                     stop=True,
                 )
-            return dx_sums
 
-        def empty_dx(g, dx_sums, on=None):
-            dx_rows = keep([P, K_TILES, C1], F32, "dx%d" % g, on)
-            nc.scalar.copy(dx_rows[:], dx_sums[:])
-            return dx_rows
+        def dx_sums(g, numbers, on=None):
+            sums = [bank(number, [P, C1], "dx_sums") for number in numbers]
+            second_product(g, [sums[k][:] for k in range(K_TILES)], on)
+            return sums
 
-        def scatter_dx(g, k):
-            window = out_rows[k][:].indirect(entries(offs_list, g * C1, (g + 1) * C1))
-            nc.vector.tensor_copy(window, dx[g][:, k, :])
+        def empty_dx(g, k, sums, copy, on=None):
+            rows = keep([P, C1], F32, "dx%d_%d" % (g, k), on)
+            copy(rows[:], sums[k][:])
+            return rows
 
-        first_product(0, TILE_0_APART)
-        for c in range(I_TILES):
-            scatter_z(z_back[c], c, FIRST_CUT)
-        for e in range(*EXPERT_CUTS[MIDDLE_CUT]):
-            first_product(e, WHOLE)
-        for c in range(I_TILES):
-            scatter_z(z_back[c], c, MIDDLE_CUT)
-        for e in LAST_EXPERTS:
-            first_product(e, TILE_0_APART)
-        last_windows = [keep([P, T], F32, "z_last%d" % c) for c in range(EARLY_TILES)]
-        for c in range(EARLY_TILES):
-            scatter_z(last_windows[c], c, LAST_CUT)
+        def dx_window(g, k):
+            return out_rows[k][:].indirect(entries(offs_list, g * C1, (g + 1) * C1))
 
-        sigmoid_rows = keep([P, I_TILES, T // 2], F32, "sigmoid_rows")
-        nc.scalar.activation(sigmoid_rows[:], a_halves[0][:], ACT.Sigmoid, scale=one)
-        a_turned, sigmoid = {}, {}
-        for b in range(ON_VECTOR, BLOCKS):
-            a_turned.setdefault(b, turn(2 + b, "a_turned", a_block(b)))
-            sigmoid.setdefault(b, keep([P, H], F32, "sigmoid%d" % b))
-            nc.scalar.activation(sigmoid[b][:], a_turned[b][:], ACT.Sigmoid, scale=one)
-        silu_neg = keep([P, BLOCKS, H], F32, "silu_neg", "a_half1")
-        minus_d = {}
+        def scatter_dx_on_scalar(g, k, rows):
+            nc.scalar.activation(dx_window(g, k), rows[:], ACT.Copy)
 
-        def make_silu(b):
-            nc.scalar.activation(silu_neg[:, b], a_turned[b][:], ACT.Silu, scale=-1.0)
+        def scatter_dx_on_vector(g, k, rows):
+            nc.vector.tensor_copy(dx_window(g, k), rows[:])
 
-        def minus_d_on_gpsimd(b, on=None):
-            less_one = keep([P, H], F32, "less_one%d" % b)
-            nc.scalar.activation(less_one[:], silu_neg[:, b], ACT.Copy, bias=-1.0)
-            minus_d.setdefault(b, keep([P, H], F32, "minus_d%d" % b, on))
-            nc.gpsimd.tensor_tensor(minus_d[b][:], less_one[:], sigmoid[b][:], ALU.mult)
+        words0, words1 = gather_words(0), gather_words(1)
+        low0, high0 = bank(0, [P, 2, C1], "low0"), bank(1, [P, 2, C1], "high0")
+        first_product(0, words0, [low0[:, 0], low0[:, 1], high0[:, 0], high0[:, 1]])
+        z_low0 = empty_gated(0, low0, 2, "z_low0")
+        z_high0 = empty_plain(high0, 2, "z_high0")
+        words2 = gather_words(2, "words0")
+        low1, high1 = bank(2, [P, 2, C1], "low1"), bank(3, [P, 2, C1], "high1")
+        first_product(1, words1, [low1[:, 0], low1[:, 1], high1[:, 0], high1[:, 1]])
+        z_low1 = empty_gated(1, low1, 2, "z_low1")
+        low2, third2, fourth2 = bank(4, [P, 2, C1], "low2"), bank(5, [P, 1, C1], "third2"), bank(6, [P, 1, C1], "fourth2")
+        first_product(2, words2, [low2[:, 0], low2[:, 1], third2[:, 0], fourth2[:, 0]])
+        scatter_on_scalar(0, 0, z_low0[:, 0])
+        z_high1 = empty_plain(high1, 2, "z_high1")
+        scatter_on_scalar(1, 0, z_low0[:, 1], "wet_w1")
+        z_fourth2 = empty_plain(fourth2, 1, "z_fourth2")
+        for c in range(2):
+            scatter_on_vector(2 + c, 0, z_high0[:, c])
+        z_low2 = empty_gated(2, low2, 2, "z_low2")
+        z_third2 = empty_gated(2, third2, 1, "z_third2")
+        scatter_on_scalar(0, 1, z_low1[:, 0], "wet_w2")
+        scatter_on_scalar(1, 1, z_low1[:, 1], "words0")
+        for c in range(2):
+            scatter_on_vector(2 + c, 1, z_high1[:, c])
+        scatter_on_vector(3, 2, z_fourth2[:, 0])
 
-        make_silu(ON_VECTOR)
-        minus_d_on_gpsimd(ON_VECTOR, "last_first")
-        for b in range(ON_VECTOR + 1, BLOCKS):
-            make_silu(b)
-        for b, number in enumerate([0, 1, 5]):
-            a_turned.setdefault(b, turn(number, "a_turned", a_block(b)))
-            make_silu(b)
-            sigmoid_turned = turn(2 + b, "sigmoid", lambda c, b=b: sigmoid_rows[:, c, b * P : (b + 1) * P])
-            minus_d.setdefault(b, keep([P, H], F32, "minus_d%d" % b))
-            nc.vector.scalar_tensor_tensor(minus_d[b][:], silu_neg[:, b], 1.0, sigmoid_turned[:], ALU.subtract, ALU.mult)
-        for b in range(ON_VECTOR + 1, BLOCKS):
-            minus_d_on_gpsimd(b)
-
-        z_turned = turn_group(0, z_back)
-        z_turned.append(turn(2, "z_turned", z_block(z_back, 2)))
-        z_turned.append(turn(5, "z_turned", z_block(z_back, 3)))
-        da = [keep([P, H], BF16, "da%d" % b)[:] for b in range(LAST * HALVES)]
-        for b in range(LAST * HALVES):
-            make_da(b, slice(0, H))
-        for g, on in enumerate(["a_half1", "da1"]):
-            weave_wgt(g, on)
-            for b in range(g * HALVES, (g + 1) * HALVES):
-                regroup(b)
-        dx = [empty_dx(0, second_product(0))]
-        weave_wgt(LAST, "codes0")
-        for c, on in enumerate(["minus_d2", "wgt_planes1"], EARLY_TILES):
-            last_windows.append(keep([P, T], F32, "z_last%d" % c, on))
-            scatter_z(last_windows[c], c, LAST_CUT)
-        da_last = keep([P, HALVES, H], BF16, "da_last", "wgt_planes2")
-        z_turned.extend(turn_group(LAST, last_windows))
-        da.extend(da_last[:, half] for half in range(HALVES))
-        end_block = BLOCKS - 1
-        lower, upper = slice(0, H // 2), slice(H // 2, H)
-        minus_z = keep([P, H // 2], F32, "minus_z")
-        nc.scalar.activation(minus_z[:], z_turned[end_block][:, upper], ACT.Copy, scale=-1.0)
-        nc.gpsimd.tensor_tensor(da[end_block][:, upper], minus_z[:], minus_d[end_block][:, upper], ALU.mult)
-        make_da(end_block - 1, slice(0, H))
-        make_da(end_block, lower)
-        middle_sums = second_product(1, "minus_d4")
-        for b in range(LAST * HALVES, BLOCKS):
-            regroup(b)
-        out_rows = [keep([P, T], F32, "out_rows0"), keep([P, T], F32, "out_rows1", "minus_d5")]
-        last_sums = second_product(LAST)
-        dx.append(empty_dx(1, middle_sums, "wgt_planes2"))
-        dx.append(empty_dx(LAST, last_sums))
-        for g in range(LAST):
-            for k in range(K_TILES):
-                scatter_dx(g, k)
+        a_turned0 = turn_a(0, [7, 0])
+        a_turned1 = turn_a(1, [1, 2])
+        sigmoid0 = make_sigmoid(0, a_turned0, "z_low0")
+        z_turned0 = turn_z(0, [3, 4])
+        a_turned2 = turn_a(2, [5, 6])
+        weave_wgt(0, nc.vector.tensor_copy)
+        minus_d0 = make_minus_d(0, a_turned0, sigmoid0)
+        da0 = make_da(0, z_turned0, minus_d0)
+        scatter_on_scalar(0, 2, z_low2[:, 0], "a_rows0")
+        sigmoid1 = make_sigmoid(1, a_turned1, "z_low1")
+        scatter_on_scalar(1, 2, z_low2[:, 1], "a_rows1")
+        z_turned1 = turn_z(1, [7, 0])
+        weave_wgt(1, nc.vector.tensor_copy)
+        regroup(0, da0, 3, nc.scalar.copy)
+        sigmoid2 = make_sigmoid(2, a_turned2, "da0_1")
+        minus_d1 = make_minus_d(1, a_turned1, sigmoid1)
+        sums0 = dx_sums(0, [4, 1])
+        scatter_on_scalar(2, 2, z_third2[:, 0], "woven0")
+        da1 = make_da(1, z_turned1, minus_d1)
+        dx0 = [empty_dx(0, k, sums0, nc.scalar.copy) for k in range(K_TILES)]
+        regroup(1, da1, 2, nc.scalar.copy)
+        weave_wgt(2, nc.scalar.copy, "da1_1")
+        z_turned2 = turn_z(2, [0, 7])
+        minus_d2 = make_minus_d(2, a_turned2, sigmoid2)
+        out_rows = [keep([P, T], F32, "out_rows0", "minus_d2_0"), keep([P, T], F32, "out_rows1", "wgt_planes2")]
+        scatter_dx_on_scalar(0, 1, dx0[1])
+        sums1 = dx_sums(1, [3, 4])
+        da2 = make_da(2, z_turned2, minus_d2)
+        regroup(2, da2, 2, nc.scalar.copy)
+        dx1 = keep([P, K_TILES, C1], F32, "dx1", "da2_1")
+        for k in reversed(range(K_TILES)):
+            nc.scalar.copy(dx1[:, k], sums1[k][:])
+        scatter_dx_on_vector(0, 0, dx0[0])
+        sums2 = dx_sums(2, [5, 6])
+        scatter_dx_on_scalar(1, 1, dx1[:, 1])
+        scatter_dx_on_vector(1, 0, dx1[:, 0])
+        scatter_dx_on_vector(2, 0, empty_dx(2, 0, sums2, nc.vector.tensor_copy))
+        scatter_dx_on_scalar(2, 1, empty_dx(2, 1, sums2, nc.scalar.copy))
         for k in range(K_TILES):
-            scatter_dx(LAST, k)
             nc.sync.dma_start(out[k * P : (k + 1) * P, :], out_rows[k][:])

@@ -99,8 +99,13 @@ def tile_moe_hib_silu_kernel(
         def entries(list_tile, lo, hi):
             return list_tile[:, lo // PER_COL : hi // PER_COL]
 
-        scale_bytes = keep([P, T], U8, "scale_bytes")
-        nc.vector.tensor_copy(scale_bytes[:], dy_s[:].indirect(dst_list[:]))
+        slot_scales = {}
+
+        def gather_scales(lo, hi):
+            scale_bytes = keep([P, (hi - lo) * C1], U8, "scale_bytes%d" % lo)
+            nc.vector.tensor_copy(scale_bytes[:], dy_s[:].indirect(entries(dst_list, lo * C1, hi * C1)))
+            for g in range(lo, hi):
+                slot_scales.setdefault(g, scale_bytes[:, (g - lo) * C1 : (g - lo + 1) * C1])
 
         def gather_words(g, on=None):
             words = keep([P, C1], U32, "words%d" % g, on)
@@ -112,36 +117,40 @@ def tile_moe_hib_silu_kernel(
                 for half in range(HALVES):
                     e = g * HALVES + half
                     nc.tensor.matmul_mx(
-                        out=places[c][:, half * C2 : (half + 1) * C2],
+                        out=places[c][half],
                         lhsT=wet_w[g][:, half, 2 * P * c : 2 * P * (c + 1)].bitcast(FP4X4),
                         lhsT_scale=wet_s[:, e, P * c : P * (c + 1)],
                         rhs=words[:, half * C2 : (half + 1) * C2].bitcast(FP8X4),
-                        rhs_scale=scale_bytes[:, e * C2 : (e + 1) * C2],
+                        rhs_scale=slot_scales[g][:, half * C2 : (half + 1) * C2],
                         start=True,
                         stop=True,
                     )
 
-        def empty_gated(g, sums, tiles, name):
-            rows = keep([P, tiles, C1], F32, name)
-            gates = gate_rows[:, g * C1 : (g + 1) * C1].unsqueeze(1).to_broadcast([P, tiles, C1])
+        def by_expert(columns):
+            return [columns[:, half * C2 : (half + 1) * C2] for half in range(HALVES)]
+
+        def empty_gated(g, sums, rows):
+            gates = gate_rows[:, g * C1 : (g + 1) * C1].unsqueeze(1).to_broadcast([P, 2, C1])
             nc.vector.tensor_tensor(rows[:], sums[:], gates, ALU.mult)
             return rows
 
-        def empty_plain(sums, tiles, name):
-            rows = keep([P, tiles, C1], F32, name)
-            nc.scalar.copy(rows[:], sums[:])
+        def empty_plain(sums, name):
+            rows = keep(list(sums.shape), F32, name)
+            nc.scalar.copy(rows[:], sums)
             return rows
 
         z_back = {}
 
-        def scatter_on_scalar(c, g, source, on=None):
-            z_back.setdefault((c, g), keep([P, T], F32, "z_back%d_%d" % (c, g), on))
-            nc.scalar.activation(z_back[c, g][:].indirect(entries(offs2_list, g * C1, (g + 1) * C1)), source, ACT.Copy)
+        def z_window(c, g, lo, hi, on):
+            if (c, g) not in z_back:
+                z_back.setdefault((c, g), keep([P, T], F32, "z_back%d_%d" % (c, g), on))
+            return z_back[c, g][:].indirect(entries(offs2_list, g * C1 + lo, g * C1 + hi))
 
-        def scatter_on_vector(c, g, source, on=None):
-            z_back.setdefault((c, g), keep([P, T], F32, "z_back%d_%d" % (c, g), on))
-            scattered = z_back[c, g][:].indirect(entries(offs2_list, g * C1, (g + 1) * C1))
-            nc.vector.tensor_tensor(scattered, source, gate_rows[:, g * C1 : (g + 1) * C1], ALU.mult)
+        def scatter_on_scalar(c, g, source, on=None, lo=0, hi=C1):
+            nc.scalar.activation(z_window(c, g, lo, hi, on), source, ACT.Copy)
+
+        def scatter_on_vector(c, g, source, on=None, lo=0, hi=C1):
+            nc.vector.tensor_tensor(z_window(c, g, lo, hi, on), source, gate_rows[:, g * C1 + lo : g * C1 + hi], ALU.mult)
 
         def turn(numbers, name, block_of):
             turned = [bank(number, [P, H], name) for number in numbers]
@@ -164,17 +173,16 @@ def tile_moe_hib_silu_kernel(
                 nc.scalar.activation(sigmoid[:, half], a_turned[half][:], ACT.Sigmoid, scale=one)
             return sigmoid
 
-        def make_minus_d(g, a_turned, sigmoid, on=(None, None)):
-            inner = [keep([P, H], F32, "inner%d_%d" % (g, half), on[half]) for half in range(HALVES)]
-            minus_d = [keep([P, H], F32, "minus_d%d_%d" % (g, half)) for half in range(HALVES)]
+        def make_inner(a_turned, sigmoid, inner):
             for half in range(HALVES):
                 nc.vector.scalar_tensor_tensor(
-                    inner[half][:], sigmoid[:, half], 1.0, a_turned[half][:], ALU.subtract, ALU.mult
+                    inner[:, half], sigmoid[:, half], 1.0, a_turned[half][:], ALU.subtract, ALU.mult
                 )
-            for half in range(HALVES):
-                nc.vector.scalar_tensor_tensor(
-                    minus_d[half][:], inner[half][:], 1.0, sigmoid[:, half], ALU.subtract, ALU.mult
-                )
+            return inner
+
+        def make_minus_d(g, half, inner, sigmoid):
+            minus_d = keep([P, H], F32, "minus_d%d_%d" % (g, half))
+            nc.vector.scalar_tensor_tensor(minus_d[:], inner[:, half], 1.0, sigmoid[:, half], ALU.subtract, ALU.mult)
             return minus_d
 
         def make_da(g, z_turned, minus_d):
@@ -185,12 +193,10 @@ def tile_moe_hib_silu_kernel(
 
         woven = {}
 
-        def weave_wgt(g, copy, on=None):
+        def weave_wgt(g, on):
             woven.setdefault(g, keep([P, K + C1, PACK], BF16, "woven%d" % g, on))
-            copy(
-                woven[g][:, 0:K, :].rearrange("p (c i) t -> p c t i", i=4),
-                wgt_planes[g][:].rearrange("p t (c i) -> p c t i", i=4),
-            )
+            planes = wgt_planes[g][:].rearrange("p t k -> p k t")
+            nc.gpsimd.tensor_scalar(woven[g][:, 0:K, :], planes, 1.0, 0.0, ALU.mult, ALU.add)
 
         def regroup(g, da, number, copy):
             by_word = bank(number, [P, HALVES, 2, P], "by_word")
@@ -237,68 +243,79 @@ def tile_moe_hib_silu_kernel(
         def scatter_dx_on_vector(g, k, rows):
             nc.vector.tensor_copy(dx_window(g, k), rows[:])
 
+        gather_scales(0, G)
         words0, words1 = gather_words(0), gather_words(1)
-        low0, high0 = bank(0, [P, 2, C1], "low0"), bank(1, [P, 2, C1], "high0")
-        first_product(0, words0, [low0[:, 0], low0[:, 1], high0[:, 0], high0[:, 1]])
-        z_low0 = empty_gated(0, low0, 2, "z_low0")
-        z_high0 = empty_plain(high0, 2, "z_high0")
+        low0, high0, rest0 = bank(0, [P, 2, C1], "low0"), bank(1, [P, 3, C2], "high0"), bank(6, [P, C2], "rest0")
+        first_product(0, words0, [by_expert(low0[:, 0]), by_expert(low0[:, 1]), [high0[:, 0], rest0[:]], [high0[:, 1], high0[:, 2]]])
+        z_low0 = empty_gated(0, low0, keep([P, 2, C1], F32, "z_low0"))
+        z_part0 = empty_plain(high0[:, 0], "z_part0")
+        z_fourth0 = empty_plain(high0[:, 1:].rearrange("p e s -> p (e s)"), "z_fourth0")
         words2 = gather_words(2, "words0")
+        z_rest0 = keep([P, C2], F32, "z_rest0")
+        nc.vector.tensor_tensor(z_rest0[:], rest0[:], gate_rows[:, C2:C1], ALU.mult)
         low1, high1 = bank(2, [P, 2, C1], "low1"), bank(3, [P, 2, C1], "high1")
-        first_product(1, words1, [low1[:, 0], low1[:, 1], high1[:, 0], high1[:, 1]])
-        z_low1 = empty_gated(1, low1, 2, "z_low1")
-        low2, third2, fourth2 = bank(4, [P, 2, C1], "low2"), bank(5, [P, 1, C1], "third2"), bank(6, [P, 1, C1], "fourth2")
-        first_product(2, words2, [low2[:, 0], low2[:, 1], third2[:, 0], fourth2[:, 0]])
+        first_product(1, words1, [by_expert(low1[:, 0]), by_expert(low1[:, 1]), by_expert(high1[:, 0]), by_expert(high1[:, 1])])
+        z_low1 = empty_gated(1, low1, keep([P, 2, C1], F32, "z_low1"))
+        low2, high2 = bank(4, [P, 2, C1], "low2"), bank(5, [P, 2, C1], "high2")
+        first_product(2, words2, [by_expert(low2[:, 0]), by_expert(low2[:, 1]), by_expert(high2[:, 0]), by_expert(high2[:, 1])])
         scatter_on_scalar(0, 0, z_low0[:, 0])
-        z_high1 = empty_plain(high1, 2, "z_high1")
+        z_third1, z_fourth1 = empty_plain(high1[:, 0], "z_third1"), empty_plain(high1[:, 1], "z_fourth1")
         scatter_on_scalar(1, 0, z_low0[:, 1], "wet_w1")
-        z_fourth2 = empty_plain(fourth2, 1, "z_fourth2")
-        for c in range(2):
-            scatter_on_vector(2 + c, 0, z_high0[:, c])
-        z_low2 = empty_gated(2, low2, 2, "z_low2")
-        z_third2 = empty_gated(2, third2, 1, "z_third2")
+        z_third2, z_fourth2 = empty_plain(high2[:, 0], "z_third2"), empty_plain(high2[:, 1], "z_fourth2")
+        scatter_on_vector(2, 0, z_part0[:], None, 0, C2)
+        scatter_on_vector(3, 0, z_fourth0[:])
+        scatter_on_scalar(2, 0, z_rest0[:], None, C2, C1)
         scatter_on_scalar(0, 1, z_low1[:, 0], "wet_w2")
-        scatter_on_scalar(1, 1, z_low1[:, 1], "words0")
-        for c in range(2):
-            scatter_on_vector(2 + c, 1, z_high1[:, c])
-        scatter_on_vector(3, 2, z_fourth2[:, 0])
-
+        scatter_on_vector(2, 1, z_third1[:])
+        scatter_on_vector(3, 1, z_fourth1[:])
         a_turned0 = turn_a(0, [7, 0])
-        a_turned1 = turn_a(1, [1, 2])
         sigmoid0 = make_sigmoid(0, a_turned0, "z_low0")
-        z_turned0 = turn_z(0, [3, 4])
-        a_turned2 = turn_a(2, [5, 6])
-        weave_wgt(0, nc.vector.tensor_copy)
-        minus_d0 = make_minus_d(0, a_turned0, sigmoid0)
+        scatter_on_scalar(1, 1, z_low1[:, 1], "a_rows0")
+        scatter_on_vector(2, 2, z_third2[:], "z_fourth0")
+        scatter_on_vector(3, 2, z_fourth2[:])
+        late = keep([P, 2 * C1 + HALVES * H], F32, "late", "z_third2")
+        z_low2 = empty_gated(2, low2, late[:, 0 : 2 * C1].rearrange("p (c s) -> p c s", c=2))
+
+        a_turned1 = turn_a(1, [1, 2])
+        z_turned0 = turn_z(0, [3, 5])
+        a_turned2 = turn_a(2, [6, 4])
+        weave_wgt(0, "z_fourth2")
+        inner0 = make_inner(a_turned0, sigmoid0, late[:, 2 * C1 :].rearrange("p (b i) -> p b i", b=HALVES))
+        minus_d0 = [make_minus_d(0, half, inner0, sigmoid0) for half in range(HALVES)]
         da0 = make_da(0, z_turned0, minus_d0)
-        scatter_on_scalar(0, 2, z_low2[:, 0], "a_rows0")
-        sigmoid1 = make_sigmoid(1, a_turned1, "z_low1")
-        scatter_on_scalar(1, 2, z_low2[:, 1], "a_rows1")
+        sigmoid1 = make_sigmoid(1, a_turned1)
+        scatter_on_scalar(0, 2, z_low2[:, 0], "a_rows1")
         z_turned1 = turn_z(1, [7, 0])
-        weave_wgt(1, nc.vector.tensor_copy)
+        weave_wgt(1, "z_low0")
         regroup(0, da0, 3, nc.scalar.copy)
         sigmoid2 = make_sigmoid(2, a_turned2, "da0_1")
-        minus_d1 = make_minus_d(1, a_turned1, sigmoid1)
-        sums0 = dx_sums(0, [4, 1])
-        scatter_on_scalar(2, 2, z_third2[:, 0], "woven0")
+        inner1 = make_inner(a_turned1, sigmoid1, keep([P, HALVES, H], F32, "inner1"))
+        minus_d1 = [make_minus_d(1, half, inner1, sigmoid1) for half in range(HALVES)]
+        sums0 = dx_sums(0, [5, 1])
+        scatter_on_scalar(1, 2, z_low2[:, 1], "sigmoid1")
         da1 = make_da(1, z_turned1, minus_d1)
-        dx0 = [empty_dx(0, k, sums0, nc.scalar.copy) for k in range(K_TILES)]
+        weave_wgt(2, "z_fourth2")
         regroup(1, da1, 2, nc.scalar.copy)
-        weave_wgt(2, nc.scalar.copy, "da1_1")
-        z_turned2 = turn_z(2, [0, 7])
-        minus_d2 = make_minus_d(2, a_turned2, sigmoid2)
-        out_rows = [keep([P, T], F32, "out_rows0", "minus_d2_0"), keep([P, T], F32, "out_rows1", "wgt_planes2")]
-        scatter_dx_on_scalar(0, 1, dx0[1])
-        sums1 = dx_sums(1, [3, 4])
+        dx0 = keep([P, K_TILES, C1], F32, "dx0", "da1_1")
+        for k in reversed(range(K_TILES)):
+            nc.scalar.copy(dx0[:, k], sums0[k][:])
+        inner2 = make_inner(a_turned2, sigmoid2, keep([P, HALVES, H], F32, "inner2"))
+        z_turned2 = turn_z(2, [0, 6])
+        minus_d2 = [make_minus_d(2, 0, inner2, sigmoid2)]
+        sums1 = dx_sums(1, [3, 2])
+        minus_d2.append(make_minus_d(2, 1, inner2, sigmoid2))
+        out_rows = [keep([P, T], F32, "out_rows0", "minus_d2_0"), keep([P, T], F32, "out_rows1")]
+        scatter_dx_on_scalar(0, 1, dx0[:, 1])
         da2 = make_da(2, z_turned2, minus_d2)
-        regroup(2, da2, 2, nc.scalar.copy)
+        regroup(2, da2, 5, nc.scalar.copy)
         dx1 = keep([P, K_TILES, C1], F32, "dx1", "da2_1")
         for k in reversed(range(K_TILES)):
             nc.scalar.copy(dx1[:, k], sums1[k][:])
-        scatter_dx_on_vector(0, 0, dx0[0])
-        sums2 = dx_sums(2, [5, 6])
+        scatter_dx_on_vector(0, 0, dx0[:, 0])
+        sums2 = dx_sums(2, [7, 4])
         scatter_dx_on_scalar(1, 1, dx1[:, 1])
         scatter_dx_on_vector(1, 0, dx1[:, 0])
         scatter_dx_on_vector(2, 0, empty_dx(2, 0, sums2, nc.vector.tensor_copy))
         scatter_dx_on_scalar(2, 1, empty_dx(2, 1, sums2, nc.scalar.copy))
-        for k in range(K_TILES):
-            nc.sync.dma_start(out[k * P : (k + 1) * P, :], out_rows[k][:])
+        for k, queue in enumerate([nc.sync, nc.scalar]):
+            queue.dma_start(out[k * P : (k + 1) * P, :], out_rows[k][:])

@@ -59,12 +59,12 @@ def tile_moe_hib_silu_kernel(
         ident = keep([P, P], F32, "ident")
 
         nc.vector.memset(wet_s[:].rearrange("p e h -> p (e h)").bitcast(I32), 0)
-        nc.vector.memset(dy_w[:, T:], 0)
-        nc.vector.memset(dy_s[:, T:].bitcast(I32), 0)
         unit = held.tile([P, 2], F32, name="unit")
         nc.vector.memset(unit[:, 0:1], 64.0)
         nc.scalar.activation(unit[:, 1:2], unit[:, 0:1], ACT.Sigmoid)
         one = unit[:, 1:2]
+        nc.vector.memset(dy_w[:, T:], 0)
+        nc.vector.memset(dy_s[:, T:].bitcast(I32), 0)
         make_identity(nc, ident[:])
 
         def load_wet_words(g):
@@ -74,6 +74,10 @@ def tile_moe_hib_silu_kernel(
         def load_gate(lo, hi):
             nc.sync.dma_start(gate_rows[:, lo:hi], gate[:, lo:hi])
 
+        def load_a(g):
+            columns = a[:, g * C1 : (g + 1) * C1]
+            nc.sync.dma_start(a_rows[g][:], columns.rearrange("(c p) j -> p c j", p=P))
+
         nc.sync.dma_start(dst_list[:], dst)
         for q in range(P // QUAD):
             rows = dy_scales[0, SCALE_ROWS * q : SCALE_ROWS * (q + 1), :].bitcast(I32)
@@ -82,17 +86,18 @@ def tile_moe_hib_silu_kernel(
             queue.dma_start(dy_s[QUAD * q : QUAD * (q + 1), 0:T].bitcast(I32), repeated)
         nc.sync.dma_start(dy_w[:, 0:T], dy_words[0].rearrange("p t d -> p (t d)").bitcast(I32))
         load_wet_words(0)
-        load_gate(0, C1)
         for r in range(SCALE_ROWS):
             rows = wet_scales[:, 0, r : N // 32 : SCALE_ROWS, :].rearrange("e q h -> q e h")
             nc.sync.dma_start(wet_s[r:P:QUAD, :, :].bitcast(I32), rows.bitcast(I32))
+        load_gate(0, C1)
         nc.sync.dma_start(offs2_list[:], offs2)
         load_wet_words(1)
         load_gate(C1, T)
         load_wet_words(2)
+        load_a(0)
         for g in range(G):
-            columns = a[:, g * C1 : (g + 1) * C1]
-            nc.sync.dma_start(a_rows[g][:], columns.rearrange("(c p) j -> p c j", p=P))
+            if g + 1 < G:
+                load_a(g + 1)
             nc.sync.dma_start(wgt_planes[g][:], wgt[g].rearrange("(p t) k -> p t k", t=PACK))
         nc.sync.dma_start(offs_list[:], offs)
 
@@ -112,8 +117,8 @@ def tile_moe_hib_silu_kernel(
             nc.vector.tensor_copy(words[:], dy_w[:].bitcast(U32).indirect(entries(dst_list, g * C1, (g + 1) * C1)))
             return words
 
-        def first_product(g, words, places):
-            for c in range(I_TILES):
+        def first_product(g, words, places, tiles=range(I_TILES)):
+            for c in tiles:
                 for half in range(HALVES):
                     e = g * HALVES + half
                     nc.tensor.matmul_mx(
@@ -130,7 +135,7 @@ def tile_moe_hib_silu_kernel(
             return [columns[:, half * C2 : (half + 1) * C2] for half in range(HALVES)]
 
         def empty_gated(g, sums, rows):
-            gates = gate_rows[:, g * C1 : (g + 1) * C1].unsqueeze(1).to_broadcast([P, 2, C1])
+            gates = gate_rows[:, g * C1 : (g + 1) * C1].unsqueeze(1).to_broadcast(list(rows.shape))
             nc.vector.tensor_tensor(rows[:], sums[:], gates, ALU.mult)
             return rows
 
@@ -160,29 +165,37 @@ def tile_moe_hib_silu_kernel(
             return turned
 
         def turn_a(g, numbers):
-            return turn(numbers, "a_turned", lambda c, half: a_rows[g][:, c, half * P : (half + 1) * P])
+            turned = [bank(number, [P, H], "a_turned") for number in numbers]
+            for half in range(HALVES):
+                for c in range(I_TILES):
+                    block = a_rows[g][:, c, half * P : (half + 1) * P]
+                    nc.tensor.transpose(turned[half][:, c * P : (c + 1) * P], block, ident[:])
+            return turned
 
         def turn_z(g, numbers):
             return turn(
                 numbers, "z_turned", lambda c, half: z_back[c, g][:, g * C1 + half * P : g * C1 + (half + 1) * P]
             )
 
-        def make_sigmoid(g, a_turned, on=None):
-            sigmoid = keep([P, HALVES, H], F32, "sigmoid%d" % g, on)
+        def make_sigmoid(a_turned, sigmoid):
             for half in range(HALVES):
-                nc.scalar.activation(sigmoid[:, half], a_turned[half][:], ACT.Sigmoid, scale=one)
+                nc.scalar.activation(sigmoid[half], a_turned[half][:], ACT.Sigmoid, scale=one)
             return sigmoid
+
+        def halves(name, on=None):
+            tile = keep([P, HALVES, H], F32, name, on)
+            return [tile[:, half] for half in range(HALVES)]
 
         def make_inner(a_turned, sigmoid, inner):
             for half in range(HALVES):
                 nc.vector.scalar_tensor_tensor(
-                    inner[:, half], sigmoid[:, half], 1.0, a_turned[half][:], ALU.subtract, ALU.mult
+                    inner[:, half], sigmoid[half], 1.0, a_turned[half][:], ALU.subtract, ALU.mult
                 )
             return inner
 
-        def make_minus_d(g, half, inner, sigmoid):
-            minus_d = keep([P, H], F32, "minus_d%d_%d" % (g, half))
-            nc.vector.scalar_tensor_tensor(minus_d[:], inner[:, half], 1.0, sigmoid[:, half], ALU.subtract, ALU.mult)
+        def make_minus_d(g, half, inner, sigmoid, on=None):
+            minus_d = keep([P, H], F32, "minus_d%d_%d" % (g, half), on)
+            nc.vector.scalar_tensor_tensor(minus_d[:], inner[:, half], 1.0, sigmoid[half], ALU.subtract, ALU.mult)
             return minus_d
 
         def make_da(g, z_turned, minus_d):
@@ -193,25 +206,39 @@ def tile_moe_hib_silu_kernel(
 
         woven = {}
 
-        def weave_wgt(g, on):
-            woven.setdefault(g, keep([P, K + C1, PACK], BF16, "woven%d" % g, on))
+        def weave_wgt(g, place):
+            woven.setdefault(g, place)
             planes = wgt_planes[g][:].rearrange("p t k -> p k t")
             nc.gpsimd.tensor_scalar(woven[g][:, 0:K, :], planes, 1.0, 0.0, ALU.mult, ALU.add)
 
-        def regroup(g, da, number, copy):
+        def woven_tile(g, on):
+            return keep([P, K + C1, PACK], BF16, "woven%d" % g, on)[:]
+
+        def turn_words(da, by_word):
+            pairs = da[:].bitcast(F32)
+            for u in range(2):
+                nc.tensor.transpose(by_word[:, u, :], pairs[:, u : H // 2 : 2], ident[:])
+
+        def word_columns(g, lo, hi):
+            columns = woven[g][:, K + lo * P : K + hi * P, :].rearrange("p s t -> p (s t)").bitcast(F32)
+            return columns.rearrange("p (b s u) -> p b s u", b=hi - lo, u=2)
+
+        def regroup(g, da, number):
             by_word = bank(number, [P, HALVES, 2, P], "by_word")
             for half in range(HALVES):
-                pairs = da[half][:].bitcast(F32)
-                for u in range(2):
-                    nc.tensor.transpose(by_word[:, half, u, :], pairs[:, u : H // 2 : 2], ident[:])
-            columns = woven[g][:, K:, :].rearrange("p s t -> p (s t)").bitcast(F32)
-            copy(columns.rearrange("p (b s u) -> p b s u", b=HALVES, u=2), by_word[:].rearrange("p b u s -> p b s u"))
+                turn_words(da[half], by_word[:, half])
+            nc.scalar.copy(word_columns(g, 0, HALVES), by_word[:].rearrange("p b u s -> p b s u"))
+
+        def regroup_block(g, half, da, number):
+            by_word = bank(number, [P, 1, 2, P], "by_word")
+            turn_words(da[half], by_word[:, 0])
+            nc.scalar.copy(word_columns(g, half, half + 1), by_word[:].rearrange("p b u s -> p b s u"))
 
         def second_product(g, places, on=None):
             codes = keep([P, K + C1], U32, "codes%d" % g, on)
             scales = keep([P, K + C1], U8, "scales%d" % g)
             nc.vector.quantize_mx(
-                out=codes[:].bitcast(FP8X4), scales=scales[:], in_=woven[g][:].rearrange("p c t -> p (c t)")
+                out=codes[:].bitcast(FP8X4), scales=scales[:], in_=woven[g].rearrange("p c t -> p (c t)")
             )
             for k in range(K_TILES):
                 nc.tensor.matmul_mx(
@@ -244,17 +271,19 @@ def tile_moe_hib_silu_kernel(
             nc.vector.tensor_copy(dx_window(g, k), rows[:])
 
         gather_scales(0, G)
-        words0, words1 = gather_words(0), gather_words(1)
-        low0, high0, rest0 = bank(0, [P, 2, C1], "low0"), bank(1, [P, 3, C2], "high0"), bank(6, [P, C2], "rest0")
-        first_product(0, words0, [by_expert(low0[:, 0]), by_expert(low0[:, 1]), [high0[:, 0], rest0[:]], [high0[:, 1], high0[:, 2]]])
-        z_low0 = empty_gated(0, low0, keep([P, 2, C1], F32, "z_low0"))
-        z_part0 = empty_plain(high0[:, 0], "z_part0")
+        words0, words1, words2 = [gather_words(g) for g in range(G)]
+        first0, second0, high0 = bank(0, [P, C1], "first0"), bank(6, [P, 3, C2], "second0"), bank(1, [P, 3, C2], "high0")
+        places = [by_expert(first0), [second0[:, 0], second0[:, 1]], [high0[:, 0], second0[:, 2]], [high0[:, 1], high0[:, 2]]]
+        first_product(0, words0, places, [3, 0, 2, 1])
         z_fourth0 = empty_plain(high0[:, 1:].rearrange("p e s -> p (e s)"), "z_fourth0")
-        words2 = gather_words(2, "words0")
-        z_rest0 = keep([P, C2], F32, "z_rest0")
-        nc.vector.tensor_tensor(z_rest0[:], rest0[:], gate_rows[:, C2:C1], ALU.mult)
+        z_part0 = empty_plain(high0[:, 0], "z_part0")
+        z_low0 = keep([P, 2, C1], F32, "z_low0")
+        nc.vector.tensor_tensor(z_low0[:, 0], first0[:], gate_rows[:, 0:C1], ALU.mult)
+        nc.vector.tensor_tensor(z_low0[:, 1], second0[:, 0:2].rearrange("p e s -> p (e s)"), gate_rows[:, 0:C1], ALU.mult)
         low1, high1 = bank(2, [P, 2, C1], "low1"), bank(3, [P, 2, C1], "high1")
         first_product(1, words1, [by_expert(low1[:, 0]), by_expert(low1[:, 1]), by_expert(high1[:, 0]), by_expert(high1[:, 1])])
+        z_rest0 = keep([P, C2], F32, "z_rest0", "words1")
+        nc.vector.tensor_tensor(z_rest0[:], second0[:, 2], gate_rows[:, C2:C1], ALU.mult)
         z_low1 = empty_gated(1, low1, keep([P, 2, C1], F32, "z_low1"))
         low2, high2 = bank(4, [P, 2, C1], "low2"), bank(5, [P, 2, C1], "high2")
         first_product(2, words2, [by_expert(low2[:, 0]), by_expert(low2[:, 1]), by_expert(high2[:, 0]), by_expert(high2[:, 1])])
@@ -269,7 +298,7 @@ def tile_moe_hib_silu_kernel(
         scatter_on_vector(2, 1, z_third1[:])
         scatter_on_vector(3, 1, z_fourth1[:])
         a_turned0 = turn_a(0, [7, 0])
-        sigmoid0 = make_sigmoid(0, a_turned0, "z_low0")
+        sigmoid0 = make_sigmoid(a_turned0, [keep([P, H], F32, "sigmoid0_0", "z_low0")[:], keep([P, H], F32, "sigmoid0_1")[:]])
         scatter_on_scalar(1, 1, z_low1[:, 1], "a_rows0")
         scatter_on_vector(2, 2, z_third2[:], "z_fourth0")
         scatter_on_vector(3, 2, z_fourth2[:])
@@ -279,23 +308,23 @@ def tile_moe_hib_silu_kernel(
         a_turned1 = turn_a(1, [1, 2])
         z_turned0 = turn_z(0, [3, 5])
         a_turned2 = turn_a(2, [6, 4])
-        weave_wgt(0, "z_fourth2")
+        weave_wgt(0, woven_tile(0, "z_fourth2"))
         inner0 = make_inner(a_turned0, sigmoid0, late[:, 2 * C1 :].rearrange("p (b i) -> p b i", b=HALVES))
         minus_d0 = [make_minus_d(0, half, inner0, sigmoid0) for half in range(HALVES)]
         da0 = make_da(0, z_turned0, minus_d0)
-        sigmoid1 = make_sigmoid(1, a_turned1)
+        sigmoid1 = make_sigmoid(a_turned1, halves("sigmoid1"))
         scatter_on_scalar(0, 2, z_low2[:, 0], "a_rows1")
         z_turned1 = turn_z(1, [7, 0])
-        weave_wgt(1, "z_low0")
-        regroup(0, da0, 3, nc.scalar.copy)
-        sigmoid2 = make_sigmoid(2, a_turned2, "da0_1")
+        weave_wgt(1, woven_tile(1, "z_low0"))
+        regroup(0, da0, 3)
+        sigmoid2 = make_sigmoid(a_turned2, halves("sigmoid2", "da0_1"))
         inner1 = make_inner(a_turned1, sigmoid1, keep([P, HALVES, H], F32, "inner1"))
         minus_d1 = [make_minus_d(1, half, inner1, sigmoid1) for half in range(HALVES)]
         sums0 = dx_sums(0, [5, 1])
         scatter_on_scalar(1, 2, z_low2[:, 1], "sigmoid1")
         da1 = make_da(1, z_turned1, minus_d1)
-        weave_wgt(2, "z_fourth2")
-        regroup(1, da1, 2, nc.scalar.copy)
+        weave_wgt(2, woven_tile(2, "z_fourth2"))
+        regroup(1, da1, 2)
         dx0 = keep([P, K_TILES, C1], F32, "dx0", "da1_1")
         for k in reversed(range(K_TILES)):
             nc.scalar.copy(dx0[:, k], sums0[k][:])
@@ -307,15 +336,16 @@ def tile_moe_hib_silu_kernel(
         out_rows = [keep([P, T], F32, "out_rows0", "minus_d2_0"), keep([P, T], F32, "out_rows1")]
         scatter_dx_on_scalar(0, 1, dx0[:, 1])
         da2 = make_da(2, z_turned2, minus_d2)
-        regroup(2, da2, 5, nc.scalar.copy)
-        dx1 = keep([P, K_TILES, C1], F32, "dx1", "da2_1")
-        for k in reversed(range(K_TILES)):
-            nc.scalar.copy(dx1[:, k], sums1[k][:])
+        regroup_block(2, 0, da2, 5)
+        dx1_high = empty_dx(1, 1, sums1, nc.scalar.copy, "da2_0")
+        regroup_block(2, 1, da2, 1)
+        dx1_low = empty_dx(1, 0, sums1, nc.scalar.copy, "da2_1")
         scatter_dx_on_vector(0, 0, dx0[:, 0])
         sums2 = dx_sums(2, [7, 4])
-        scatter_dx_on_scalar(1, 1, dx1[:, 1])
-        scatter_dx_on_vector(1, 0, dx1[:, 0])
-        scatter_dx_on_vector(2, 0, empty_dx(2, 0, sums2, nc.vector.tensor_copy))
-        scatter_dx_on_scalar(2, 1, empty_dx(2, 1, sums2, nc.scalar.copy))
+        scatter_dx_on_scalar(1, 1, dx1_high)
+        scatter_dx_on_vector(1, 0, dx1_low)
+        dx2 = [empty_dx(2, k, sums2, nc.scalar.copy) for k in range(K_TILES)]
+        scatter_dx_on_vector(2, 0, dx2[0])
+        scatter_dx_on_scalar(2, 1, dx2[1])
         for k, queue in enumerate([nc.sync, nc.scalar]):
             queue.dma_start(out[k * P : (k + 1) * P, :], out_rows[k][:])

@@ -38,6 +38,7 @@ def tile_moe_hib_silu_kernel(
     nc = tc.nc
     with ExitStack() as ctx:
         held = ctx.enter_context(tc.tile_pool(name="held", bufs=1))
+        placed = ctx.enter_context(tc.tile_pool(name="placed", bufs=1))
         psum = ctx.enter_context(tc.psum_pool(name="psum", bufs=1))
 
         def keep(shape, dtype, name, on=None):
@@ -54,7 +55,8 @@ def tile_moe_hib_silu_kernel(
         wet_w = [keep([P, HALVES, 2 * H], U8, "wet_w%d" % g) for g in range(G)]
         wet_s = keep([P, E, H], U8, "wet_s")
         gate_rows = keep([P, T], F32, "gate_rows")
-        a_rows = [keep([P, I_TILES, C1], F32, "a_rows%d" % g) for g in range(G)]
+        a_rows = [placed.tile([P, I_TILES, C1], F32, name="a_rows0", offset=4 * C1)]
+        a_rows.extend(keep([P, I_TILES, C1], F32, "a_rows%d" % g) for g in range(1, G))
         wgt_planes = [keep([P, PACK, K], F32, "wgt_planes%d" % g) for g in range(G)]
         ident = keep([P, P], F32, "ident")
 
@@ -94,10 +96,9 @@ def tile_moe_hib_silu_kernel(
         load_wet_words(1)
         load_gate(C1, T)
         load_wet_words(2)
-        load_a(0)
         for g in range(G):
-            if g + 1 < G:
-                load_a(g + 1)
+            load_a(g)
+        for g in range(G):
             nc.sync.dma_start(wgt_planes[g][:], wgt[g].rearrange("(p t) k -> p t k", t=PACK))
         nc.sync.dma_start(offs_list[:], offs)
 
@@ -147,6 +148,8 @@ def tile_moe_hib_silu_kernel(
         z_back = {}
 
         def z_window(c, g, lo, hi, on):
+            if isinstance(on, int):
+                z_back.setdefault((c, g), placed.tile([P, T], F32, name="z_back%d_%d" % (c, g), offset=on))
             if (c, g) not in z_back:
                 z_back.setdefault((c, g), keep([P, T], F32, "z_back%d_%d" % (c, g), on))
             return z_back[c, g][:].indirect(entries(offs2_list, g * C1 + lo, g * C1 + hi))
@@ -272,73 +275,69 @@ def tile_moe_hib_silu_kernel(
 
         gather_scales(0, G)
         words0, words1, words2 = [gather_words(g) for g in range(G)]
-        first0, second0, high0 = bank(0, [P, C1], "first0"), bank(6, [P, 3, C2], "second0"), bank(1, [P, 3, C2], "high0")
-        places = [by_expert(first0), [second0[:, 0], second0[:, 1]], [high0[:, 0], second0[:, 2]], [high0[:, 1], high0[:, 2]]]
-        first_product(0, words0, places, [3, 0, 2, 1])
-        z_fourth0 = empty_plain(high0[:, 1:].rearrange("p e s -> p (e s)"), "z_fourth0")
-        z_part0 = empty_plain(high0[:, 0], "z_part0")
+        sums = [bank(number, [P, 1, C1], "sums") for number in (0, 6, 1, 7)]
+        first_product(0, words0, [by_expert(sums[c][:, 0]) for c in range(I_TILES)], [2, 0, 3, 1])
         z_low0 = keep([P, 2, C1], F32, "z_low0")
-        nc.vector.tensor_tensor(z_low0[:, 0], first0[:], gate_rows[:, 0:C1], ALU.mult)
-        nc.vector.tensor_tensor(z_low0[:, 1], second0[:, 0:2].rearrange("p e s -> p (e s)"), gate_rows[:, 0:C1], ALU.mult)
-        low1, high1 = bank(2, [P, 2, C1], "low1"), bank(3, [P, 2, C1], "high1")
-        first_product(1, words1, [by_expert(low1[:, 0]), by_expert(low1[:, 1]), by_expert(high1[:, 0]), by_expert(high1[:, 1])])
-        z_rest0 = keep([P, C2], F32, "z_rest0", "words1")
-        nc.vector.tensor_tensor(z_rest0[:], second0[:, 2], gate_rows[:, C2:C1], ALU.mult)
-        z_low1 = empty_gated(1, low1, keep([P, 2, C1], F32, "z_low1"))
+        for c in range(2):
+            empty_gated(0, sums[c], z_low0[:, c : c + 1])
+        z_third0, z_fourth0 = empty_plain(sums[2][:, 0], "z_third0"), empty_plain(sums[3][:, 0], "z_fourth0")
+        low1, third1, fourth1 = bank(2, [P, 2, C1], "low1"), bank(3, [P, 1, C1], "third1"), bank(1, [P, C1], "fourth1")
+        first_product(1, words1, [by_expert(low1[:, 0]), by_expert(low1[:, 1]), by_expert(third1[:, 0]), by_expert(fourth1)], [3, 2, 0, 1])
         low2, high2 = bank(4, [P, 2, C1], "low2"), bank(5, [P, 2, C1], "high2")
-        first_product(2, words2, [by_expert(low2[:, 0]), by_expert(low2[:, 1]), by_expert(high2[:, 0]), by_expert(high2[:, 1])])
+        first_product(2, words2, [by_expert(low2[:, 0]), by_expert(low2[:, 1]), by_expert(high2[:, 0]), by_expert(high2[:, 1])], [2, 3, 0, 1])
         scatter_on_scalar(0, 0, z_low0[:, 0])
-        z_third1, z_fourth1 = empty_plain(high1[:, 0], "z_third1"), empty_plain(high1[:, 1], "z_fourth1")
+        z_fourth1 = empty_plain(fourth1[:], "z_fourth1")
         scatter_on_scalar(1, 0, z_low0[:, 1], "wet_w1")
         z_third2, z_fourth2 = empty_plain(high2[:, 0], "z_third2"), empty_plain(high2[:, 1], "z_fourth2")
-        scatter_on_vector(2, 0, z_part0[:], None, 0, C2)
+        scatter_on_vector(2, 0, z_third0[:])
         scatter_on_vector(3, 0, z_fourth0[:])
-        scatter_on_scalar(2, 0, z_rest0[:], None, C2, C1)
-        scatter_on_scalar(0, 1, z_low1[:, 0], "wet_w2")
-        scatter_on_vector(2, 1, z_third1[:])
+        z_gated1 = keep([P, 3, C1], F32, "z_gated1", "z_third0")
+        z_third1 = empty_gated(1, third1, z_gated1[:, 2:3])
+        z_low1 = empty_gated(1, low1, z_gated1[:, 0:2])
+        scatter_on_scalar(2, 1, z_third1[:, 0], "wet_w2")
         scatter_on_vector(3, 1, z_fourth1[:])
         a_turned0 = turn_a(0, [7, 0])
         sigmoid0 = make_sigmoid(a_turned0, [keep([P, H], F32, "sigmoid0_0", "z_low0")[:], keep([P, H], F32, "sigmoid0_1")[:]])
-        scatter_on_scalar(1, 1, z_low1[:, 1], "a_rows0")
+        for c in range(2):
+            scatter_on_scalar(c, 1, z_low1[:, c], c * 4 * T)
         scatter_on_vector(2, 2, z_third2[:], "z_fourth0")
         scatter_on_vector(3, 2, z_fourth2[:])
         late = keep([P, 2 * C1 + HALVES * H], F32, "late", "z_third2")
         z_low2 = empty_gated(2, low2, late[:, 0 : 2 * C1].rearrange("p (c s) -> p c s", c=2))
 
-        a_turned1 = turn_a(1, [1, 2])
+        a_turned1 = turn_a(1, [6, 1])
         z_turned0 = turn_z(0, [3, 5])
-        a_turned2 = turn_a(2, [6, 4])
+        a_turned2 = turn_a(2, [2, 4])
         weave_wgt(0, woven_tile(0, "z_fourth2"))
         inner0 = make_inner(a_turned0, sigmoid0, late[:, 2 * C1 :].rearrange("p (b i) -> p b i", b=HALVES))
         minus_d0 = [make_minus_d(0, half, inner0, sigmoid0) for half in range(HALVES)]
         da0 = make_da(0, z_turned0, minus_d0)
         sigmoid1 = make_sigmoid(a_turned1, halves("sigmoid1"))
-        scatter_on_scalar(0, 2, z_low2[:, 0], "a_rows1")
+        sigmoid2 = make_sigmoid(a_turned2, halves("sigmoid2"))
         z_turned1 = turn_z(1, [7, 0])
         weave_wgt(1, woven_tile(1, "z_low0"))
         regroup(0, da0, 3)
-        sigmoid2 = make_sigmoid(a_turned2, halves("sigmoid2", "da0_1"))
-        inner1 = make_inner(a_turned1, sigmoid1, keep([P, HALVES, H], F32, "inner1"))
+        scatter_on_scalar(0, 2, z_low2[:, 0], "da0_1")
+        inner1 = make_inner(a_turned1, sigmoid1, keep([P, HALVES, H], F32, "inner1", "minus_d0_0"))
         minus_d1 = [make_minus_d(1, half, inner1, sigmoid1) for half in range(HALVES)]
-        sums0 = dx_sums(0, [5, 1])
+        sums0 = dx_sums(0, [5, 6])
         scatter_on_scalar(1, 2, z_low2[:, 1], "sigmoid1")
         da1 = make_da(1, z_turned1, minus_d1)
         weave_wgt(2, woven_tile(2, "z_fourth2"))
-        regroup(1, da1, 2)
+        regroup(1, da1, 1)
         dx0 = keep([P, K_TILES, C1], F32, "dx0", "da1_1")
         for k in reversed(range(K_TILES)):
             nc.scalar.copy(dx0[:, k], sums0[k][:])
-        inner2 = make_inner(a_turned2, sigmoid2, keep([P, HALVES, H], F32, "inner2"))
-        z_turned2 = turn_z(2, [0, 6])
-        minus_d2 = [make_minus_d(2, 0, inner2, sigmoid2)]
-        sums1 = dx_sums(1, [3, 2])
-        minus_d2.append(make_minus_d(2, 1, inner2, sigmoid2))
+        inner2 = make_inner(a_turned2, sigmoid2, keep([P, HALVES, H], F32, "inner2", "minus_d1_0"))
+        z_turned2 = turn_z(2, [0, 2])
+        minus_d2 = [make_minus_d(2, half, inner2, sigmoid2) for half in range(HALVES)]
+        sums1 = dx_sums(1, [3, 1])
         out_rows = [keep([P, T], F32, "out_rows0", "minus_d2_0"), keep([P, T], F32, "out_rows1")]
         scatter_dx_on_scalar(0, 1, dx0[:, 1])
         da2 = make_da(2, z_turned2, minus_d2)
         regroup_block(2, 0, da2, 5)
         dx1_high = empty_dx(1, 1, sums1, nc.scalar.copy, "da2_0")
-        regroup_block(2, 1, da2, 1)
+        regroup_block(2, 1, da2, 6)
         dx1_low = empty_dx(1, 0, sums1, nc.scalar.copy, "da2_1")
         scatter_dx_on_vector(0, 0, dx0[:, 0])
         sums2 = dx_sums(2, [7, 4])

@@ -19,6 +19,8 @@ HALVES = C1 // P
 
 
 WINDOW = 1024
+LATE_AT = 8 * T
+WOVEN_AT = LATE_AT + 4 * (2 * C1 + HALVES * H)
 
 F32 = mybir.dt.float32
 BF16 = mybir.dt.bfloat16
@@ -140,8 +142,11 @@ def tile_moe_hib_silu_kernel(
             nc.vector.tensor_tensor(rows[:], sums[:], gates, ALU.mult)
             return rows
 
-        def empty_plain(sums, name):
-            rows = keep(list(sums.shape), F32, name)
+        def empty_plain(sums, name, offset=None):
+            if offset is None:
+                rows = keep(list(sums.shape), F32, name)
+            else:
+                rows = placed.tile(list(sums.shape), F32, name=name, offset=offset)
             nc.scalar.copy(rows[:], sums)
             return rows
 
@@ -288,7 +293,7 @@ def tile_moe_hib_silu_kernel(
         scatter_on_scalar(0, 0, z_low0[:, 0])
         z_fourth1 = empty_plain(fourth1[:], "z_fourth1")
         scatter_on_scalar(1, 0, z_low0[:, 1], "wet_w1")
-        z_third2, z_fourth2 = empty_plain(high2[:, 0], "z_third2"), empty_plain(high2[:, 1], "z_fourth2")
+        z_third2, z_fourth2 = empty_plain(high2[:, 0], "z_third2", WOVEN_AT - 2 * C1), empty_plain(high2[:, 1], "z_fourth2")
         scatter_on_vector(2, 0, z_third0[:])
         scatter_on_vector(3, 0, z_fourth0[:])
         z_gated1 = keep([P, 3, C1], F32, "z_gated1", "z_third0")
@@ -300,15 +305,16 @@ def tile_moe_hib_silu_kernel(
         sigmoid0 = make_sigmoid(a_turned0, [keep([P, H], F32, "sigmoid0_0", "z_low0")[:], keep([P, H], F32, "sigmoid0_1")[:]])
         for c in range(2):
             scatter_on_scalar(c, 1, z_low1[:, c], c * 4 * T)
-        scatter_on_vector(2, 2, z_third2[:], "z_fourth0")
-        scatter_on_vector(3, 2, z_fourth2[:])
-        late = keep([P, 2 * C1 + HALVES * H], F32, "late", "z_third2")
+        for lo in (0, C2):
+            scatter_on_vector(2, 2, z_third2[:, lo : lo + C2], "z_fourth0", lo, lo + C2)
+            scatter_on_vector(3, 2, z_fourth2[:, lo : lo + C2], None, lo, lo + C2)
+        late = placed.tile([P, 2 * C1 + HALVES * H], F32, name="late", offset=LATE_AT)
         z_low2 = empty_gated(2, low2, late[:, 0 : 2 * C1].rearrange("p (c s) -> p c s", c=2))
 
         a_turned1 = turn_a(1, [6, 1])
         z_turned0 = turn_z(0, [3, 5])
         a_turned2 = turn_a(2, [2, 4])
-        weave_wgt(0, woven_tile(0, "z_fourth2"))
+        weave_wgt(0, placed.tile([P, K + C1, PACK], BF16, name="woven0", offset=WOVEN_AT)[:])
         inner0 = make_inner(a_turned0, sigmoid0, late[:, 2 * C1 :].rearrange("p (b i) -> p b i", b=HALVES))
         minus_d0 = [make_minus_d(0, half, inner0, sigmoid0) for half in range(HALVES)]
         da0 = make_da(0, z_turned0, minus_d0)
@@ -323,7 +329,7 @@ def tile_moe_hib_silu_kernel(
         sums0 = dx_sums(0, [5, 6])
         scatter_on_scalar(1, 2, z_low2[:, 1], "sigmoid1")
         da1 = make_da(1, z_turned1, minus_d1)
-        weave_wgt(2, woven_tile(2, "z_fourth2"))
+        weave_wgt(2, placed.tile([P, K + C1, PACK], BF16, name="woven2", offset=WOVEN_AT)[:])
         regroup(1, da1, 1)
         dx0 = keep([P, K_TILES, C1], F32, "dx0", "da1_1")
         for k in reversed(range(K_TILES)):

@@ -20,7 +20,7 @@ HALVES = C1 // P
 
 WINDOW = 1024
 LATE_AT = 8 * T
-WOVEN_AT = LATE_AT + 4 * (2 * C1 + HALVES * H)
+WOVEN_AT = LATE_AT + 4 * (3 * C1 + HALVES * H)
 
 F32 = mybir.dt.float32
 BF16 = mybir.dt.bfloat16
@@ -283,70 +283,70 @@ def tile_moe_hib_silu_kernel(
         sums = [bank(number, [P, 1, C1], "sums") for number in (0, 6, 1, 7)]
         first_product(0, words0, [by_expert(sums[c][:, 0]) for c in range(I_TILES)], [2, 0, 3, 1])
         z_low0 = keep([P, 2, C1], F32, "z_low0")
-        for c in range(2):
-            empty_gated(0, sums[c], z_low0[:, c : c + 1])
+        empty_gated(0, sums[0], z_low0[:, 0:1])
         z_third0, z_fourth0 = empty_plain(sums[2][:, 0], "z_third0"), empty_plain(sums[3][:, 0], "z_fourth0")
+        scatter_on_vector(2, 0, z_third0[:])
+        empty_gated(0, sums[1], z_low0[:, 1:2])
         low1, third1, fourth1 = bank(2, [P, 2, C1], "low1"), bank(3, [P, 1, C1], "third1"), bank(1, [P, C1], "fourth1")
-        first_product(1, words1, [by_expert(low1[:, 0]), by_expert(low1[:, 1]), by_expert(third1[:, 0]), by_expert(fourth1)], [3, 2, 0, 1])
+        first_product(1, words1, [by_expert(low1[:, 0]), by_expert(low1[:, 1]), by_expert(third1[:, 0]), by_expert(fourth1)], [3, 0, 1, 2])
         low2, high2 = bank(4, [P, 2, C1], "low2"), bank(5, [P, 2, C1], "high2")
         first_product(2, words2, [by_expert(low2[:, 0]), by_expert(low2[:, 1]), by_expert(high2[:, 0]), by_expert(high2[:, 1])], [2, 3, 0, 1])
         scatter_on_scalar(0, 0, z_low0[:, 0])
         z_fourth1 = empty_plain(fourth1[:], "z_fourth1")
         scatter_on_scalar(1, 0, z_low0[:, 1], "wet_w1")
         z_third2, z_fourth2 = empty_plain(high2[:, 0], "z_third2", WOVEN_AT - 2 * C1), empty_plain(high2[:, 1], "z_fourth2")
-        scatter_on_vector(2, 0, z_third0[:])
         scatter_on_vector(3, 0, z_fourth0[:])
-        z_gated1 = keep([P, 3, C1], F32, "z_gated1", "z_third0")
-        z_third1 = empty_gated(1, third1, z_gated1[:, 2:3])
-        z_low1 = empty_gated(1, low1, z_gated1[:, 0:2])
-        scatter_on_scalar(2, 1, z_third1[:, 0], "wet_w2")
+        z_low1 = empty_gated(1, low1, keep([P, 2, C1], F32, "z_low1", "z_third0"))
+        scatter_on_scalar(0, 1, z_low1[:, 0], "wet_w2")
         scatter_on_vector(3, 1, z_fourth1[:])
         a_turned0 = turn_a(0, [7, 0])
         sigmoid0 = make_sigmoid(a_turned0, [keep([P, H], F32, "sigmoid0_0", "z_low0")[:], keep([P, H], F32, "sigmoid0_1")[:]])
-        for c in range(2):
-            scatter_on_scalar(c, 1, z_low1[:, c], c * 4 * T)
+        scatter_on_scalar(1, 1, z_low1[:, 1], 0)
         for lo in (0, C2):
             scatter_on_vector(2, 2, z_third2[:, lo : lo + C2], "z_fourth0", lo, lo + C2)
             scatter_on_vector(3, 2, z_fourth2[:, lo : lo + C2], None, lo, lo + C2)
-        late = placed.tile([P, 2 * C1 + HALVES * H], F32, name="late", offset=LATE_AT)
-        z_low2 = empty_gated(2, low2, late[:, 0 : 2 * C1].rearrange("p (c s) -> p c s", c=2))
+        late = placed.tile([P, 3 * C1 + HALVES * H], F32, name="late", offset=LATE_AT)
+        late_rows = late[:, 0 : 3 * C1].rearrange("p (c s) -> p c s", s=C1)
+        z_third1 = empty_gated(1, third1, late_rows[:, 0:1])
+        z_low2 = empty_gated(2, low2, late_rows[:, 1:3])
+        scatter_on_scalar(2, 1, z_third1[:, 0], 4 * T)
 
         a_turned1 = turn_a(1, [6, 1])
-        z_turned0 = turn_z(0, [3, 5])
-        a_turned2 = turn_a(2, [2, 4])
+        z_turned0 = turn_z(0, [2, 5])
+        a_turned2 = turn_a(2, [3, 4])
         weave_wgt(0, placed.tile([P, K + C1, PACK], BF16, name="woven0", offset=WOVEN_AT)[:])
-        inner0 = make_inner(a_turned0, sigmoid0, late[:, 2 * C1 :].rearrange("p (b i) -> p b i", b=HALVES))
+        inner0 = make_inner(a_turned0, sigmoid0, late[:, 3 * C1 :].rearrange("p (b i) -> p b i", b=HALVES))
         minus_d0 = [make_minus_d(0, half, inner0, sigmoid0) for half in range(HALVES)]
         da0 = make_da(0, z_turned0, minus_d0)
         sigmoid1 = make_sigmoid(a_turned1, halves("sigmoid1"))
         sigmoid2 = make_sigmoid(a_turned2, halves("sigmoid2"))
-        z_turned1 = turn_z(1, [7, 0])
         weave_wgt(1, woven_tile(1, "z_low0"))
-        regroup(0, da0, 3)
+        regroup(0, da0, 2)
         scatter_on_scalar(0, 2, z_low2[:, 0], "da0_1")
         inner1 = make_inner(a_turned1, sigmoid1, keep([P, HALVES, H], F32, "inner1", "minus_d0_0"))
+        z_turned1 = turn_z(1, [6, 1])
         minus_d1 = [make_minus_d(1, half, inner1, sigmoid1) for half in range(HALVES)]
-        sums0 = dx_sums(0, [5, 6])
+        sums0 = dx_sums(0, [5, 7])
         scatter_on_scalar(1, 2, z_low2[:, 1], "sigmoid1")
         da1 = make_da(1, z_turned1, minus_d1)
         weave_wgt(2, placed.tile([P, K + C1, PACK], BF16, name="woven2", offset=WOVEN_AT)[:])
-        regroup(1, da1, 1)
+        regroup(1, da1, 0)
         dx0 = keep([P, K_TILES, C1], F32, "dx0", "da1_1")
         for k in reversed(range(K_TILES)):
             nc.scalar.copy(dx0[:, k], sums0[k][:])
         inner2 = make_inner(a_turned2, sigmoid2, keep([P, HALVES, H], F32, "inner2", "minus_d1_0"))
-        z_turned2 = turn_z(2, [0, 2])
+        z_turned2 = turn_z(2, [1, 3])
         minus_d2 = [make_minus_d(2, half, inner2, sigmoid2) for half in range(HALVES)]
-        sums1 = dx_sums(1, [3, 1])
+        sums1 = dx_sums(1, [2, 0])
         out_rows = [keep([P, T], F32, "out_rows0", "minus_d2_0"), keep([P, T], F32, "out_rows1")]
         scatter_dx_on_scalar(0, 1, dx0[:, 1])
         da2 = make_da(2, z_turned2, minus_d2)
         regroup_block(2, 0, da2, 5)
         dx1_high = empty_dx(1, 1, sums1, nc.scalar.copy, "da2_0")
-        regroup_block(2, 1, da2, 6)
+        regroup_block(2, 1, da2, 7)
         dx1_low = empty_dx(1, 0, sums1, nc.scalar.copy, "da2_1")
         scatter_dx_on_vector(0, 0, dx0[:, 0])
-        sums2 = dx_sums(2, [7, 4])
+        sums2 = dx_sums(2, [6, 4])
         scatter_dx_on_scalar(1, 1, dx1_high)
         scatter_dx_on_vector(1, 0, dx1_low)
         dx2 = [empty_dx(2, k, sums2, nc.scalar.copy) for k in range(K_TILES)]

@@ -19,6 +19,7 @@ HALVES = C1 // P
 
 
 WINDOW = 1024
+SHARE = 64
 LATE_AT = 8 * T
 WOVEN_AT = LATE_AT + 4 * (3 * C1 + HALVES * H)
 
@@ -284,10 +285,11 @@ def tile_moe_hib_silu_kernel(
         first_product(0, words0, [by_expert(sums[c][:, 0]) for c in range(I_TILES)], [2, 0, 3, 1])
         z_low0 = keep([P, 2, C1], F32, "z_low0")
         empty_gated(0, sums[0], z_low0[:, 0:1])
-        z_third0, z_fourth0 = empty_plain(sums[2][:, 0], "z_third0"), empty_plain(sums[3][:, 0], "z_fourth0")
-        scatter_on_vector(2, 0, z_third0[:])
+        z_third0, z_fourth0 = empty_plain(sums[2][:, 0, 0 : C1 - SHARE], "z_third0"), empty_plain(sums[3][:, 0], "z_fourth0")
+        z_back.setdefault((2, 0), keep([P, 2 * C1], F32, "z_back2_0"))
+        scatter_on_vector(2, 0, z_third0[:], None, 0, C1 - SHARE)
         empty_gated(0, sums[1], z_low0[:, 1:2])
-        low1, third1, fourth1 = bank(2, [P, 2, C1], "low1"), bank(3, [P, 1, C1], "third1"), bank(1, [P, C1], "fourth1")
+        low1, third1, fourth1 = bank(2, [P, 2, C1], "low1"), bank(3, [P, 1, C1], "third1"), bank(7, [P, C1], "fourth1")
         first_product(1, words1, [by_expert(low1[:, 0]), by_expert(low1[:, 1]), by_expert(third1[:, 0]), by_expert(fourth1)], [3, 0, 1, 2])
         low2, high2 = bank(4, [P, 2, C1], "low2"), bank(5, [P, 2, C1], "high2")
         first_product(2, words2, [by_expert(low2[:, 0]), by_expert(low2[:, 1]), by_expert(high2[:, 0]), by_expert(high2[:, 1])], [2, 3, 0, 1])
@@ -297,9 +299,12 @@ def tile_moe_hib_silu_kernel(
         z_third2, z_fourth2 = empty_plain(high2[:, 0], "z_third2", WOVEN_AT - 2 * C1), empty_plain(high2[:, 1], "z_fourth2")
         scatter_on_vector(3, 0, z_fourth0[:])
         z_low1 = empty_gated(1, low1, keep([P, 2, C1], F32, "z_low1", "z_third0"))
+        z_rest0 = keep([P, SHARE], F32, "z_rest0", "words2")
+        nc.vector.tensor_tensor(z_rest0[:], sums[2][:, 0, C1 - SHARE :], gate_rows[:, C1 - SHARE : C1], ALU.mult)
         scatter_on_scalar(0, 1, z_low1[:, 0], "wet_w2")
+        scatter_on_scalar(2, 0, z_rest0[:], None, C1 - SHARE, C1)
         scatter_on_vector(3, 1, z_fourth1[:])
-        a_turned0 = turn_a(0, [7, 0])
+        a_turned0 = turn_a(0, [0, 6])
         sigmoid0 = make_sigmoid(a_turned0, [keep([P, H], F32, "sigmoid0_0", "z_low0")[:], keep([P, H], F32, "sigmoid0_1")[:]])
         scatter_on_scalar(1, 1, z_low1[:, 1], 0)
         for lo in (0, C2):
@@ -311,7 +316,7 @@ def tile_moe_hib_silu_kernel(
         z_low2 = empty_gated(2, low2, late_rows[:, 1:3])
         scatter_on_scalar(2, 1, z_third1[:, 0], 4 * T)
 
-        a_turned1 = turn_a(1, [6, 1])
+        a_turned1 = turn_a(1, [7, 1])
         z_turned0 = turn_z(0, [2, 5])
         a_turned2 = turn_a(2, [3, 4])
         weave_wgt(0, placed.tile([P, K + C1, PACK], BF16, name="woven0", offset=WOVEN_AT)[:])
@@ -324,31 +329,31 @@ def tile_moe_hib_silu_kernel(
         regroup(0, da0, 2)
         scatter_on_scalar(0, 2, z_low2[:, 0], "da0_1")
         inner1 = make_inner(a_turned1, sigmoid1, keep([P, HALVES, H], F32, "inner1", "minus_d0_0"))
-        z_turned1 = turn_z(1, [6, 1])
+        z_turned1 = turn_z(1, [7, 1])
         minus_d1 = [make_minus_d(1, half, inner1, sigmoid1) for half in range(HALVES)]
-        sums0 = dx_sums(0, [5, 7])
+        sums0 = dx_sums(0, [5, 6])
         scatter_on_scalar(1, 2, z_low2[:, 1], "sigmoid1")
         da1 = make_da(1, z_turned1, minus_d1)
         weave_wgt(2, placed.tile([P, K + C1, PACK], BF16, name="woven2", offset=WOVEN_AT)[:])
         regroup(1, da1, 0)
         dx0 = keep([P, K_TILES, C1], F32, "dx0", "da1_1")
-        for k in reversed(range(K_TILES)):
+        for k in range(K_TILES):
             nc.scalar.copy(dx0[:, k], sums0[k][:])
         inner2 = make_inner(a_turned2, sigmoid2, keep([P, HALVES, H], F32, "inner2", "minus_d1_0"))
         z_turned2 = turn_z(2, [1, 3])
         minus_d2 = [make_minus_d(2, half, inner2, sigmoid2) for half in range(HALVES)]
         sums1 = dx_sums(1, [2, 0])
-        out_rows = [keep([P, T], F32, "out_rows0", "minus_d2_0"), keep([P, T], F32, "out_rows1")]
-        scatter_dx_on_scalar(0, 1, dx0[:, 1])
+        out_rows = [keep([P, T], F32, "out_rows0"), keep([P, T], F32, "out_rows1", "minus_d2_0")]
+        scatter_dx_on_scalar(0, 0, dx0[:, 0])
         da2 = make_da(2, z_turned2, minus_d2)
         regroup_block(2, 0, da2, 5)
-        dx1_high = empty_dx(1, 1, sums1, nc.scalar.copy, "da2_0")
-        regroup_block(2, 1, da2, 7)
-        dx1_low = empty_dx(1, 0, sums1, nc.scalar.copy, "da2_1")
-        scatter_dx_on_vector(0, 0, dx0[:, 0])
-        sums2 = dx_sums(2, [6, 4])
-        scatter_dx_on_scalar(1, 1, dx1_high)
-        scatter_dx_on_vector(1, 0, dx1_low)
+        dx1_high = empty_dx(1, 0, sums1, nc.scalar.copy, "da2_0")
+        regroup_block(2, 1, da2, 6)
+        dx1_low = empty_dx(1, 1, sums1, nc.scalar.copy, "da2_1")
+        scatter_dx_on_vector(0, 1, dx0[:, 1])
+        sums2 = dx_sums(2, [7, 4])
+        scatter_dx_on_scalar(1, 0, dx1_high)
+        scatter_dx_on_vector(1, 1, dx1_low)
         dx2 = [empty_dx(2, k, sums2, nc.scalar.copy) for k in range(K_TILES)]
         scatter_dx_on_vector(2, 0, dx2[0])
         scatter_dx_on_scalar(2, 1, dx2[1])

@@ -17,11 +17,16 @@ K_TILES = K // P
 I_TILES = H // P
 HALVES = C1 // P
 
-
-WINDOW = 1024
+SCALE_WINDOW = 1024
 SHARE = 64
-LATE_AT = 8 * T
-WOVEN_AT = LATE_AT + 4 * (3 * C1 + HALVES * H)
+
+F32_BYTES = 4
+WINDOW_BYTES = F32_BYTES * T
+A0_AT = F32_BYTES * C1
+LATE_COLUMNS = 3 * C1 + HALVES * H
+LATE_AT = 2 * WINDOW_BYTES
+WOVEN_AT = LATE_AT + F32_BYTES * LATE_COLUMNS
+THIRD2_AT = WOVEN_AT - F32_BYTES * C1 // 2
 
 F32 = mybir.dt.float32
 BF16 = mybir.dt.bfloat16
@@ -47,18 +52,21 @@ def tile_moe_hib_silu_kernel(
         def keep(shape, dtype, name, on=None):
             return held.tile(shape, dtype, name=name, tag=on or name, align_bytes=64)
 
+        def place(shape, dtype, name, offset):
+            return placed.tile(shape, dtype, name=name, offset=offset)
+
         def bank(number, shape, name):
             return psum.tile(shape, F32, name=name, tag="bank%d" % number)
 
         dst_list = held.tile([P, T // PER_COL], U16, name="dst_list")
         offs2_list = held.tile([P, T // PER_COL], U16, name="offs2_list")
         offs_list = held.tile([P, T // PER_COL], U16, name="offs_list")
-        dy_w = keep([P, WINDOW], I32, "dy_w")
-        dy_s = keep([P, WINDOW], U8, "dy_s")
+        dy_w = keep([P, T], I32, "dy_w")
+        dy_s = keep([P, SCALE_WINDOW], U8, "dy_s")
         wet_w = [keep([P, HALVES, 2 * H], U8, "wet_w%d" % g) for g in range(G)]
         wet_s = keep([P, E, H], U8, "wet_s")
         gate_rows = keep([P, T], F32, "gate_rows")
-        a_rows = [placed.tile([P, I_TILES, C1], F32, name="a_rows0", offset=4 * C1)]
+        a_rows = [place([P, I_TILES, C1], F32, "a_rows0", A0_AT)]
         a_rows.extend(keep([P, I_TILES, C1], F32, "a_rows%d" % g) for g in range(1, G))
         wgt_planes = [keep([P, PACK, K], F32, "wgt_planes%d" % g) for g in range(G)]
         ident = keep([P, P], F32, "ident")
@@ -68,7 +76,6 @@ def tile_moe_hib_silu_kernel(
         nc.vector.memset(unit[:, 0:1], 64.0)
         nc.scalar.activation(unit[:, 1:2], unit[:, 0:1], ACT.Sigmoid)
         one = unit[:, 1:2]
-        nc.vector.memset(dy_w[:, T:], 0)
         nc.vector.memset(dy_s[:, T:].bitcast(I32), 0)
         make_identity(nc, ident[:])
 
@@ -79,17 +86,13 @@ def tile_moe_hib_silu_kernel(
         def load_gate(lo, hi):
             nc.sync.dma_start(gate_rows[:, lo:hi], gate[:, lo:hi])
 
-        def load_a(g):
-            columns = a[:, g * C1 : (g + 1) * C1]
-            nc.sync.dma_start(a_rows[g][:], columns.rearrange("(c p) j -> p c j", p=P))
-
         nc.sync.dma_start(dst_list[:], dst)
         for q in range(P // QUAD):
             rows = dy_scales[0, SCALE_ROWS * q : SCALE_ROWS * (q + 1), :].bitcast(I32)
             repeated = rows.unsqueeze(0).to_broadcast([QUAD // SCALE_ROWS, SCALE_ROWS, T // 4])
             queue = nc.scalar if q % 2 else nc.sync
             queue.dma_start(dy_s[QUAD * q : QUAD * (q + 1), 0:T].bitcast(I32), repeated)
-        nc.sync.dma_start(dy_w[:, 0:T], dy_words[0].rearrange("p t d -> p (t d)").bitcast(I32))
+        nc.sync.dma_start(dy_w[:], dy_words[0].rearrange("p t d -> p (t d)").bitcast(I32))
         load_wet_words(0)
         for r in range(SCALE_ROWS):
             rows = wet_scales[:, 0, r : N // 32 : SCALE_ROWS, :].rearrange("e q h -> q e h")
@@ -100,7 +103,8 @@ def tile_moe_hib_silu_kernel(
         load_gate(C1, T)
         load_wet_words(2)
         for g in range(G):
-            load_a(g)
+            columns = a[:, g * C1 : (g + 1) * C1]
+            nc.sync.dma_start(a_rows[g][:], columns.rearrange("(c p) j -> p c j", p=P))
         for g in range(G):
             nc.sync.dma_start(wgt_planes[g][:], wgt[g].rearrange("(p t) k -> p t k", t=PACK))
         nc.sync.dma_start(offs_list[:], offs)
@@ -108,70 +112,45 @@ def tile_moe_hib_silu_kernel(
         def entries(list_tile, lo, hi):
             return list_tile[:, lo // PER_COL : hi // PER_COL]
 
-        slot_scales = {}
-
-        def gather_scales(lo, hi):
-            scale_bytes = keep([P, (hi - lo) * C1], U8, "scale_bytes%d" % lo)
-            nc.vector.tensor_copy(scale_bytes[:], dy_s[:].indirect(entries(dst_list, lo * C1, hi * C1)))
-            for g in range(lo, hi):
-                slot_scales.setdefault(g, scale_bytes[:, (g - lo) * C1 : (g - lo + 1) * C1])
-
-        def gather_words(g, on=None):
-            words = keep([P, C1], U32, "words%d" % g, on)
-            nc.vector.tensor_copy(words[:], dy_w[:].bitcast(U32).indirect(entries(dst_list, g * C1, (g + 1) * C1)))
-            return words
-
-        def first_product(g, words, places, tiles=range(I_TILES)):
+        def first_product(g, places, tiles):
             for c in tiles:
                 for half in range(HALVES):
                     e = g * HALVES + half
                     nc.tensor.matmul_mx(
-                        out=places[c][half],
+                        out=places[c][:, half * C2 : (half + 1) * C2],
                         lhsT=wet_w[g][:, half, 2 * P * c : 2 * P * (c + 1)].bitcast(FP4X4),
                         lhsT_scale=wet_s[:, e, P * c : P * (c + 1)],
-                        rhs=words[:, half * C2 : (half + 1) * C2].bitcast(FP8X4),
-                        rhs_scale=slot_scales[g][:, half * C2 : (half + 1) * C2],
+                        rhs=words[g][:, half * C2 : (half + 1) * C2].bitcast(FP8X4),
+                        rhs_scale=scale_bytes[:, e * C2 : (e + 1) * C2],
                         start=True,
                         stop=True,
                     )
-
-        def by_expert(columns):
-            return [columns[:, half * C2 : (half + 1) * C2] for half in range(HALVES)]
 
         def empty_gated(g, sums, rows):
             gates = gate_rows[:, g * C1 : (g + 1) * C1].unsqueeze(1).to_broadcast(list(rows.shape))
             nc.vector.tensor_tensor(rows[:], sums[:], gates, ALU.mult)
             return rows
 
-        def empty_plain(sums, name, offset=None):
-            if offset is None:
-                rows = keep(list(sums.shape), F32, name)
-            else:
-                rows = placed.tile(list(sums.shape), F32, name=name, offset=offset)
+        def empty_plain(sums, rows):
             nc.scalar.copy(rows[:], sums)
             return rows
 
         z_back = {}
 
-        def z_window(c, g, lo, hi, on):
-            if isinstance(on, int):
-                z_back.setdefault((c, g), placed.tile([P, T], F32, name="z_back%d_%d" % (c, g), offset=on))
-            if (c, g) not in z_back:
-                z_back.setdefault((c, g), keep([P, T], F32, "z_back%d_%d" % (c, g), on))
+        def open_window(c, g, on=None, columns=T):
+            z_back.setdefault((c, g), keep([P, columns], F32, "z_back%d_%d" % (c, g), on))
+
+        def place_window(c, g, offset):
+            z_back.setdefault((c, g), place([P, T], F32, "z_back%d_%d" % (c, g), offset))
+
+        def z_window(c, g, lo, hi):
             return z_back[c, g][:].indirect(entries(offs2_list, g * C1 + lo, g * C1 + hi))
 
-        def scatter_on_scalar(c, g, source, on=None, lo=0, hi=C1):
-            nc.scalar.activation(z_window(c, g, lo, hi, on), source, ACT.Copy)
+        def scatter_on_scalar(c, g, gated, lo=0, hi=C1):
+            nc.scalar.activation(z_window(c, g, lo, hi), gated, ACT.Copy)
 
-        def scatter_on_vector(c, g, source, on=None, lo=0, hi=C1):
-            nc.vector.tensor_tensor(z_window(c, g, lo, hi, on), source, gate_rows[:, g * C1 + lo : g * C1 + hi], ALU.mult)
-
-        def turn(numbers, name, block_of):
-            turned = [bank(number, [P, H], name) for number in numbers]
-            for c in range(I_TILES):
-                for half in range(HALVES):
-                    nc.tensor.transpose(turned[half][:, c * P : (c + 1) * P], block_of(c, half), ident[:])
-            return turned
+        def scatter_on_vector(c, g, sums, lo=0, hi=C1):
+            nc.vector.tensor_tensor(z_window(c, g, lo, hi), sums, gate_rows[:, g * C1 + lo : g * C1 + hi], ALU.mult)
 
         def turn_a(g, numbers):
             turned = [bank(number, [P, H], "a_turned") for number in numbers]
@@ -182,17 +161,20 @@ def tile_moe_hib_silu_kernel(
             return turned
 
         def turn_z(g, numbers):
-            return turn(
-                numbers, "z_turned", lambda c, half: z_back[c, g][:, g * C1 + half * P : g * C1 + (half + 1) * P]
-            )
+            turned = [bank(number, [P, H], "z_turned") for number in numbers]
+            for c in range(I_TILES):
+                for half in range(HALVES):
+                    block = z_back[c, g][:, g * C1 + half * P : g * C1 + (half + 1) * P]
+                    nc.tensor.transpose(turned[half][:, c * P : (c + 1) * P], block, ident[:])
+            return turned
 
         def make_sigmoid(a_turned, sigmoid):
             for half in range(HALVES):
                 nc.scalar.activation(sigmoid[half], a_turned[half][:], ACT.Sigmoid, scale=one)
             return sigmoid
 
-        def halves(name, on=None):
-            tile = keep([P, HALVES, H], F32, name, on)
+        def both_halves(name):
+            tile = keep([P, HALVES, H], F32, name)
             return [tile[:, half] for half in range(HALVES)]
 
         def make_inner(a_turned, sigmoid, inner):
@@ -202,56 +184,52 @@ def tile_moe_hib_silu_kernel(
                 )
             return inner
 
-        def make_minus_d(g, half, inner, sigmoid, on=None):
-            minus_d = keep([P, H], F32, "minus_d%d_%d" % (g, half), on)
-            nc.vector.scalar_tensor_tensor(minus_d[:], inner[:, half], 1.0, sigmoid[half], ALU.subtract, ALU.mult)
+        def make_minus_d(g, inner, sigmoid):
+            minus_d = []
+            for half in range(HALVES):
+                minus_d.append(keep([P, H], F32, "minus_d%d_%d" % (g, half)))
+                nc.vector.scalar_tensor_tensor(
+                    minus_d[half][:], inner[:, half], 1.0, sigmoid[half], ALU.subtract, ALU.mult
+                )
             return minus_d
 
         def make_da(g, z_turned, minus_d):
             da = [keep([P, H], BF16, "da%d_%d" % (g, half)) for half in range(HALVES)]
             for half in range(HALVES):
-                nc.vector.scalar_tensor_tensor(da[half][:], z_turned[half][:], -1.0, minus_d[half][:], ALU.mult, ALU.mult)
+                nc.vector.scalar_tensor_tensor(
+                    da[half][:], z_turned[half][:], -1.0, minus_d[half][:], ALU.mult, ALU.mult
+                )
             return da
 
+        woven_shape = [P, K + C1, PACK]
         woven = {}
 
-        def weave_wgt(g, place):
-            woven.setdefault(g, place)
+        def weave_wgt(g, tile):
+            woven.setdefault(g, tile)
             planes = wgt_planes[g][:].rearrange("p t k -> p k t")
-            nc.gpsimd.tensor_scalar(woven[g][:, 0:K, :], planes, 1.0, 0.0, ALU.mult, ALU.add)
+            nc.gpsimd.tensor_scalar(tile[:, 0:K, :], planes, 1.0, 0.0, ALU.mult, ALU.add)
 
-        def woven_tile(g, on):
-            return keep([P, K + C1, PACK], BF16, "woven%d" % g, on)[:]
-
-        def turn_words(da, by_word):
-            pairs = da[:].bitcast(F32)
-            for u in range(2):
-                nc.tensor.transpose(by_word[:, u, :], pairs[:, u : H // 2 : 2], ident[:])
-
-        def word_columns(g, lo, hi):
+        def regroup(g, da, lo, hi, number):
+            by_word = bank(number, [P, hi - lo, 2, P], "by_word")
+            for half in range(lo, hi):
+                pairs = da[half][:].bitcast(F32)
+                for u in range(2):
+                    nc.tensor.transpose(by_word[:, half - lo, u, :], pairs[:, u : H // 2 : 2], ident[:])
             columns = woven[g][:, K + lo * P : K + hi * P, :].rearrange("p s t -> p (s t)").bitcast(F32)
-            return columns.rearrange("p (b s u) -> p b s u", b=hi - lo, u=2)
+            nc.scalar.copy(
+                columns.rearrange("p (b s u) -> p b s u", b=hi - lo, u=2), by_word[:].rearrange("p b u s -> p b s u")
+            )
 
-        def regroup(g, da, number):
-            by_word = bank(number, [P, HALVES, 2, P], "by_word")
-            for half in range(HALVES):
-                turn_words(da[half], by_word[:, half])
-            nc.scalar.copy(word_columns(g, 0, HALVES), by_word[:].rearrange("p b u s -> p b s u"))
-
-        def regroup_block(g, half, da, number):
-            by_word = bank(number, [P, 1, 2, P], "by_word")
-            turn_words(da[half], by_word[:, 0])
-            nc.scalar.copy(word_columns(g, half, half + 1), by_word[:].rearrange("p b u s -> p b s u"))
-
-        def second_product(g, places, on=None):
-            codes = keep([P, K + C1], U32, "codes%d" % g, on)
+        def second_product(g, numbers):
+            sums = [bank(number, [P, C1], "dx_sums") for number in numbers]
+            codes = keep([P, K + C1], U32, "codes%d" % g)
             scales = keep([P, K + C1], U8, "scales%d" % g)
             nc.vector.quantize_mx(
-                out=codes[:].bitcast(FP8X4), scales=scales[:], in_=woven[g].rearrange("p c t -> p (c t)")
+                out=codes[:].bitcast(FP8X4), scales=scales[:], in_=woven[g][:].rearrange("p c t -> p (c t)")
             )
             for k in range(K_TILES):
                 nc.tensor.matmul_mx(
-                    out=places[k],
+                    out=sums[k][:],
                     lhsT=codes[:, k * P : (k + 1) * P].bitcast(FP8X4),
                     lhsT_scale=scales[:, k * P : (k + 1) * P],
                     rhs=codes[:, K:].bitcast(FP8X4),
@@ -259,16 +237,7 @@ def tile_moe_hib_silu_kernel(
                     start=True,
                     stop=True,
                 )
-
-        def dx_sums(g, numbers, on=None):
-            sums = [bank(number, [P, C1], "dx_sums") for number in numbers]
-            second_product(g, [sums[k][:] for k in range(K_TILES)], on)
             return sums
-
-        def empty_dx(g, k, sums, copy, on=None):
-            rows = keep([P, C1], F32, "dx%d_%d" % (g, k), on)
-            copy(rows[:], sums[k][:])
-            return rows
 
         def dx_window(g, k):
             return out_rows[k][:].indirect(entries(offs_list, g * C1, (g + 1) * C1))
@@ -279,82 +248,107 @@ def tile_moe_hib_silu_kernel(
         def scatter_dx_on_vector(g, k, rows):
             nc.vector.tensor_copy(dx_window(g, k), rows[:])
 
-        gather_scales(0, G)
-        words0, words1, words2 = [gather_words(g) for g in range(G)]
-        sums = [bank(number, [P, 1, C1], "sums") for number in (0, 6, 1, 7)]
-        first_product(0, words0, [by_expert(sums[c][:, 0]) for c in range(I_TILES)], [2, 0, 3, 1])
+        scale_bytes = keep([P, T], U8, "scale_bytes")
+        nc.vector.tensor_copy(scale_bytes[:], dy_s[:].indirect(dst_list[:]))
+        words = []
+        for g in range(G):
+            words.append(keep([P, C1], U32, "words%d" % g))
+            nc.vector.tensor_copy(words[g][:], dy_w[:].bitcast(U32).indirect(entries(dst_list, g * C1, (g + 1) * C1)))
+
+        sums0 = [bank(number, [P, 1, C1], "sums0") for number in (0, 6, 1, 7)]
+        first_product(0, [sums0[c][:, 0] for c in range(I_TILES)], [2, 0, 3, 1])
         z_low0 = keep([P, 2, C1], F32, "z_low0")
-        empty_gated(0, sums[0], z_low0[:, 0:1])
-        z_third0, z_fourth0 = empty_plain(sums[2][:, 0, 0 : C1 - SHARE], "z_third0"), empty_plain(sums[3][:, 0], "z_fourth0")
-        z_back.setdefault((2, 0), keep([P, 2 * C1], F32, "z_back2_0"))
-        scatter_on_vector(2, 0, z_third0[:], None, 0, C1 - SHARE)
-        empty_gated(0, sums[1], z_low0[:, 1:2])
+        empty_gated(0, sums0[0], z_low0[:, 0:1])
+        z_third0 = empty_plain(sums0[2][:, 0, 0 : C1 - SHARE], keep([P, C1 - SHARE], F32, "z_third0"))
+        z_fourth0 = empty_plain(sums0[3][:, 0], keep([P, C1], F32, "z_fourth0"))
+        open_window(2, 0, columns=2 * C1)
+        scatter_on_vector(2, 0, z_third0[:], 0, C1 - SHARE)
+        empty_gated(0, sums0[1], z_low0[:, 1:2])
         low1, third1, fourth1 = bank(2, [P, 2, C1], "low1"), bank(3, [P, 1, C1], "third1"), bank(7, [P, C1], "fourth1")
-        first_product(1, words1, [by_expert(low1[:, 0]), by_expert(low1[:, 1]), by_expert(third1[:, 0]), by_expert(fourth1)], [3, 0, 1, 2])
+        first_product(1, [low1[:, 0], low1[:, 1], third1[:, 0], fourth1], [3, 0, 1, 2])
         low2, high2 = bank(4, [P, 2, C1], "low2"), bank(5, [P, 2, C1], "high2")
-        first_product(2, words2, [by_expert(low2[:, 0]), by_expert(low2[:, 1]), by_expert(high2[:, 0]), by_expert(high2[:, 1])], [2, 3, 0, 1])
+        first_product(2, [low2[:, 0], low2[:, 1], high2[:, 0], high2[:, 1]], [2, 3, 0, 1])
+
+        open_window(0, 0)
         scatter_on_scalar(0, 0, z_low0[:, 0])
-        z_fourth1 = empty_plain(fourth1[:], "z_fourth1")
-        scatter_on_scalar(1, 0, z_low0[:, 1], "wet_w1")
-        z_third2, z_fourth2 = empty_plain(high2[:, 0], "z_third2", WOVEN_AT - 2 * C1), empty_plain(high2[:, 1], "z_fourth2")
+        z_fourth1 = empty_plain(fourth1[:], keep([P, C1], F32, "z_fourth1"))
+        open_window(1, 0, "wet_w1")
+        scatter_on_scalar(1, 0, z_low0[:, 1])
+        z_third2 = empty_plain(high2[:, 0], place([P, C1], F32, "z_third2", THIRD2_AT))
+        z_fourth2 = empty_plain(high2[:, 1], keep([P, C1], F32, "z_fourth2"))
+        open_window(3, 0)
         scatter_on_vector(3, 0, z_fourth0[:])
         z_low1 = empty_gated(1, low1, keep([P, 2, C1], F32, "z_low1", "z_third0"))
-        z_rest0 = keep([P, SHARE], F32, "z_rest0", "words2")
-        nc.vector.tensor_tensor(z_rest0[:], sums[2][:, 0, C1 - SHARE :], gate_rows[:, C1 - SHARE : C1], ALU.mult)
-        scatter_on_scalar(0, 1, z_low1[:, 0], "wet_w2")
-        scatter_on_scalar(2, 0, z_rest0[:], None, C1 - SHARE, C1)
+        z_share = keep([P, SHARE], F32, "z_share", "words2")
+        nc.vector.tensor_tensor(z_share[:], sums0[2][:, 0, C1 - SHARE :], gate_rows[:, C1 - SHARE : C1], ALU.mult)
+        open_window(0, 1, "wet_w2")
+        scatter_on_scalar(0, 1, z_low1[:, 0])
+        scatter_on_scalar(2, 0, z_share[:], C1 - SHARE, C1)
+        open_window(3, 1)
         scatter_on_vector(3, 1, z_fourth1[:])
         a_turned0 = turn_a(0, [0, 6])
-        sigmoid0 = make_sigmoid(a_turned0, [keep([P, H], F32, "sigmoid0_0", "z_low0")[:], keep([P, H], F32, "sigmoid0_1")[:]])
-        scatter_on_scalar(1, 1, z_low1[:, 1], 0)
-        for lo in (0, C2):
-            scatter_on_vector(2, 2, z_third2[:, lo : lo + C2], "z_fourth0", lo, lo + C2)
-            scatter_on_vector(3, 2, z_fourth2[:, lo : lo + C2], None, lo, lo + C2)
-        late = placed.tile([P, 3 * C1 + HALVES * H], F32, name="late", offset=LATE_AT)
+        sigmoid0 = make_sigmoid(
+            a_turned0, [keep([P, H], F32, "sigmoid0_0", "z_low0")[:], keep([P, H], F32, "sigmoid0_1")[:]]
+        )
+        place_window(1, 1, 0)
+        scatter_on_scalar(1, 1, z_low1[:, 1])
+        open_window(2, 2, "z_fourth0")
+        scatter_on_vector(2, 2, z_third2[:, 0:C2], 0, C2)
+        open_window(3, 2)
+        scatter_on_vector(3, 2, z_fourth2[:, 0:C2], 0, C2)
+        scatter_on_vector(2, 2, z_third2[:, C2:C1], C2, C1)
+        scatter_on_vector(3, 2, z_fourth2[:, C2:C1], C2, C1)
+
+        late = place([P, LATE_COLUMNS], F32, "late", LATE_AT)
         late_rows = late[:, 0 : 3 * C1].rearrange("p (c s) -> p c s", s=C1)
         z_third1 = empty_gated(1, third1, late_rows[:, 0:1])
         z_low2 = empty_gated(2, low2, late_rows[:, 1:3])
-        scatter_on_scalar(2, 1, z_third1[:, 0], 4 * T)
-
+        place_window(2, 1, WINDOW_BYTES)
+        scatter_on_scalar(2, 1, z_third1[:, 0])
         a_turned1 = turn_a(1, [7, 1])
         z_turned0 = turn_z(0, [2, 5])
         a_turned2 = turn_a(2, [3, 4])
-        weave_wgt(0, placed.tile([P, K + C1, PACK], BF16, name="woven0", offset=WOVEN_AT)[:])
+        weave_wgt(0, place(woven_shape, BF16, "woven0", WOVEN_AT))
         inner0 = make_inner(a_turned0, sigmoid0, late[:, 3 * C1 :].rearrange("p (b i) -> p b i", b=HALVES))
-        minus_d0 = [make_minus_d(0, half, inner0, sigmoid0) for half in range(HALVES)]
+        minus_d0 = make_minus_d(0, inner0, sigmoid0)
+
         da0 = make_da(0, z_turned0, minus_d0)
-        sigmoid1 = make_sigmoid(a_turned1, halves("sigmoid1"))
-        sigmoid2 = make_sigmoid(a_turned2, halves("sigmoid2"))
-        weave_wgt(1, woven_tile(1, "z_low0"))
-        regroup(0, da0, 2)
-        scatter_on_scalar(0, 2, z_low2[:, 0], "da0_1")
+        sigmoid1 = make_sigmoid(a_turned1, both_halves("sigmoid1"))
+        sigmoid2 = make_sigmoid(a_turned2, both_halves("sigmoid2"))
+        weave_wgt(1, keep(woven_shape, BF16, "woven1", "z_low0"))
+        regroup(0, da0, 0, HALVES, 2)
+        open_window(0, 2, "da0_1")
+        scatter_on_scalar(0, 2, z_low2[:, 0])
         inner1 = make_inner(a_turned1, sigmoid1, keep([P, HALVES, H], F32, "inner1", "minus_d0_0"))
         z_turned1 = turn_z(1, [7, 1])
-        minus_d1 = [make_minus_d(1, half, inner1, sigmoid1) for half in range(HALVES)]
-        sums0 = dx_sums(0, [5, 6])
-        scatter_on_scalar(1, 2, z_low2[:, 1], "sigmoid1")
+        minus_d1 = make_minus_d(1, inner1, sigmoid1)
+        dx_sums0 = second_product(0, [5, 6])
+        open_window(1, 2, "sigmoid1")
+        scatter_on_scalar(1, 2, z_low2[:, 1])
+
         da1 = make_da(1, z_turned1, minus_d1)
-        weave_wgt(2, placed.tile([P, K + C1, PACK], BF16, name="woven2", offset=WOVEN_AT)[:])
-        regroup(1, da1, 0)
+        weave_wgt(2, place(woven_shape, BF16, "woven2", WOVEN_AT))
+        regroup(1, da1, 0, HALVES, 0)
         dx0 = keep([P, K_TILES, C1], F32, "dx0", "da1_1")
         for k in range(K_TILES):
-            nc.scalar.copy(dx0[:, k], sums0[k][:])
+            empty_plain(dx_sums0[k][:], dx0[:, k])
         inner2 = make_inner(a_turned2, sigmoid2, keep([P, HALVES, H], F32, "inner2", "minus_d1_0"))
         z_turned2 = turn_z(2, [1, 3])
-        minus_d2 = [make_minus_d(2, half, inner2, sigmoid2) for half in range(HALVES)]
-        sums1 = dx_sums(1, [2, 0])
+        minus_d2 = make_minus_d(2, inner2, sigmoid2)
+        dx_sums1 = second_product(1, [2, 0])
+
         out_rows = [keep([P, T], F32, "out_rows0"), keep([P, T], F32, "out_rows1", "minus_d2_0")]
         scatter_dx_on_scalar(0, 0, dx0[:, 0])
         da2 = make_da(2, z_turned2, minus_d2)
-        regroup_block(2, 0, da2, 5)
-        dx1_high = empty_dx(1, 0, sums1, nc.scalar.copy, "da2_0")
-        regroup_block(2, 1, da2, 6)
-        dx1_low = empty_dx(1, 1, sums1, nc.scalar.copy, "da2_1")
+        dx1 = []
+        for half, number in enumerate([5, 6]):
+            regroup(2, da2, half, half + 1, number)
+            dx1.append(empty_plain(dx_sums1[half][:], keep([P, C1], F32, "dx1_%d" % half, "da2_%d" % half)))
         scatter_dx_on_vector(0, 1, dx0[:, 1])
-        sums2 = dx_sums(2, [7, 4])
-        scatter_dx_on_scalar(1, 0, dx1_high)
-        scatter_dx_on_vector(1, 1, dx1_low)
-        dx2 = [empty_dx(2, k, sums2, nc.scalar.copy) for k in range(K_TILES)]
+        dx_sums2 = second_product(2, [7, 4])
+        scatter_dx_on_scalar(1, 0, dx1[0])
+        scatter_dx_on_vector(1, 1, dx1[1])
+        dx2 = [empty_plain(dx_sums2[k][:], keep([P, C1], F32, "dx2_%d" % k)) for k in range(K_TILES)]
         scatter_dx_on_vector(2, 0, dx2[0])
         scatter_dx_on_scalar(2, 1, dx2[1])
         for k, queue in enumerate([nc.sync, nc.scalar]):

@@ -17,16 +17,15 @@ K_TILES = K // P
 I_TILES = H // P
 HALVES = C1 // P
 
-SCALE_WINDOW = 1024
-SHARE = 64
-
-F32_BYTES = 4
-WINDOW_BYTES = F32_BYTES * T
-A0_AT = F32_BYTES * C1
-LATE_COLUMNS = 3 * C1 + HALVES * H
-LATE_AT = 2 * WINDOW_BYTES
-WOVEN_AT = LATE_AT + F32_BYTES * LATE_COLUMNS
-THIRD2_AT = WOVEN_AT - F32_BYTES * C1 // 2
+W01_AT = 0
+A1_AT = 1024
+W11_AT = 3072
+INNER1_AT = 6144
+A2_AT = INNER1_AT + 3584
+W31_AT = INNER1_AT + 4096
+W21_AT = W31_AT + 3072
+REST0_AT = W21_AT + 3072
+AROWS = {1: A1_AT, 2: A2_AT}
 
 F32 = mybir.dt.float32
 BF16 = mybir.dt.bfloat16
@@ -50,10 +49,9 @@ def tile_moe_hib_silu_kernel(
         psum = ctx.enter_context(tc.psum_pool(name="psum", bufs=1))
 
         def keep(shape, dtype, name, on=None):
+            if isinstance(on, int):
+                return placed.tile(shape, dtype, name=name, offset=on)
             return held.tile(shape, dtype, name=name, tag=on or name, align_bytes=64)
-
-        def place(shape, dtype, name, offset):
-            return placed.tile(shape, dtype, name=name, offset=offset)
 
         def bank(number, shape, name):
             return psum.tile(shape, F32, name=name, tag="bank%d" % number)
@@ -62,21 +60,18 @@ def tile_moe_hib_silu_kernel(
         offs2_list = held.tile([P, T // PER_COL], U16, name="offs2_list")
         offs_list = held.tile([P, T // PER_COL], U16, name="offs_list")
         dy_w = keep([P, T], I32, "dy_w")
-        dy_s = keep([P, SCALE_WINDOW], U8, "dy_s")
+        dy_s = keep([P, T], U8, "dy_s")
         wet_w = [keep([P, HALVES, 2 * H], U8, "wet_w%d" % g) for g in range(G)]
         wet_s = keep([P, E, H], U8, "wet_s")
         gate_rows = keep([P, T], F32, "gate_rows")
-        a_rows = [place([P, I_TILES, C1], F32, "a_rows0", A0_AT)]
-        a_rows.extend(keep([P, I_TILES, C1], F32, "a_rows%d" % g) for g in range(1, G))
+        a_rows = [keep([P, I_TILES, C1], F32, "a_rows%d" % g, AROWS.get(g)) for g in range(G)]
         wgt_planes = [keep([P, PACK, K], F32, "wgt_planes%d" % g) for g in range(G)]
         ident = keep([P, P], F32, "ident")
 
         nc.vector.memset(wet_s[:].rearrange("p e h -> p (e h)").bitcast(I32), 0)
         unit = held.tile([P, 2], F32, name="unit")
         nc.vector.memset(unit[:, 0:1], 64.0)
-        nc.scalar.activation(unit[:, 1:2], unit[:, 0:1], ACT.Sigmoid)
         one = unit[:, 1:2]
-        nc.vector.memset(dy_s[:, T:].bitcast(I32), 0)
         make_identity(nc, ident[:])
 
         def load_wet_words(g):
@@ -86,33 +81,27 @@ def tile_moe_hib_silu_kernel(
         def load_gate(lo, hi):
             nc.sync.dma_start(gate_rows[:, lo:hi], gate[:, lo:hi])
 
-        nc.sync.dma_start(dst_list[:], dst)
-        for q in range(P // QUAD):
-            rows = dy_scales[0, SCALE_ROWS * q : SCALE_ROWS * (q + 1), :].bitcast(I32)
-            repeated = rows.unsqueeze(0).to_broadcast([QUAD // SCALE_ROWS, SCALE_ROWS, T // 4])
-            queue = nc.scalar if q % 2 else nc.sync
-            queue.dma_start(dy_s[QUAD * q : QUAD * (q + 1), 0:T].bitcast(I32), repeated)
-        nc.sync.dma_start(dy_w[:], dy_words[0].rearrange("p t d -> p (t d)").bitcast(I32))
-        load_wet_words(0)
-        for r in range(SCALE_ROWS):
-            rows = wet_scales[:, 0, r : N // 32 : SCALE_ROWS, :].rearrange("e q h -> q e h")
-            nc.sync.dma_start(wet_s[r:P:QUAD, :, :].bitcast(I32), rows.bitcast(I32))
-        load_gate(0, C1)
-        nc.sync.dma_start(offs2_list[:], offs2)
-        load_wet_words(1)
-        load_gate(C1, T)
-        load_wet_words(2)
-        for g in range(G):
+        def load_a(g):
             columns = a[:, g * C1 : (g + 1) * C1]
             nc.sync.dma_start(a_rows[g][:], columns.rearrange("(c p) j -> p c j", p=P))
-        for g in range(G):
+
+        def load_wgt(g):
             nc.sync.dma_start(wgt_planes[g][:], wgt[g].rearrange("(p t) k -> p t k", t=PACK))
-        nc.sync.dma_start(offs_list[:], offs)
 
         def entries(list_tile, lo, hi):
             return list_tile[:, lo // PER_COL : hi // PER_COL]
 
-        def first_product(g, places, tiles):
+        def gather_scales(lo, hi, on=None):
+            gathered = keep([P, hi - lo], U8, "scale_bytes%d" % lo, on)
+            nc.vector.tensor_copy(gathered[:], dy_s[:].indirect(entries(dst_list, lo, hi)))
+            return gathered
+
+        def gather_words(g, on=None):
+            gathered = keep([P, C1], U32, "words%d" % g, on)
+            nc.vector.tensor_copy(gathered[:], dy_w[:].bitcast(U32).indirect(entries(dst_list, g * C1, (g + 1) * C1)))
+            return gathered
+
+        def first_product(g, words, scale_bytes, places, tiles):
             for c in tiles:
                 for half in range(HALVES):
                     e = g * HALVES + half
@@ -120,37 +109,44 @@ def tile_moe_hib_silu_kernel(
                         out=places[c][:, half * C2 : (half + 1) * C2],
                         lhsT=wet_w[g][:, half, 2 * P * c : 2 * P * (c + 1)].bitcast(FP4X4),
                         lhsT_scale=wet_s[:, e, P * c : P * (c + 1)],
-                        rhs=words[g][:, half * C2 : (half + 1) * C2].bitcast(FP8X4),
-                        rhs_scale=scale_bytes[:, e * C2 : (e + 1) * C2],
+                        rhs=words[:, half * C2 : (half + 1) * C2].bitcast(FP8X4),
+                        rhs_scale=scale_bytes[:, half * C2 : (half + 1) * C2],
                         start=True,
                         stop=True,
                     )
 
-        def empty_gated(g, sums, rows):
-            gates = gate_rows[:, g * C1 : (g + 1) * C1].unsqueeze(1).to_broadcast(list(rows.shape))
+        def empty_gated(g, sums, name, on=None):
+            rows = keep(list(sums.shape), F32, name, on)
+            gates = gate_rows[:, g * C1 : (g + 1) * C1].unsqueeze(1).to_broadcast(list(sums.shape))
             nc.vector.tensor_tensor(rows[:], sums[:], gates, ALU.mult)
             return rows
 
-        def empty_plain(sums, rows):
-            nc.scalar.copy(rows[:], sums)
+        def empty_plain(sums, name, on=None):
+            rows = keep(list(sums.shape), F32, name, on)
+            nc.scalar.copy(rows[:], sums[:])
+            return rows
+
+        def empty_on_vector(sums, name, on=None):
+            rows = keep(list(sums.shape), F32, name, on)
+            nc.vector.tensor_copy(rows[:], sums[:])
             return rows
 
         z_back = {}
 
-        def open_window(c, g, on=None, columns=T):
-            z_back.setdefault((c, g), keep([P, columns], F32, "z_back%d_%d" % (c, g), on))
-
-        def place_window(c, g, offset):
-            z_back.setdefault((c, g), place([P, T], F32, "z_back%d_%d" % (c, g), offset))
-
-        def z_window(c, g, lo, hi):
+        def z_window(c, g, lo, hi, on):
+            if (c, g) not in z_back:
+                z_back.setdefault((c, g), keep([P, T], F32, "z_back%d_%d" % (c, g), on))
             return z_back[c, g][:].indirect(entries(offs2_list, g * C1 + lo, g * C1 + hi))
 
-        def scatter_on_scalar(c, g, gated, lo=0, hi=C1):
-            nc.scalar.activation(z_window(c, g, lo, hi), gated, ACT.Copy)
+        def z_on_scalar(c, g, gated, on=None, lo=0, hi=C1):
+            nc.scalar.activation(z_window(c, g, lo, hi, on), gated[:, lo:hi], ACT.Copy)
 
-        def scatter_on_vector(c, g, sums, lo=0, hi=C1):
-            nc.vector.tensor_tensor(z_window(c, g, lo, hi), sums, gate_rows[:, g * C1 + lo : g * C1 + hi], ALU.mult)
+        def z_on_vector(c, g, gated, on=None, lo=0, hi=C1):
+            nc.vector.tensor_copy(z_window(c, g, lo, hi, on), gated[:, lo:hi])
+
+        def z_gating_on_vector(c, g, sums, on=None, lo=0, hi=C1):
+            gates = gate_rows[:, g * C1 + lo : g * C1 + hi]
+            nc.vector.tensor_tensor(z_window(c, g, lo, hi, on), sums[:, lo:hi], gates, ALU.mult)
 
         def turn_a(g, numbers):
             turned = [bank(number, [P, H], "a_turned") for number in numbers]
@@ -160,54 +156,50 @@ def tile_moe_hib_silu_kernel(
                     nc.tensor.transpose(turned[half][:, c * P : (c + 1) * P], block, ident[:])
             return turned
 
-        def turn_z(g, numbers):
+        def turn_z(g, numbers, blocks):
             turned = [bank(number, [P, H], "z_turned") for number in numbers]
-            for c in range(I_TILES):
-                for half in range(HALVES):
-                    block = z_back[c, g][:, g * C1 + half * P : g * C1 + (half + 1) * P]
-                    nc.tensor.transpose(turned[half][:, c * P : (c + 1) * P], block, ident[:])
+            for c, half in blocks:
+                block = z_back[c, g][:, g * C1 + half * P : g * C1 + (half + 1) * P]
+                nc.tensor.transpose(turned[half][:, c * P : (c + 1) * P], block, ident[:])
             return turned
 
-        def make_sigmoid(a_turned, sigmoid):
+        def make_sigmoid(g, a_turned, on=None):
+            sigmoid = keep([P, HALVES, H], F32, "sigmoid%d" % g, on)
             for half in range(HALVES):
-                nc.scalar.activation(sigmoid[half], a_turned[half][:], ACT.Sigmoid, scale=one)
+                nc.scalar.activation(sigmoid[:, half], a_turned[half][:], ACT.Sigmoid, scale=one)
             return sigmoid
 
-        def both_halves(name):
-            tile = keep([P, HALVES, H], F32, name)
-            return [tile[:, half] for half in range(HALVES)]
-
-        def make_inner(a_turned, sigmoid, inner):
+        def make_inner(g, a_turned, sigmoid, on=None):
+            inner = keep([P, HALVES, H], F32, "inner%d" % g, on)
             for half in range(HALVES):
                 nc.vector.scalar_tensor_tensor(
-                    inner[:, half], sigmoid[half], 1.0, a_turned[half][:], ALU.subtract, ALU.mult
+                    inner[:, half], sigmoid[:, half], 1.0, a_turned[half][:], ALU.subtract, ALU.mult
                 )
             return inner
 
-        def make_minus_d(g, inner, sigmoid):
-            minus_d = []
-            for half in range(HALVES):
-                minus_d.append(keep([P, H], F32, "minus_d%d_%d" % (g, half)))
-                nc.vector.scalar_tensor_tensor(
-                    minus_d[half][:], inner[:, half], 1.0, sigmoid[half], ALU.subtract, ALU.mult
-                )
-            return minus_d
+        def flat(tile):
+            return tile.rearrange("p b i -> p (b i)")
 
-        def make_da(g, z_turned, minus_d):
-            da = [keep([P, H], BF16, "da%d_%d" % (g, half)) for half in range(HALVES)]
-            for half in range(HALVES):
-                nc.vector.scalar_tensor_tensor(
-                    da[half][:], z_turned[half][:], -1.0, minus_d[half][:], ALU.mult, ALU.mult
-                )
+        def make_rest(rest, inner):
+            nc.gpsimd.tensor_scalar(rest, inner, -1.0, 1.0, ALU.mult, ALU.add)
+
+        def make_d(d, rest, sigmoid):
+            nc.gpsimd.tensor_tensor(d, rest, sigmoid, ALU.mult)
+
+        def turned_tile(name, on=None):
+            return keep([P, HALVES, H], F32, name, on)
+
+        def make_da(g, half, z_turned, d, on=None):
+            da = keep([P, H], BF16, "da%d_%d" % (g, half), on)
+            nc.vector.tensor_tensor(da[:], z_turned[half][:], d[:, half], ALU.mult)
             return da
 
-        woven_shape = [P, K + C1, PACK]
         woven = {}
 
-        def weave_wgt(g, tile):
-            woven.setdefault(g, tile)
+        def weave_wgt(g, on=None):
+            woven.setdefault(g, keep([P, K + C1, PACK], BF16, "woven%d" % g, on))
             planes = wgt_planes[g][:].rearrange("p t k -> p k t")
-            nc.gpsimd.tensor_scalar(tile[:, 0:K, :], planes, 1.0, 0.0, ALU.mult, ALU.add)
+            nc.gpsimd.tensor_scalar(woven[g][:, 0:K, :], planes, 1.0, 0.0, ALU.mult, ALU.add)
 
         def regroup(g, da, lo, hi, number):
             by_word = bank(number, [P, hi - lo, 2, P], "by_word")
@@ -220,16 +212,18 @@ def tile_moe_hib_silu_kernel(
                 columns.rearrange("p (b s u) -> p b s u", b=hi - lo, u=2), by_word[:].rearrange("p b u s -> p b s u")
             )
 
-        def second_product(g, numbers):
-            sums = [bank(number, [P, C1], "dx_sums") for number in numbers]
-            codes = keep([P, K + C1], U32, "codes%d" % g)
+        def second_product(g, places, cuts, on=None):
+            codes = keep([P, K + C1], U32, "codes%d" % g, on)
             scales = keep([P, K + C1], U8, "scales%d" % g)
-            nc.vector.quantize_mx(
-                out=codes[:].bitcast(FP8X4), scales=scales[:], in_=woven[g][:].rearrange("p c t -> p (c t)")
-            )
+            for lo, hi in zip([0] + cuts, cuts + [K + C1]):
+                nc.vector.quantize_mx(
+                    out=codes[:, lo:hi].bitcast(FP8X4),
+                    scales=scales[:, lo:hi],
+                    in_=woven[g][:, lo:hi, :].rearrange("p c t -> p (c t)"),
+                )
             for k in range(K_TILES):
                 nc.tensor.matmul_mx(
-                    out=sums[k][:],
+                    out=places[k],
                     lhsT=codes[:, k * P : (k + 1) * P].bitcast(FP8X4),
                     lhsT_scale=scales[:, k * P : (k + 1) * P],
                     rhs=codes[:, K:].bitcast(FP8X4),
@@ -237,119 +231,131 @@ def tile_moe_hib_silu_kernel(
                     start=True,
                     stop=True,
                 )
-            return sums
 
-        def dx_window(g, k):
-            return out_rows[k][:].indirect(entries(offs_list, g * C1, (g + 1) * C1))
+        out_rows = {}
 
-        def scatter_dx_on_scalar(g, k, rows):
-            nc.scalar.activation(dx_window(g, k), rows[:], ACT.Copy)
+        def dx_window(g, k, lo, hi, on):
+            if k not in out_rows:
+                out_rows.setdefault(k, keep([P, T], F32, "out_rows%d" % k, on))
+            return out_rows[k][:].indirect(entries(offs_list, g * C1 + lo, g * C1 + hi))
 
-        def scatter_dx_on_vector(g, k, rows):
-            nc.vector.tensor_copy(dx_window(g, k), rows[:])
+        def dx_on_scalar(g, k, rows, on=None, lo=0, hi=C1):
+            nc.scalar.activation(dx_window(g, k, lo, hi, on), rows[:, lo:hi], ACT.Copy)
 
-        scale_bytes = keep([P, T], U8, "scale_bytes")
-        nc.vector.tensor_copy(scale_bytes[:], dy_s[:].indirect(dst_list[:]))
-        words = []
-        for g in range(G):
-            words.append(keep([P, C1], U32, "words%d" % g))
-            nc.vector.tensor_copy(words[g][:], dy_w[:].bitcast(U32).indirect(entries(dst_list, g * C1, (g + 1) * C1)))
+        def dx_on_vector(g, k, rows, on=None, lo=0, hi=C1):
+            nc.vector.tensor_copy(dx_window(g, k, lo, hi, on), rows[:, lo:hi])
 
-        sums0 = [bank(number, [P, 1, C1], "sums0") for number in (0, 6, 1, 7)]
-        first_product(0, [sums0[c][:, 0] for c in range(I_TILES)], [2, 0, 3, 1])
-        z_low0 = keep([P, 2, C1], F32, "z_low0")
-        empty_gated(0, sums0[0], z_low0[:, 0:1])
-        z_third0 = empty_plain(sums0[2][:, 0, 0 : C1 - SHARE], keep([P, C1 - SHARE], F32, "z_third0"))
-        z_fourth0 = empty_plain(sums0[3][:, 0], keep([P, C1], F32, "z_fourth0"))
-        open_window(2, 0, columns=2 * C1)
-        scatter_on_vector(2, 0, z_third0[:], 0, C1 - SHARE)
-        empty_gated(0, sums0[1], z_low0[:, 1:2])
-        low1, third1, fourth1 = bank(2, [P, 2, C1], "low1"), bank(3, [P, 1, C1], "third1"), bank(7, [P, C1], "fourth1")
-        first_product(1, [low1[:, 0], low1[:, 1], third1[:, 0], fourth1], [3, 0, 1, 2])
-        low2, high2 = bank(4, [P, 2, C1], "low2"), bank(5, [P, 2, C1], "high2")
-        first_product(2, [low2[:, 0], low2[:, 1], high2[:, 0], high2[:, 1]], [2, 3, 0, 1])
+        def load_dy():
+            nc.sync.dma_start(dst_list[:], dst)
+            for q in range(P // QUAD):
+                rows = dy_scales[0, SCALE_ROWS * q : SCALE_ROWS * (q + 1), :].bitcast(I32)
+                repeated = rows.unsqueeze(0).to_broadcast([QUAD // SCALE_ROWS, SCALE_ROWS, T // 4])
+                queue = nc.scalar if q % 2 else nc.sync
+                queue.dma_start(dy_s[QUAD * q : QUAD * (q + 1), :].bitcast(I32), repeated)
+            nc.sync.dma_start(dy_w[:], dy_words[0].rearrange("p t d -> p (t d)").bitcast(I32))
 
-        open_window(0, 0)
-        scatter_on_scalar(0, 0, z_low0[:, 0])
-        z_fourth1 = empty_plain(fourth1[:], keep([P, C1], F32, "z_fourth1"))
-        open_window(1, 0, "wet_w1")
-        scatter_on_scalar(1, 0, z_low0[:, 1])
-        z_third2 = empty_plain(high2[:, 0], place([P, C1], F32, "z_third2", THIRD2_AT))
-        z_fourth2 = empty_plain(high2[:, 1], keep([P, C1], F32, "z_fourth2"))
-        open_window(3, 0)
-        scatter_on_vector(3, 0, z_fourth0[:])
-        z_low1 = empty_gated(1, low1, keep([P, 2, C1], F32, "z_low1", "z_third0"))
-        z_share = keep([P, SHARE], F32, "z_share", "words2")
-        nc.vector.tensor_tensor(z_share[:], sums0[2][:, 0, C1 - SHARE :], gate_rows[:, C1 - SHARE : C1], ALU.mult)
-        open_window(0, 1, "wet_w2")
-        scatter_on_scalar(0, 1, z_low1[:, 0])
-        scatter_on_scalar(2, 0, z_share[:], C1 - SHARE, C1)
-        open_window(3, 1)
-        scatter_on_vector(3, 1, z_fourth1[:])
-        a_turned0 = turn_a(0, [0, 6])
-        sigmoid0 = make_sigmoid(
-            a_turned0, [keep([P, H], F32, "sigmoid0_0", "z_low0")[:], keep([P, H], F32, "sigmoid0_1")[:]]
-        )
-        place_window(1, 1, 0)
-        scatter_on_scalar(1, 1, z_low1[:, 1])
-        open_window(2, 2, "z_fourth0")
-        scatter_on_vector(2, 2, z_third2[:, 0:C2], 0, C2)
-        open_window(3, 2)
-        scatter_on_vector(3, 2, z_fourth2[:, 0:C2], 0, C2)
-        scatter_on_vector(2, 2, z_third2[:, C2:C1], C2, C1)
-        scatter_on_vector(3, 2, z_fourth2[:, C2:C1], C2, C1)
+        def load_wet_scales():
+            for r in range(SCALE_ROWS):
+                rows = wet_scales[:, 0, r : N // 32 : SCALE_ROWS, :].rearrange("e q h -> q e h")
+                nc.sync.dma_start(wet_s[r:P:QUAD, :, :].bitcast(I32), rows.bitcast(I32))
 
-        late = place([P, LATE_COLUMNS], F32, "late", LATE_AT)
-        late_rows = late[:, 0 : 3 * C1].rearrange("p (c s) -> p c s", s=C1)
-        z_third1 = empty_gated(1, third1, late_rows[:, 0:1])
-        z_low2 = empty_gated(2, low2, late_rows[:, 1:3])
-        place_window(2, 1, WINDOW_BYTES)
-        scatter_on_scalar(2, 1, z_third1[:, 0])
-        a_turned1 = turn_a(1, [7, 1])
-        z_turned0 = turn_z(0, [2, 5])
-        a_turned2 = turn_a(2, [3, 4])
-        weave_wgt(0, place(woven_shape, BF16, "woven0", WOVEN_AT))
-        inner0 = make_inner(a_turned0, sigmoid0, late[:, 3 * C1 :].rearrange("p (b i) -> p b i", b=HALVES))
-        minus_d0 = make_minus_d(0, inner0, sigmoid0)
+        load_dy()
+        nc.scalar.activation(unit[:, 1:2], unit[:, 0:1], ACT.Sigmoid)
+        load_wet_words(0)
+        load_wet_scales()
+        load_gate(0, C1)
+        nc.sync.dma_start(offs2_list[:], offs2)
+        load_a(0)
+        load_wgt(0)
+        load_gate(C1, T)
+        load_wet_words(1)
+        load_a(1)
+        load_a(2)
+        load_wet_words(2)
+        load_wgt(1)
+        load_wgt(2)
+        nc.sync.dma_start(offs_list[:], offs)
 
-        da0 = make_da(0, z_turned0, minus_d0)
-        sigmoid1 = make_sigmoid(a_turned1, both_halves("sigmoid1"))
-        sigmoid2 = make_sigmoid(a_turned2, both_halves("sigmoid2"))
-        weave_wgt(1, keep(woven_shape, BF16, "woven1", "z_low0"))
-        regroup(0, da0, 0, HALVES, 2)
-        open_window(0, 2, "da0_1")
-        scatter_on_scalar(0, 2, z_low2[:, 0])
-        inner1 = make_inner(a_turned1, sigmoid1, keep([P, HALVES, H], F32, "inner1", "minus_d0_0"))
-        z_turned1 = turn_z(1, [7, 1])
-        minus_d1 = make_minus_d(1, inner1, sigmoid1)
-        dx_sums0 = second_product(0, [5, 6])
-        open_window(1, 2, "sigmoid1")
-        scatter_on_scalar(1, 2, z_low2[:, 1])
-
-        da1 = make_da(1, z_turned1, minus_d1)
-        weave_wgt(2, place(woven_shape, BF16, "woven2", WOVEN_AT))
-        regroup(1, da1, 0, HALVES, 0)
-        dx0 = keep([P, K_TILES, C1], F32, "dx0", "da1_1")
-        for k in range(K_TILES):
-            empty_plain(dx_sums0[k][:], dx0[:, k])
-        inner2 = make_inner(a_turned2, sigmoid2, keep([P, HALVES, H], F32, "inner2", "minus_d1_0"))
-        z_turned2 = turn_z(2, [1, 3])
-        minus_d2 = make_minus_d(2, inner2, sigmoid2)
-        dx_sums1 = second_product(1, [2, 0])
-
-        out_rows = [keep([P, T], F32, "out_rows0"), keep([P, T], F32, "out_rows1", "minus_d2_0")]
-        scatter_dx_on_scalar(0, 0, dx0[:, 0])
-        da2 = make_da(2, z_turned2, minus_d2)
+        scales01 = gather_scales(0, 2 * C1)
+        words = [gather_words(g) for g in range(G)]
+        sums0 = [bank(number, [P, 1, C1], "sums0") for number in range(4)]
+        first_product(0, words[0], scales01, [sums0[c][:, 0] for c in range(I_TILES)], [0, 2, 1, 3])
+        z00 = empty_gated(0, sums0[0], "z00")
+        z_on_scalar(0, 0, z00[:, 0])
+        z20 = empty_gated(0, sums0[2], "z20")
+        z10 = empty_gated(0, sums0[1], "z10")
+        z30 = empty_gated(0, sums0[3], "z30")
+        scales2 = gather_scales(2 * C1, T, "words0")
+        z_on_vector(2, 0, z20[:, 0])
+        a_turned0 = turn_a(0, [4, 5])
+        weave_wgt(0)
+        sigmoid0 = make_sigmoid(0, a_turned0)
+        z_on_scalar(1, 0, z10[:, 0], "a_rows0")
+        inner0 = make_inner(0, a_turned0, sigmoid0)
+        rest0, d0 = turned_tile("rest0", REST0_AT), turned_tile("d0")
+        for half in range(HALVES):
+            make_rest(rest0[:, half], inner0[:, half])
+        for half in range(HALVES):
+            make_d(d0[:, half], rest0[:, half], sigmoid0[:, half])
+        low1, high1 = bank(6, [P, 2, C1], "low1"), bank(7, [P, 2, C1], "high1")
+        first_product(1, words[1], scales01[:, C1:], [low1[:, 0], low1[:, 1], high1[:, 0], high1[:, 1]], [0, 1, 2, 3])
+        z_low1 = empty_gated(1, low1, "z_low1")
+        z_high1 = empty_gated(1, high1, "z_high1")
+        z_on_vector(3, 0, z30[:, 0], "wet_w1")
+        a_turned1 = turn_a(1, [0, 1])
+        sigmoid1 = make_sigmoid(1, a_turned1)
+        z_on_scalar(0, 1, z_low1[:, 0], W01_AT)
+        z_on_scalar(1, 1, z_low1[:, 1], W11_AT)
+        a_turned2 = turn_a(2, [4, 5])
+        inner1 = make_inner(1, a_turned1, sigmoid1, INNER1_AT)
+        rest1, d1 = turned_tile("rest1"), turned_tile("d1")
+        make_rest(flat(rest1[:]), flat(inner1[:]))
+        weave_wgt(1, "inner0")
+        make_d(flat(d1[:]), flat(rest1[:]), flat(sigmoid1[:]))
+        low2, high2 = bank(2, [P, 2, C1], "low2"), bank(3, [P, 2, C1], "high2")
+        first_product(2, words[2], scales2, [low2[:, 0], low2[:, 1], high2[:, 0], high2[:, 1]], [2, 3, 0, 1])
+        z_turned0 = turn_z(0, [0, 1], [(c, half) for half in range(HALVES) for c in range(I_TILES)])
+        z_on_vector(3, 1, z_high1[:, 1], W31_AT)
+        sigmoid2 = make_sigmoid(2, a_turned2)
+        z_on_scalar(2, 1, z_high1[:, 0], W21_AT)
+        da0 = [make_da(0, half, z_turned0, d0) for half in range(HALVES)]
+        regroup(0, da0, 0, HALVES, 6)
+        z_high2 = empty_gated(2, high2, "z_high2", REST0_AT)
+        z_low2 = empty_gated(2, low2, "z_low2", REST0_AT + 2048)
+        inner2 = make_inner(2, a_turned2, sigmoid2, "sigmoid0")
+        rest2 = turned_tile("rest2")
+        make_rest(flat(rest2[:]), flat(inner2[:]))
+        z_on_scalar(0, 2, z_low2[:, 0])
+        z_on_vector(2, 2, z_high2[:, 0])
+        z_turned1 = turn_z(1, [4, 5], [(c, half) for half in range(HALVES) for c in (0, 3, 1, 2)])
+        da1 = [make_da(1, 0, z_turned1, d1)]
+        dx_sums0 = [bank(number, [P, C1], "dx_sums0") for number in (7, 2)]
+        second_product(0, [dx_sums0[k][:] for k in range(K_TILES)], [], "sigmoid1")
+        da1.append(make_da(1, 1, z_turned1, d1))
+        d2 = turned_tile("d2", "woven0")
+        make_d(flat(d2[:]), flat(rest2[:]), flat(sigmoid2[:]))
+        z_on_scalar(1, 2, z_low2[:, 1])
+        dx0 = [empty_plain(dx_sums0[0], "dx0_0")]
+        regroup(1, da1, 0, HALVES, 3)
+        z_on_vector(3, 2, z_high2[:, 1], "rest1")
+        dx0.append(empty_on_vector(dx_sums0[1], "dx0_1"))
+        dx_on_scalar(0, 0, dx0[0], "da1_1")
+        z_turned2 = turn_z(2, [5, 7], [(c, half) for c in (2, 0, 1, 3) for half in range(HALVES)])
+        dx_sums1 = [bank(number, [P, C1], "dx_sums1") for number in (0, 1)]
+        second_product(1, [dx_sums1[k][:] for k in range(K_TILES)], [])
+        weave_wgt(2, "inner0")
+        da2 = [make_da(2, half, z_turned2, d2) for half in range(HALVES)]
         dx1 = []
-        for half, number in enumerate([5, 6]):
+        for half, number in enumerate([4, 6]):
             regroup(2, da2, half, half + 1, number)
-            dx1.append(empty_plain(dx_sums1[half][:], keep([P, C1], F32, "dx1_%d" % half, "da2_%d" % half)))
-        scatter_dx_on_vector(0, 1, dx0[:, 1])
-        dx_sums2 = second_product(2, [7, 4])
-        scatter_dx_on_scalar(1, 0, dx1[0])
-        scatter_dx_on_vector(1, 1, dx1[1])
-        dx2 = [empty_plain(dx_sums2[k][:], keep([P, C1], F32, "dx2_%d" % k)) for k in range(K_TILES)]
-        scatter_dx_on_vector(2, 0, dx2[0])
-        scatter_dx_on_scalar(2, 1, dx2[1])
+            dx1.append(empty_plain(dx_sums1[half], "dx1_%d" % half, "da2_%d" % half))
+        dx_on_vector(0, 1, dx0[1], "woven0")
+        dx_sums2 = [bank(number, [P, C1], "dx_sums2") for number in (2, 3)]
+        second_product(2, [dx_sums2[k][:] for k in range(K_TILES)], [K + P])
+        dx_on_scalar(1, 0, dx1[0])
+        dx_on_vector(1, 1, dx1[1])
+        dx2 = [empty_plain(dx_sums2[k], "dx2_%d" % k) for k in range(K_TILES)]
+        dx_on_vector(2, 0, dx2[0])
+        dx_on_scalar(2, 1, dx2[1])
         for k, queue in enumerate([nc.sync, nc.scalar]):
             queue.dma_start(out[k * P : (k + 1) * P, :], out_rows[k][:])

@@ -17,15 +17,16 @@ K_TILES = K // P
 I_TILES = H // P
 HALVES = C1 // P
 
-W01_AT = 0
-A1_AT = 1024
+W30_AT = 0
+A1_AT = 2560
 W11_AT = 3072
-INNER1_AT = 6144
-A2_AT = INNER1_AT + 3584
-W31_AT = INNER1_AT + 4096
-W21_AT = W31_AT + 3072
-REST0_AT = W21_AT + 3072
-AROWS = {1: A1_AT, 2: A2_AT}
+W21_AT = 6144
+SIGMOID2_AT = 9216
+DA01_AT = SIGMOID2_AT + 3584
+W12_AT = SIGMOID2_AT + 4096
+CODES0_AT = W12_AT + 3072
+SIGMOID1_AT = CODES0_AT
+INNER2_AT = CODES0_AT + 2048
 
 F32 = mybir.dt.float32
 BF16 = mybir.dt.bfloat16
@@ -64,7 +65,8 @@ def tile_moe_hib_silu_kernel(
         wet_w = [keep([P, HALVES, 2 * H], U8, "wet_w%d" % g) for g in range(G)]
         wet_s = keep([P, E, H], U8, "wet_s")
         gate_rows = keep([P, T], F32, "gate_rows")
-        a_rows = [keep([P, I_TILES, C1], F32, "a_rows%d" % g, AROWS.get(g)) for g in range(G)]
+        gate_pairs = keep([P, G, 2], F32, "gate_pairs")
+        a_rows = [keep([P, I_TILES, C1], F32, "a_rows%d" % g, A1_AT if g == 1 else None) for g in range(G)]
         wgt_planes = [keep([P, PACK, K], F32, "wgt_planes%d" % g) for g in range(G)]
         ident = keep([P, P], F32, "ident")
 
@@ -78,12 +80,19 @@ def tile_moe_hib_silu_kernel(
             source = wet_words[g * HALVES : (g + 1) * HALVES, 0].rearrange("e p b -> p e b")
             nc.sync.dma_start(wet_w[g][:].bitcast(I32), source.bitcast(I32))
 
-        def load_gate(lo, hi):
-            nc.sync.dma_start(gate_rows[:, lo:hi], gate[:, lo:hi])
-
         def load_a(g):
             columns = a[:, g * C1 : (g + 1) * C1]
             nc.sync.dma_start(a_rows[g][:], columns.rearrange("(c p) j -> p c j", p=P))
+
+        def spread_gate(numbers):
+            spread = [bank(numbers[0], [P, 2, 2, P], "gate_low"), bank(numbers[1], [P, 1, 2, P], "gate_high")]
+            for g in range(G):
+                for u in range(2):
+                    column = gate_pairs[:, g, u : u + 1].to_broadcast([P, P])
+                    nc.tensor.transpose(spread[g // 2][:, g % 2, u, :], column, ident[:])
+            for lo, hi, part in ((0, 2, spread[0]), (2, 3, spread[1])):
+                rows = gate_rows[:, lo * C1 : hi * C1].rearrange("p (g q u) -> p g q u", q=P, u=2)
+                nc.scalar.copy(rows, part[:].rearrange("p g u q -> p g q u"))
 
         def load_wgt(g):
             nc.sync.dma_start(wgt_planes[g][:], wgt[g].rearrange("(p t) k -> p t k", t=PACK))
@@ -191,7 +200,17 @@ def tile_moe_hib_silu_kernel(
 
         def make_da(g, half, z_turned, d, on=None):
             da = keep([P, H], BF16, "da%d_%d" % (g, half), on)
-            nc.vector.tensor_tensor(da[:], z_turned[half][:], d[:, half], ALU.mult)
+            nc.vector.tensor_tensor(da[:], z_turned[half][:], d, ALU.mult)
+            return da
+
+        def make_minus_d(g, half, inner, sigmoid):
+            minus_d = keep([P, H], F32, "minus_d%d_%d" % (g, half))
+            nc.vector.scalar_tensor_tensor(minus_d[:], inner[:, half], 1.0, sigmoid[:, half], ALU.subtract, ALU.mult)
+            return minus_d
+
+        def make_da_of_minus_d(g, half, z_turned, minus_d):
+            da = keep([P, H], BF16, "da%d_%d" % (g, half))
+            nc.vector.scalar_tensor_tensor(da[:], z_turned[half][:], -1.0, minus_d[:], ALU.mult, ALU.mult)
             return da
 
         woven = {}
@@ -260,24 +279,26 @@ def tile_moe_hib_silu_kernel(
                 nc.sync.dma_start(wet_s[r:P:QUAD, :, :].bitcast(I32), rows.bitcast(I32))
 
         load_dy()
+        nc.sync.dma_start(gate_pairs[:], gate[0].rearrange("(g q u) -> q g u", q=P, u=2))
         nc.scalar.activation(unit[:, 1:2], unit[:, 0:1], ACT.Sigmoid)
         load_wet_words(0)
         load_wet_scales()
-        load_gate(0, C1)
         nc.sync.dma_start(offs2_list[:], offs2)
         load_a(0)
         load_wgt(0)
-        load_gate(C1, T)
         load_wet_words(1)
         load_a(1)
-        load_a(2)
         load_wet_words(2)
         load_wgt(1)
+        load_a(2)
         load_wgt(2)
         nc.sync.dma_start(offs_list[:], offs)
 
+        spread_gate([6, 7])
         scales01 = gather_scales(0, 2 * C1)
-        words = [gather_words(g) for g in range(G)]
+        words = [gather_words(0)]
+        scales2 = gather_scales(2 * C1, T)
+        words.extend(gather_words(g) for g in range(1, G))
         sums0 = [bank(number, [P, 1, C1], "sums0") for number in range(4)]
         first_product(0, words[0], scales01, [sums0[c][:, 0] for c in range(I_TILES)], [0, 2, 1, 3])
         z00 = empty_gated(0, sums0[0], "z00")
@@ -285,72 +306,69 @@ def tile_moe_hib_silu_kernel(
         z20 = empty_gated(0, sums0[2], "z20")
         z10 = empty_gated(0, sums0[1], "z10")
         z30 = empty_gated(0, sums0[3], "z30")
-        scales2 = gather_scales(2 * C1, T, "words0")
         z_on_vector(2, 0, z20[:, 0])
         a_turned0 = turn_a(0, [4, 5])
         weave_wgt(0)
         sigmoid0 = make_sigmoid(0, a_turned0)
         z_on_scalar(1, 0, z10[:, 0], "a_rows0")
         inner0 = make_inner(0, a_turned0, sigmoid0)
-        rest0, d0 = turned_tile("rest0", REST0_AT), turned_tile("d0")
+        rest0 = turned_tile("rest0")
+        d0 = [keep([P, H], F32, "d0_%d" % half) for half in range(HALVES)]
         for half in range(HALVES):
             make_rest(rest0[:, half], inner0[:, half])
         for half in range(HALVES):
-            make_d(d0[:, half], rest0[:, half], sigmoid0[:, half])
+            make_d(d0[half][:], rest0[:, half], sigmoid0[:, half])
         low1, high1 = bank(6, [P, 2, C1], "low1"), bank(7, [P, 2, C1], "high1")
-        first_product(1, words[1], scales01[:, C1:], [low1[:, 0], low1[:, 1], high1[:, 0], high1[:, 1]], [0, 1, 2, 3])
-        z_low1 = empty_gated(1, low1, "z_low1")
+        first_product(1, words[1], scales01[:, C1:], [low1[:, 0], low1[:, 1], high1[:, 0], high1[:, 1]], [2, 3, 0, 1])
         z_high1 = empty_gated(1, high1, "z_high1")
-        z_on_vector(3, 0, z30[:, 0], "wet_w1")
+        z_low1 = empty_gated(1, low1, "z_low1")
+        z_on_scalar(2, 1, z_high1[:, 0])
+        z_on_vector(3, 1, z_high1[:, 1])
         a_turned1 = turn_a(1, [0, 1])
-        sigmoid1 = make_sigmoid(1, a_turned1)
-        z_on_scalar(0, 1, z_low1[:, 0], W01_AT)
-        z_on_scalar(1, 1, z_low1[:, 1], W11_AT)
-        a_turned2 = turn_a(2, [4, 5])
-        inner1 = make_inner(1, a_turned1, sigmoid1, INNER1_AT)
+        z_on_vector(3, 0, z30[:, 0], W30_AT)
+        sigmoid1 = make_sigmoid(1, a_turned1, SIGMOID1_AT)
+        z_on_scalar(0, 1, z_low1[:, 0], W11_AT)
+        z_on_scalar(1, 1, z_low1[:, 1], W21_AT)
+        inner1 = make_inner(1, a_turned1, sigmoid1)
+        weave_wgt(1, "inner0")
         rest1, d1 = turned_tile("rest1"), turned_tile("d1")
         make_rest(flat(rest1[:]), flat(inner1[:]))
-        weave_wgt(1, "inner0")
         make_d(flat(d1[:]), flat(rest1[:]), flat(sigmoid1[:]))
+        weave_wgt(2, "rest1")
         low2, high2 = bank(2, [P, 2, C1], "low2"), bank(3, [P, 2, C1], "high2")
         first_product(2, words[2], scales2, [low2[:, 0], low2[:, 1], high2[:, 0], high2[:, 1]], [2, 3, 0, 1])
-        z_turned0 = turn_z(0, [0, 1], [(c, half) for half in range(HALVES) for c in range(I_TILES)])
-        z_on_vector(3, 1, z_high1[:, 1], W31_AT)
-        sigmoid2 = make_sigmoid(2, a_turned2)
-        z_on_scalar(2, 1, z_high1[:, 0], W21_AT)
-        da0 = [make_da(0, half, z_turned0, d0) for half in range(HALVES)]
-        regroup(0, da0, 0, HALVES, 6)
-        z_high2 = empty_gated(2, high2, "z_high2", REST0_AT)
-        z_low2 = empty_gated(2, low2, "z_low2", REST0_AT + 2048)
-        inner2 = make_inner(2, a_turned2, sigmoid2, "sigmoid0")
-        rest2 = turned_tile("rest2")
-        make_rest(flat(rest2[:]), flat(inner2[:]))
+        z_turned0 = turn_z(0, [4, 5], [(c, half) for half in range(HALVES) for c in (3, 0, 1, 2)])
+        a_turned2 = turn_a(2, [6, 7])
+        z_high2 = empty_gated(2, high2, "z_high2")
+        z_low2 = empty_gated(2, low2, "z_low2")
         z_on_scalar(0, 2, z_low2[:, 0])
-        z_on_vector(2, 2, z_high2[:, 0])
-        z_turned1 = turn_z(1, [4, 5], [(c, half) for half in range(HALVES) for c in (0, 3, 1, 2)])
-        da1 = [make_da(1, 0, z_turned1, d1)]
-        dx_sums0 = [bank(number, [P, C1], "dx_sums0") for number in (7, 2)]
-        second_product(0, [dx_sums0[k][:] for k in range(K_TILES)], [], "sigmoid1")
-        da1.append(make_da(1, 1, z_turned1, d1))
-        d2 = turned_tile("d2", "woven0")
-        make_d(flat(d2[:]), flat(rest2[:]), flat(sigmoid2[:]))
-        z_on_scalar(1, 2, z_low2[:, 1])
-        dx0 = [empty_plain(dx_sums0[0], "dx0_0")]
+        da0 = [make_da(0, 0, z_turned0, d0[0][:]), make_da(0, 1, z_turned0, d0[1][:], DA01_AT)]
+        regroup(0, da0, 0, HALVES, 0)
+        sigmoid2 = make_sigmoid(2, a_turned2, SIGMOID2_AT)
+        z_on_scalar(1, 2, z_low2[:, 1], W12_AT)
+        z_on_vector(2, 2, z_high2[:, 0], "d0_0")
+        z_on_vector(3, 2, z_high2[:, 1], "d0_1")
+        z_turned1 = turn_z(1, [4, 5], [(c, half) for half in range(HALVES) for c in (2, 3, 0, 1)])
+        da1 = [make_da(1, half, z_turned1, d1[:, half]) for half in range(HALVES)]
         regroup(1, da1, 0, HALVES, 3)
-        z_on_vector(3, 2, z_high2[:, 1], "rest1")
-        dx0.append(empty_on_vector(dx_sums0[1], "dx0_1"))
-        dx_on_scalar(0, 0, dx0[0], "da1_1")
-        z_turned2 = turn_z(2, [5, 7], [(c, half) for c in (2, 0, 1, 3) for half in range(HALVES)])
-        dx_sums1 = [bank(number, [P, C1], "dx_sums1") for number in (0, 1)]
+        dx_sums0 = [bank(number, [P, C1], "dx_sums0") for number in (1, 2)]
+        second_product(0, [dx_sums0[k][:] for k in range(K_TILES)], [], CODES0_AT)
+        dx0 = keep([P, K_TILES, C1], F32, "dx0", "da1_1")
+        for k in range(K_TILES):
+            nc.scalar.copy(dx0[:, k], dx_sums0[k][:])
+        dx_on_scalar(0, 0, dx0[:, 0])
+        inner2 = make_inner(2, a_turned2, sigmoid2, INNER2_AT)
+        minus_d2 = [make_minus_d(2, half, inner2, sigmoid2) for half in range(HALVES)]
+        z_turned2 = turn_z(2, [6, 7], [(c, half) for half in range(HALVES) for c in (0, 2, 3, 1)])
+        dx_sums1 = [bank(number, [P, C1], "dx_sums1") for number in (4, 5)]
         second_product(1, [dx_sums1[k][:] for k in range(K_TILES)], [])
-        weave_wgt(2, "inner0")
-        da2 = [make_da(2, half, z_turned2, d2) for half in range(HALVES)]
+        da2 = [make_da_of_minus_d(2, half, z_turned2, minus_d2[half]) for half in range(HALVES)]
         dx1 = []
-        for half, number in enumerate([4, 6]):
+        for half, number in enumerate([0, 3]):
             regroup(2, da2, half, half + 1, number)
             dx1.append(empty_plain(dx_sums1[half], "dx1_%d" % half, "da2_%d" % half))
-        dx_on_vector(0, 1, dx0[1], "woven0")
-        dx_sums2 = [bank(number, [P, C1], "dx_sums2") for number in (2, 3)]
+        dx_on_vector(0, 1, dx0[:, 1], "minus_d2_0")
+        dx_sums2 = [bank(number, [P, C1], "dx_sums2") for number in (1, 2)]
         second_product(2, [dx_sums2[k][:] for k in range(K_TILES)], [K + P])
         dx_on_scalar(1, 0, dx1[0])
         dx_on_vector(1, 1, dx1[1])

@@ -24,9 +24,11 @@ W21_AT = 6144
 SIGMOID2_AT = 9216
 DA01_AT = SIGMOID2_AT + 3584
 W12_AT = SIGMOID2_AT + 4096
-CODES0_AT = W12_AT + 3072
-SIGMOID1_AT = CODES0_AT
-INNER2_AT = CODES0_AT + 2048
+INNER2_AT = W12_AT + 3072
+OUT0_AT = INNER2_AT + 4096
+WOVEN0_AT = OUT0_AT + 2816
+DA1_AT = (WOVEN0_AT + 512, WOVEN0_AT - 512)
+WOVEN2_AT = WOVEN0_AT + 2048
 
 F32 = mybir.dt.float32
 BF16 = mybir.dt.bfloat16
@@ -51,7 +53,7 @@ def tile_moe_hib_silu_kernel(
 
         def keep(shape, dtype, name, on=None):
             if isinstance(on, int):
-                return placed.tile(shape, dtype, name=name, offset=on)
+                return placed.tile(shape, dtype, name=name, offset=on, align_bytes=64)
             return held.tile(shape, dtype, name=name, tag=on or name, align_bytes=64)
 
         def bank(number, shape, name):
@@ -124,10 +126,10 @@ def tile_moe_hib_silu_kernel(
                         stop=True,
                     )
 
-        def empty_gated(g, sums, name, on=None):
+        def empty_gated(g, sums, name, on=None, sign=1.0):
             rows = keep(list(sums.shape), F32, name, on)
             gates = gate_rows[:, g * C1 : (g + 1) * C1].unsqueeze(1).to_broadcast(list(sums.shape))
-            nc.vector.tensor_tensor(rows[:], sums[:], gates, ALU.mult)
+            nc.vector.scalar_tensor_tensor(rows[:], sums[:], sign, gates, ALU.mult, ALU.mult)
             return rows
 
         def empty_plain(sums, name, on=None):
@@ -198,9 +200,15 @@ def tile_moe_hib_silu_kernel(
         def turned_tile(name, on=None):
             return keep([P, HALVES, H], F32, name, on)
 
+        def by_pair(turned):
+            return turned.rearrange("s (p u e) -> s u p e", u=2, e=2)
+
+        def by_plane(da):
+            return da.rearrange("s (u p e) -> s u p e", u=2, e=2)
+
         def make_da(g, half, z_turned, d, on=None):
             da = keep([P, H], BF16, "da%d_%d" % (g, half), on)
-            nc.vector.tensor_tensor(da[:], z_turned[half][:], d, ALU.mult)
+            nc.vector.tensor_tensor(by_plane(da[:]), by_pair(z_turned[half][:]), by_pair(d), ALU.mult)
             return da
 
         def make_minus_d(g, half, inner, sigmoid):
@@ -208,10 +216,6 @@ def tile_moe_hib_silu_kernel(
             nc.vector.scalar_tensor_tensor(minus_d[:], inner[:, half], 1.0, sigmoid[:, half], ALU.subtract, ALU.mult)
             return minus_d
 
-        def make_da_of_minus_d(g, half, z_turned, minus_d):
-            da = keep([P, H], BF16, "da%d_%d" % (g, half))
-            nc.vector.scalar_tensor_tensor(da[:], z_turned[half][:], -1.0, minus_d[:], ALU.mult, ALU.mult)
-            return da
 
         woven = {}
 
@@ -225,13 +229,13 @@ def tile_moe_hib_silu_kernel(
             for half in range(lo, hi):
                 pairs = da[half][:].bitcast(F32)
                 for u in range(2):
-                    nc.tensor.transpose(by_word[:, half - lo, u, :], pairs[:, u : H // 2 : 2], ident[:])
+                    nc.tensor.transpose(by_word[:, half - lo, u, :], pairs[:, u * P : (u + 1) * P], ident[:])
             columns = woven[g][:, K + lo * P : K + hi * P, :].rearrange("p s t -> p (s t)").bitcast(F32)
             nc.scalar.copy(
                 columns.rearrange("p (b s u) -> p b s u", b=hi - lo, u=2), by_word[:].rearrange("p b u s -> p b s u")
             )
 
-        def second_product(g, places, cuts, on=None):
+        def quantize(g, cuts, on=None):
             codes = keep([P, K + C1], U32, "codes%d" % g, on)
             scales = keep([P, K + C1], U8, "scales%d" % g)
             for lo, hi in zip([0] + cuts, cuts + [K + C1]):
@@ -240,6 +244,10 @@ def tile_moe_hib_silu_kernel(
                     scales=scales[:, lo:hi],
                     in_=woven[g][:, lo:hi, :].rearrange("p c t -> p (c t)"),
                 )
+            return codes, scales
+
+        def second_product(quantized, places):
+            codes, scales = quantized
             for k in range(K_TILES):
                 nc.tensor.matmul_mx(
                     out=places[k],
@@ -308,7 +316,7 @@ def tile_moe_hib_silu_kernel(
         z30 = empty_gated(0, sums0[3], "z30")
         z_on_vector(2, 0, z20[:, 0])
         a_turned0 = turn_a(0, [4, 5])
-        weave_wgt(0)
+        weave_wgt(0, WOVEN0_AT)
         sigmoid0 = make_sigmoid(0, a_turned0)
         z_on_scalar(1, 0, z10[:, 0], "a_rows0")
         inner0 = make_inner(0, a_turned0, sigmoid0)
@@ -326,7 +334,7 @@ def tile_moe_hib_silu_kernel(
         z_on_vector(3, 1, z_high1[:, 1])
         a_turned1 = turn_a(1, [0, 1])
         z_on_vector(3, 0, z30[:, 0], W30_AT)
-        sigmoid1 = make_sigmoid(1, a_turned1, SIGMOID1_AT)
+        sigmoid1 = make_sigmoid(1, a_turned1, INNER2_AT)
         z_on_scalar(0, 1, z_low1[:, 0], W11_AT)
         z_on_scalar(1, 1, z_low1[:, 1], W21_AT)
         inner1 = make_inner(1, a_turned1, sigmoid1)
@@ -334,13 +342,12 @@ def tile_moe_hib_silu_kernel(
         rest1, d1 = turned_tile("rest1"), turned_tile("d1")
         make_rest(flat(rest1[:]), flat(inner1[:]))
         make_d(flat(d1[:]), flat(rest1[:]), flat(sigmoid1[:]))
-        weave_wgt(2, "rest1")
         low2, high2 = bank(2, [P, 2, C1], "low2"), bank(3, [P, 2, C1], "high2")
         first_product(2, words[2], scales2, [low2[:, 0], low2[:, 1], high2[:, 0], high2[:, 1]], [2, 3, 0, 1])
         z_turned0 = turn_z(0, [4, 5], [(c, half) for half in range(HALVES) for c in (3, 0, 1, 2)])
         a_turned2 = turn_a(2, [6, 7])
-        z_high2 = empty_gated(2, high2, "z_high2")
-        z_low2 = empty_gated(2, low2, "z_low2")
+        z_high2 = empty_gated(2, high2, "z_high2", None, -1.0)
+        z_low2 = empty_gated(2, low2, "z_low2", None, -1.0)
         z_on_scalar(0, 2, z_low2[:, 0])
         da0 = [make_da(0, 0, z_turned0, d0[0][:]), make_da(0, 1, z_turned0, d0[1][:], DA01_AT)]
         regroup(0, da0, 0, HALVES, 0)
@@ -349,29 +356,30 @@ def tile_moe_hib_silu_kernel(
         z_on_vector(2, 2, z_high2[:, 0], "d0_0")
         z_on_vector(3, 2, z_high2[:, 1], "d0_1")
         z_turned1 = turn_z(1, [4, 5], [(c, half) for half in range(HALVES) for c in (2, 3, 0, 1)])
-        da1 = [make_da(1, half, z_turned1, d1[:, half]) for half in range(HALVES)]
+        dx_sums0 = bank(1, [P, K_TILES, C1], "dx_sums0")
+        second_product(quantize(0, []), [dx_sums0[:, k] for k in range(K_TILES)])
+        weave_wgt(2, WOVEN2_AT)
+        da1 = [make_da(1, half, z_turned1, d1[:, half], DA1_AT[half]) for half in range(HALVES)]
+        dx0 = empty_plain(dx_sums0, "dx0")
         regroup(1, da1, 0, HALVES, 3)
-        dx_sums0 = [bank(number, [P, C1], "dx_sums0") for number in (1, 2)]
-        second_product(0, [dx_sums0[k][:] for k in range(K_TILES)], [], CODES0_AT)
-        dx0 = keep([P, K_TILES, C1], F32, "dx0", "da1_1")
-        for k in range(K_TILES):
-            nc.scalar.copy(dx0[:, k], dx_sums0[k][:])
-        dx_on_scalar(0, 0, dx0[:, 0])
+        dx_on_scalar(0, 0, dx0[:, 0], OUT0_AT)
         inner2 = make_inner(2, a_turned2, sigmoid2, INNER2_AT)
         minus_d2 = [make_minus_d(2, half, inner2, sigmoid2) for half in range(HALVES)]
-        z_turned2 = turn_z(2, [6, 7], [(c, half) for half in range(HALVES) for c in (0, 2, 3, 1)])
-        dx_sums1 = [bank(number, [P, C1], "dx_sums1") for number in (4, 5)]
-        second_product(1, [dx_sums1[k][:] for k in range(K_TILES)], [])
-        da2 = [make_da_of_minus_d(2, half, z_turned2, minus_d2[half]) for half in range(HALVES)]
-        dx1 = []
+        z_turned2 = turn_z(2, [5, 7], [(c, half) for half in range(HALVES) for c in (0, 2, 3, 1)])
+        dx_sums1 = [bank(number, [P, C1], "dx_sums1") for number in (4, 6)]
+        da2 = [make_da(2, half, z_turned2, minus_d2[half][:]) for half in range(HALVES)]
+        quantized1 = quantize(1, [], "minus_d2_0")
         for half, number in enumerate([0, 3]):
             regroup(2, da2, half, half + 1, number)
-            dx1.append(empty_plain(dx_sums1[half], "dx1_%d" % half, "da2_%d" % half))
-        dx_on_vector(0, 1, dx0[:, 1], "minus_d2_0")
+        second_product(quantized1, [dx_sums1[k][:] for k in range(K_TILES)])
+        dx1 = keep([P, K_TILES, C1], F32, "dx1", "da2_1")
+        for k in range(K_TILES):
+            nc.scalar.copy(dx1[:, k], dx_sums1[k][:])
+        dx_on_vector(0, 1, dx0[:, 1], "minus_d2_1")
         dx_sums2 = [bank(number, [P, C1], "dx_sums2") for number in (1, 2)]
-        second_product(2, [dx_sums2[k][:] for k in range(K_TILES)], [K + P])
-        dx_on_scalar(1, 0, dx1[0])
-        dx_on_vector(1, 1, dx1[1])
+        second_product(quantize(2, [K + P]), [dx_sums2[k][:] for k in range(K_TILES)])
+        dx_on_scalar(1, 0, dx1[:, 0])
+        dx_on_vector(1, 1, dx1[:, 1])
         dx2 = [empty_plain(dx_sums2[k], "dx2_%d" % k) for k in range(K_TILES)]
         dx_on_vector(2, 0, dx2[0])
         dx_on_scalar(2, 1, dx2[1])

@@ -29,6 +29,7 @@ OUT0_AT = INNER2_AT + 4096
 WOVEN0_AT = OUT0_AT + 2816
 DA1_AT = (WOVEN0_AT + 512, WOVEN0_AT - 512)
 WOVEN2_AT = WOVEN0_AT + 2048
+EARLY = 96
 
 F32 = mybir.dt.float32
 BF16 = mybir.dt.bfloat16
@@ -126,10 +127,10 @@ def tile_moe_hib_silu_kernel(
                         stop=True,
                     )
 
-        def empty_gated(g, sums, name, on=None, sign=1.0):
+        def empty_gated(g, sums, name, on=None, sign=1.0, lo=0, hi=C1):
             rows = keep(list(sums.shape), F32, name, on)
-            gates = gate_rows[:, g * C1 : (g + 1) * C1].unsqueeze(1).to_broadcast(list(sums.shape))
-            nc.vector.scalar_tensor_tensor(rows[:], sums[:], sign, gates, ALU.mult, ALU.mult)
+            gates = gate_rows[:, g * C1 + lo : g * C1 + hi].unsqueeze(1).to_broadcast([P, sums.shape[1], hi - lo])
+            nc.vector.scalar_tensor_tensor(rows[:, :, lo:hi], sums[:, :, lo:hi], sign, gates, ALU.mult, ALU.mult)
             return rows
 
         def empty_plain(sums, name, on=None):
@@ -144,16 +145,16 @@ def tile_moe_hib_silu_kernel(
 
         z_back = {}
 
-        def z_window(c, g, lo, hi, on):
+        def z_window(c, g, lo, hi, on, columns=T):
             if (c, g) not in z_back:
-                z_back.setdefault((c, g), keep([P, T], F32, "z_back%d_%d" % (c, g), on))
+                z_back.setdefault((c, g), keep([P, columns], F32, "z_back%d_%d" % (c, g), on))
             return z_back[c, g][:].indirect(entries(offs2_list, g * C1 + lo, g * C1 + hi))
 
         def z_on_scalar(c, g, gated, on=None, lo=0, hi=C1):
             nc.scalar.activation(z_window(c, g, lo, hi, on), gated[:, lo:hi], ACT.Copy)
 
-        def z_on_vector(c, g, gated, on=None, lo=0, hi=C1):
-            nc.vector.tensor_copy(z_window(c, g, lo, hi, on), gated[:, lo:hi])
+        def z_on_vector(c, g, gated, on=None, lo=0, hi=C1, columns=T):
+            nc.vector.tensor_copy(z_window(c, g, lo, hi, on, columns), gated[:, lo:hi])
 
         def z_gating_on_vector(c, g, sums, on=None, lo=0, hi=C1):
             gates = gate_rows[:, g * C1 + lo : g * C1 + hi]
@@ -200,15 +201,9 @@ def tile_moe_hib_silu_kernel(
         def turned_tile(name, on=None):
             return keep([P, HALVES, H], F32, name, on)
 
-        def by_pair(turned):
-            return turned.rearrange("s (p u e) -> s u p e", u=2, e=2)
-
-        def by_plane(da):
-            return da.rearrange("s (u p e) -> s u p e", u=2, e=2)
-
         def make_da(g, half, z_turned, d, on=None):
             da = keep([P, H], BF16, "da%d_%d" % (g, half), on)
-            nc.vector.tensor_tensor(by_plane(da[:]), by_pair(z_turned[half][:]), by_pair(d), ALU.mult)
+            nc.vector.tensor_tensor(da[:], z_turned[half][:], d, ALU.mult)
             return da
 
         def make_minus_d(g, half, inner, sigmoid):
@@ -229,7 +224,7 @@ def tile_moe_hib_silu_kernel(
             for half in range(lo, hi):
                 pairs = da[half][:].bitcast(F32)
                 for u in range(2):
-                    nc.tensor.transpose(by_word[:, half - lo, u, :], pairs[:, u * P : (u + 1) * P], ident[:])
+                    nc.tensor.transpose(by_word[:, half - lo, u, :], pairs[:, u : H // 2 : 2], ident[:])
             columns = woven[g][:, K + lo * P : K + hi * P, :].rearrange("p s t -> p (s t)").bitcast(F32)
             nc.scalar.copy(
                 columns.rearrange("p (b s u) -> p b s u", b=hi - lo, u=2), by_word[:].rearrange("p b u s -> p b s u")
@@ -313,27 +308,29 @@ def tile_moe_hib_silu_kernel(
         z_on_scalar(0, 0, z00[:, 0])
         z20 = empty_gated(0, sums0[2], "z20")
         z10 = empty_gated(0, sums0[1], "z10")
-        z30 = empty_gated(0, sums0[3], "z30")
+        z30 = empty_gated(0, sums0[3], "z30", None, 1.0, 0, EARLY)
         z_on_vector(2, 0, z20[:, 0])
+        z_on_vector(3, 0, z30[:, 0], None, 0, EARLY, 2 * C1)
         a_turned0 = turn_a(0, [4, 5])
         weave_wgt(0, WOVEN0_AT)
         sigmoid0 = make_sigmoid(0, a_turned0)
         z_on_scalar(1, 0, z10[:, 0], "a_rows0")
         inner0 = make_inner(0, a_turned0, sigmoid0)
         rest0 = turned_tile("rest0")
-        d0 = [keep([P, H], F32, "d0_%d" % half) for half in range(HALVES)]
+        low1, high1 = bank(6, [P, 2, C1], "low1"), bank(7, [P, 2, C1], "high1")
+        first_product(1, words[1], scales01[:, C1:], [low1[:, 0], low1[:, 1], high1[:, 0], high1[:, 1]], [2, 3, 0, 1])
+        d0 = [keep([P, H], F32, "d0_0", "words1"), keep([P, H], F32, "d0_1")]
         for half in range(HALVES):
             make_rest(rest0[:, half], inner0[:, half])
         for half in range(HALVES):
             make_d(d0[half][:], rest0[:, half], sigmoid0[:, half])
-        low1, high1 = bank(6, [P, 2, C1], "low1"), bank(7, [P, 2, C1], "high1")
-        first_product(1, words[1], scales01[:, C1:], [low1[:, 0], low1[:, 1], high1[:, 0], high1[:, 1]], [2, 3, 0, 1])
         z_high1 = empty_gated(1, high1, "z_high1")
         z_low1 = empty_gated(1, low1, "z_low1")
+        z30_late = empty_gated(0, sums0[3], "z30_late", "wet_w1", 1.0, EARLY, C1)
         z_on_scalar(2, 1, z_high1[:, 0])
         z_on_vector(3, 1, z_high1[:, 1])
+        z_on_vector(3, 0, z30_late[:, 0], None, EARLY, C1)
         a_turned1 = turn_a(1, [0, 1])
-        z_on_vector(3, 0, z30[:, 0], W30_AT)
         sigmoid1 = make_sigmoid(1, a_turned1, INNER2_AT)
         z_on_scalar(0, 1, z_low1[:, 0], W11_AT)
         z_on_scalar(1, 1, z_low1[:, 1], W21_AT)
@@ -344,19 +341,19 @@ def tile_moe_hib_silu_kernel(
         make_d(flat(d1[:]), flat(rest1[:]), flat(sigmoid1[:]))
         low2, high2 = bank(2, [P, 2, C1], "low2"), bank(3, [P, 2, C1], "high2")
         first_product(2, words[2], scales2, [low2[:, 0], low2[:, 1], high2[:, 0], high2[:, 1]], [2, 3, 0, 1])
-        z_turned0 = turn_z(0, [4, 5], [(c, half) for half in range(HALVES) for c in (3, 0, 1, 2)])
-        a_turned2 = turn_a(2, [6, 7])
-        z_high2 = empty_gated(2, high2, "z_high2", None, -1.0)
+        z_turned0 = turn_z(0, [0, 1], [(c, half) for half in range(HALVES) for c in range(I_TILES)])
+        a_turned2 = turn_a(2, [4, 5])
+        z_high2 = empty_gated(2, high2, "z_high2", "wet_w1", -1.0)
         z_low2 = empty_gated(2, low2, "z_low2", None, -1.0)
         z_on_scalar(0, 2, z_low2[:, 0])
         da0 = [make_da(0, 0, z_turned0, d0[0][:]), make_da(0, 1, z_turned0, d0[1][:], DA01_AT)]
-        regroup(0, da0, 0, HALVES, 0)
+        regroup(0, da0, 0, HALVES, 6)
         sigmoid2 = make_sigmoid(2, a_turned2, SIGMOID2_AT)
         z_on_scalar(1, 2, z_low2[:, 1], W12_AT)
-        z_on_vector(2, 2, z_high2[:, 0], "d0_0")
+        z_on_vector(2, 2, z_high2[:, 0], "words1")
         z_on_vector(3, 2, z_high2[:, 1], "d0_1")
-        z_turned1 = turn_z(1, [4, 5], [(c, half) for half in range(HALVES) for c in (2, 3, 0, 1)])
-        dx_sums0 = bank(1, [P, K_TILES, C1], "dx_sums0")
+        z_turned1 = turn_z(1, [0, 1], [(c, half) for half in range(HALVES) for c in (2, 3, 0, 1)])
+        dx_sums0 = bank(7, [P, K_TILES, C1], "dx_sums0")
         second_product(quantize(0, []), [dx_sums0[:, k] for k in range(K_TILES)])
         weave_wgt(2, WOVEN2_AT)
         da1 = [make_da(1, half, z_turned1, d1[:, half], DA1_AT[half]) for half in range(HALVES)]
@@ -365,18 +362,18 @@ def tile_moe_hib_silu_kernel(
         dx_on_scalar(0, 0, dx0[:, 0], OUT0_AT)
         inner2 = make_inner(2, a_turned2, sigmoid2, INNER2_AT)
         minus_d2 = [make_minus_d(2, half, inner2, sigmoid2) for half in range(HALVES)]
-        z_turned2 = turn_z(2, [5, 7], [(c, half) for half in range(HALVES) for c in (0, 2, 3, 1)])
-        dx_sums1 = [bank(number, [P, C1], "dx_sums1") for number in (4, 6)]
+        z_turned2 = turn_z(2, [1, 5], [(c, half) for half in range(HALVES) for c in (0, 2, 3, 1)])
+        dx_sums1 = [bank(number, [P, C1], "dx_sums1") for number in (0, 4)]
         da2 = [make_da(2, half, z_turned2, minus_d2[half][:]) for half in range(HALVES)]
         quantized1 = quantize(1, [], "minus_d2_0")
-        for half, number in enumerate([0, 3]):
+        for half, number in enumerate([6, 3]):
             regroup(2, da2, half, half + 1, number)
         second_product(quantized1, [dx_sums1[k][:] for k in range(K_TILES)])
         dx1 = keep([P, K_TILES, C1], F32, "dx1", "da2_1")
         for k in range(K_TILES):
             nc.scalar.copy(dx1[:, k], dx_sums1[k][:])
         dx_on_vector(0, 1, dx0[:, 1], "minus_d2_1")
-        dx_sums2 = [bank(number, [P, C1], "dx_sums2") for number in (1, 2)]
+        dx_sums2 = [bank(number, [P, C1], "dx_sums2") for number in (7, 2)]
         second_product(quantize(2, [K + P]), [dx_sums2[k][:] for k in range(K_TILES)])
         dx_on_scalar(1, 0, dx1[:, 0])
         dx_on_vector(1, 1, dx1[:, 1])

@@ -29,7 +29,7 @@ OUT0_AT = INNER2_AT + 4096
 WOVEN0_AT = OUT0_AT + 2816
 DA1_AT = (WOVEN0_AT + 512, WOVEN0_AT - 512)
 WOVEN2_AT = WOVEN0_AT + 2048
-EARLY = 96
+EARLY = 128
 
 F32 = mybir.dt.float32
 BF16 = mybir.dt.bfloat16
@@ -305,11 +305,11 @@ def tile_moe_hib_silu_kernel(
         sums0 = [bank(number, [P, 1, C1], "sums0") for number in range(4)]
         first_product(0, words[0], scales01, [sums0[c][:, 0] for c in range(I_TILES)], [0, 2, 1, 3])
         z00 = empty_gated(0, sums0[0], "z00")
+        z20 = empty_plain(sums0[2], "z20")
         z_on_scalar(0, 0, z00[:, 0])
-        z20 = empty_gated(0, sums0[2], "z20")
         z10 = empty_gated(0, sums0[1], "z10")
         z30 = empty_gated(0, sums0[3], "z30", None, 1.0, 0, EARLY)
-        z_on_vector(2, 0, z20[:, 0])
+        z_gating_on_vector(2, 0, z20[:, 0])
         z_on_vector(3, 0, z30[:, 0], None, 0, EARLY, 2 * C1)
         a_turned0 = turn_a(0, [4, 5])
         weave_wgt(0, WOVEN0_AT)
@@ -334,17 +334,17 @@ def tile_moe_hib_silu_kernel(
         sigmoid1 = make_sigmoid(1, a_turned1, INNER2_AT)
         z_on_scalar(0, 1, z_low1[:, 0], W11_AT)
         z_on_scalar(1, 1, z_low1[:, 1], W21_AT)
+        low2, high2 = bank(2, [P, 2, C1], "low2"), bank(3, [P, 2, C1], "high2")
+        first_product(2, words[2], scales2, [low2[:, 0], low2[:, 1], high2[:, 0], high2[:, 1]], [0, 1, 2, 3])
+        z_low2 = empty_gated(2, low2, "z_low2", None, -1.0)
         inner1 = make_inner(1, a_turned1, sigmoid1)
         weave_wgt(1, "inner0")
         rest1, d1 = turned_tile("rest1"), turned_tile("d1")
         make_rest(flat(rest1[:]), flat(inner1[:]))
         make_d(flat(d1[:]), flat(rest1[:]), flat(sigmoid1[:]))
-        low2, high2 = bank(2, [P, 2, C1], "low2"), bank(3, [P, 2, C1], "high2")
-        first_product(2, words[2], scales2, [low2[:, 0], low2[:, 1], high2[:, 0], high2[:, 1]], [2, 3, 0, 1])
-        z_turned0 = turn_z(0, [0, 1], [(c, half) for half in range(HALVES) for c in range(I_TILES)])
+        z_turned0 = turn_z(0, [0, 2], [(c, half) for half in range(HALVES) for c in range(I_TILES)])
         a_turned2 = turn_a(2, [4, 5])
         z_high2 = empty_gated(2, high2, "z_high2", "wet_w1", -1.0)
-        z_low2 = empty_gated(2, low2, "z_low2", None, -1.0)
         z_on_scalar(0, 2, z_low2[:, 0])
         da0 = [make_da(0, 0, z_turned0, d0[0][:]), make_da(0, 1, z_turned0, d0[1][:], DA01_AT)]
         regroup(0, da0, 0, HALVES, 6)
@@ -352,7 +352,7 @@ def tile_moe_hib_silu_kernel(
         z_on_scalar(1, 2, z_low2[:, 1], W12_AT)
         z_on_vector(2, 2, z_high2[:, 0], "words1")
         z_on_vector(3, 2, z_high2[:, 1], "d0_1")
-        z_turned1 = turn_z(1, [0, 1], [(c, half) for half in range(HALVES) for c in (2, 3, 0, 1)])
+        z_turned1 = turn_z(1, [0, 2], [(c, half) for half in range(HALVES) for c in (2, 3, 0, 1)])
         dx_sums0 = bank(7, [P, K_TILES, C1], "dx_sums0")
         second_product(quantize(0, []), [dx_sums0[:, k] for k in range(K_TILES)])
         weave_wgt(2, WOVEN2_AT)
@@ -362,7 +362,7 @@ def tile_moe_hib_silu_kernel(
         dx_on_scalar(0, 0, dx0[:, 0], OUT0_AT)
         inner2 = make_inner(2, a_turned2, sigmoid2, INNER2_AT)
         minus_d2 = [make_minus_d(2, half, inner2, sigmoid2) for half in range(HALVES)]
-        z_turned2 = turn_z(2, [1, 5], [(c, half) for half in range(HALVES) for c in (0, 2, 3, 1)])
+        z_turned2 = turn_z(2, [2, 5], [(c, half) for half in range(HALVES) for c in (0, 2, 3, 1)])
         dx_sums1 = [bank(number, [P, C1], "dx_sums1") for number in (0, 4)]
         da2 = [make_da(2, half, z_turned2, minus_d2[half][:]) for half in range(HALVES)]
         quantized1 = quantize(1, [], "minus_d2_0")
@@ -373,7 +373,7 @@ def tile_moe_hib_silu_kernel(
         for k in range(K_TILES):
             nc.scalar.copy(dx1[:, k], dx_sums1[k][:])
         dx_on_vector(0, 1, dx0[:, 1], "minus_d2_1")
-        dx_sums2 = [bank(number, [P, C1], "dx_sums2") for number in (7, 2)]
+        dx_sums2 = [bank(number, [P, C1], "dx_sums2") for number in (7, 1)]
         second_product(quantize(2, [K + P]), [dx_sums2[k][:] for k in range(K_TILES)])
         dx_on_scalar(1, 0, dx1[:, 0])
         dx_on_vector(1, 1, dx1[:, 1])

@@ -168,11 +168,14 @@ def tile_moe_hib_silu_kernel(
                     nc.tensor.transpose(turned[half][:, c * P : (c + 1) * P], block, ident[:])
             return turned
 
+        def turn_block(place, c, g, half):
+            block = z_back[c, g][:, g * C1 + half * P : g * C1 + (half + 1) * P]
+            nc.tensor.transpose(place, block, ident[:])
+
         def turn_z(g, numbers, blocks):
             turned = [bank(number, [P, H], "z_turned") for number in numbers]
             for c, half in blocks:
-                block = z_back[c, g][:, g * C1 + half * P : g * C1 + (half + 1) * P]
-                nc.tensor.transpose(turned[half][:, c * P : (c + 1) * P], block, ident[:])
+                turn_block(turned[half][:, c * P : (c + 1) * P], c, g, half)
             return turned
 
         def make_sigmoid(g, a_turned, on=None):
@@ -349,9 +352,9 @@ def tile_moe_hib_silu_kernel(
         da0 = [make_da(0, 0, z_turned0, d0[0][:]), make_da(0, 1, z_turned0, d0[1][:], DA01_AT)]
         regroup(0, da0, 0, HALVES, 6)
         sigmoid2 = make_sigmoid(2, a_turned2, SIGMOID2_AT)
-        z_on_scalar(1, 2, z_low2[:, 1], W12_AT)
-        z_on_vector(2, 2, z_high2[:, 0], "words1")
-        z_on_vector(3, 2, z_high2[:, 1], "d0_1")
+        z_on_scalar(3, 2, z_high2[:, 1], W12_AT)
+        z_on_vector(1, 2, z_low2[:, 1], "words1")
+        z_on_vector(2, 2, z_high2[:, 0], "d0_1")
         z_turned1 = turn_z(1, [0, 2], [(c, half) for half in range(HALVES) for c in (2, 3, 0, 1)])
         dx_sums0 = bank(7, [P, K_TILES, C1], "dx_sums0")
         second_product(quantize(0, []), [dx_sums0[:, k] for k in range(K_TILES)])
@@ -362,18 +365,29 @@ def tile_moe_hib_silu_kernel(
         dx_on_scalar(0, 0, dx0[:, 0], OUT0_AT)
         inner2 = make_inner(2, a_turned2, sigmoid2, INNER2_AT)
         minus_d2 = [make_minus_d(2, half, inner2, sigmoid2) for half in range(HALVES)]
-        z_turned2 = turn_z(2, [2, 5], [(c, half) for half in range(HALVES) for c in (0, 2, 3, 1)])
-        dx_sums1 = [bank(number, [P, C1], "dx_sums1") for number in (0, 4)]
-        da2 = [make_da(2, half, z_turned2, minus_d2[half][:]) for half in range(HALVES)]
+        early = [bank(number, [P, I_TILES - 1, P], "z_early") for number in (4, 6)]
+        late = bank(2, [P, HALVES, P], "z_late")
+        for half in (1, 0):
+            for c in range(I_TILES - 1):
+                turn_block(early[half][:, c], c, 2, half)
+        for half in range(HALVES):
+            turn_block(late[:, half], I_TILES - 1, 2, half)
+        dx_sums1 = [bank(number, [P, C1], "dx_sums1") for number in (0, 5)]
+        da2 = [keep([P, H], BF16, "da2_%d" % half) for half in range(HALVES)]
+        for half in range(HALVES):
+            cut = H - P
+            turned = early[half][:].rearrange("s c i -> s (c i)")
+            nc.vector.tensor_tensor(da2[half][:, 0:cut], turned, minus_d2[half][:, 0:cut], ALU.mult)
+            nc.vector.tensor_tensor(da2[half][:, cut:], late[:, half], minus_d2[half][:, cut:], ALU.mult)
         quantized1 = quantize(1, [], "minus_d2_0")
-        for half, number in enumerate([6, 3]):
+        for half, number in enumerate([1, 3]):
             regroup(2, da2, half, half + 1, number)
         second_product(quantized1, [dx_sums1[k][:] for k in range(K_TILES)])
         dx1 = keep([P, K_TILES, C1], F32, "dx1", "da2_1")
         for k in range(K_TILES):
             nc.scalar.copy(dx1[:, k], dx_sums1[k][:])
         dx_on_vector(0, 1, dx0[:, 1], "minus_d2_1")
-        dx_sums2 = [bank(number, [P, C1], "dx_sums2") for number in (7, 1)]
+        dx_sums2 = [bank(number, [P, C1], "dx_sums2") for number in (7, 4)]
         second_product(quantize(2, [K + P]), [dx_sums2[k][:] for k in range(K_TILES)])
         dx_on_scalar(1, 0, dx1[:, 0])
         dx_on_vector(1, 1, dx1[:, 1])

@@ -68,7 +68,6 @@ def tile_moe_hib_silu_kernel(
         wet_w = [keep([P, HALVES, 2 * H], U8, "wet_w%d" % g) for g in range(G)]
         wet_s = keep([P, E, H], U8, "wet_s")
         gate_rows = keep([P, T], F32, "gate_rows")
-        gate_pairs = keep([P, G, 2], F32, "gate_pairs")
         a_rows = [keep([P, I_TILES, C1], F32, "a_rows%d" % g, A1_AT if g == 1 else None) for g in range(G)]
         wgt_planes = [keep([P, PACK, K], F32, "wgt_planes%d" % g) for g in range(G)]
         ident = keep([P, P], F32, "ident")
@@ -87,15 +86,8 @@ def tile_moe_hib_silu_kernel(
             columns = a[:, g * C1 : (g + 1) * C1]
             nc.sync.dma_start(a_rows[g][:], columns.rearrange("(c p) j -> p c j", p=P))
 
-        def spread_gate(numbers):
-            spread = [bank(numbers[0], [P, 2, 2, P], "gate_low"), bank(numbers[1], [P, 1, 2, P], "gate_high")]
-            for g in range(G):
-                for u in range(2):
-                    column = gate_pairs[:, g, u : u + 1].to_broadcast([P, P])
-                    nc.tensor.transpose(spread[g // 2][:, g % 2, u, :], column, ident[:])
-            for lo, hi, part in ((0, 2, spread[0]), (2, 3, spread[1])):
-                rows = gate_rows[:, lo * C1 : hi * C1].rearrange("p (g q u) -> p g q u", q=P, u=2)
-                nc.scalar.copy(rows, part[:].rearrange("p g u q -> p g q u"))
+        def load_gate(lo, hi):
+            nc.sync.dma_start(gate_rows[:, lo:hi], gate[:, lo:hi])
 
         def load_wgt(g):
             nc.sync.dma_start(wgt_planes[g][:], wgt[g].rearrange("(p t) k -> p t k", t=PACK))
@@ -277,22 +269,24 @@ def tile_moe_hib_silu_kernel(
                 repeated = rows.unsqueeze(0).to_broadcast([QUAD // SCALE_ROWS, SCALE_ROWS, T // 4])
                 queue = nc.scalar if q % 2 else nc.sync
                 queue.dma_start(dy_s[QUAD * q : QUAD * (q + 1), :].bitcast(I32), repeated)
+            nc.sync.dma_start(offs2_list[:], offs2)
             nc.sync.dma_start(dy_w[:], dy_words[0].rearrange("p t d -> p (t d)").bitcast(I32))
 
-        def load_wet_scales():
+        def load_wet_scales(lo, hi):
             for r in range(SCALE_ROWS):
-                rows = wet_scales[:, 0, r : N // 32 : SCALE_ROWS, :].rearrange("e q h -> q e h")
-                nc.sync.dma_start(wet_s[r:P:QUAD, :, :].bitcast(I32), rows.bitcast(I32))
+                rows = wet_scales[lo:hi, 0, r : N // 32 : SCALE_ROWS, :].rearrange("e q h -> q e h")
+                nc.sync.dma_start(wet_s[r:P:QUAD, lo:hi, :].bitcast(I32), rows.bitcast(I32))
 
         load_dy()
-        nc.sync.dma_start(gate_pairs[:], gate[0].rearrange("(g q u) -> q g u", q=P, u=2))
         nc.scalar.activation(unit[:, 1:2], unit[:, 0:1], ACT.Sigmoid)
         load_wet_words(0)
-        load_wet_scales()
-        nc.sync.dma_start(offs2_list[:], offs2)
+        load_wet_scales(0, HALVES)
+        load_gate(0, C1)
         load_a(0)
         load_wgt(0)
         load_wet_words(1)
+        load_wet_scales(HALVES, E)
+        load_gate(C1, T)
         load_a(1)
         load_wet_words(2)
         load_wgt(1)
@@ -300,11 +294,8 @@ def tile_moe_hib_silu_kernel(
         load_wgt(2)
         nc.sync.dma_start(offs_list[:], offs)
 
-        spread_gate([6, 7])
         scales01 = gather_scales(0, 2 * C1)
-        words = [gather_words(0)]
-        scales2 = gather_scales(2 * C1, T)
-        words.extend(gather_words(g) for g in range(1, G))
+        words = [gather_words(g) for g in range(G)]
         sums0 = [bank(number, [P, 1, C1], "sums0") for number in range(4)]
         first_product(0, words[0], scales01, [sums0[c][:, 0] for c in range(I_TILES)], [0, 2, 1, 3])
         z00 = empty_gated(0, sums0[0], "z00")
@@ -312,6 +303,7 @@ def tile_moe_hib_silu_kernel(
         z_on_scalar(0, 0, z00[:, 0])
         z10 = empty_gated(0, sums0[1], "z10")
         z30 = empty_gated(0, sums0[3], "z30", None, 1.0, 0, EARLY)
+        scales2 = gather_scales(2 * C1, T, "words0")
         z_gating_on_vector(2, 0, z20[:, 0])
         z_on_vector(3, 0, z30[:, 0], None, 0, EARLY, 2 * C1)
         a_turned0 = turn_a(0, [4, 5])

@@ -29,7 +29,7 @@ OUT0_AT = INNER2_AT + 4096
 WOVEN0_AT = OUT0_AT + 2816
 DA1_AT = (WOVEN0_AT + 512, WOVEN0_AT - 512)
 WOVEN2_AT = WOVEN0_AT + 2048
-EARLY = 128
+EARLY = 96
 
 F32 = mybir.dt.float32
 BF16 = mybir.dt.bfloat16
@@ -297,9 +297,9 @@ def tile_moe_hib_silu_kernel(
         scales01 = gather_scales(0, 2 * C1)
         words = [gather_words(g) for g in range(G)]
         sums0 = [bank(number, [P, 1, C1], "sums0") for number in range(4)]
-        first_product(0, words[0], scales01, [sums0[c][:, 0] for c in range(I_TILES)], [0, 2, 1, 3])
+        first_product(0, words[0], scales01, [sums0[c][:, 0] for c in range(I_TILES)], [0, 1, 2, 3])
         z00 = empty_gated(0, sums0[0], "z00")
-        z20 = empty_plain(sums0[2], "z20")
+        z20 = empty_plain(sums0[2], "z20", WOVEN2_AT)
         z_on_scalar(0, 0, z00[:, 0])
         z10 = empty_gated(0, sums0[1], "z10")
         z30 = empty_gated(0, sums0[3], "z30", None, 1.0, 0, EARLY)

@@ -17,7 +17,6 @@ K_TILES = K // P
 I_TILES = H // P
 HALVES = C1 // P
 
-W30_AT = 0
 A1_AT = 2560
 W11_AT = 3072
 W21_AT = 6144
@@ -152,12 +151,15 @@ def tile_moe_hib_silu_kernel(
             gates = gate_rows[:, g * C1 + lo : g * C1 + hi]
             nc.vector.tensor_tensor(z_window(c, g, lo, hi, on), sums[:, lo:hi], gates, ALU.mult)
 
+        def block_of(turned, place, blocks=I_TILES):
+            return turned.rearrange("s (u b w e) -> s b w u e", u=2, b=blocks, e=2)[:, place]
+
         def turn_a(g, numbers):
             turned = [bank(number, [P, H], "a_turned") for number in numbers]
             for half in range(HALVES):
                 for c in range(I_TILES):
                     block = a_rows[g][:, c, half * P : (half + 1) * P]
-                    nc.tensor.transpose(turned[half][:, c * P : (c + 1) * P], block, ident[:])
+                    nc.tensor.transpose(block_of(turned[half][:], c), block, ident[:])
             return turned
 
         def turn_block(place, c, g, half):
@@ -167,7 +169,7 @@ def tile_moe_hib_silu_kernel(
         def turn_z(g, numbers, blocks):
             turned = [bank(number, [P, H], "z_turned") for number in numbers]
             for c, half in blocks:
-                turn_block(turned[half][:, c * P : (c + 1) * P], c, g, half)
+                turn_block(block_of(turned[half][:], c), c, g, half)
             return turned
 
         def make_sigmoid(g, a_turned, on=None):
@@ -214,12 +216,12 @@ def tile_moe_hib_silu_kernel(
             planes = wgt_planes[g][:].rearrange("p t k -> p k t")
             nc.gpsimd.tensor_scalar(woven[g][:, 0:K, :], planes, 1.0, 0.0, ALU.mult, ALU.add)
 
-        def regroup(g, da, lo, hi, number):
+        def regroup(g, da, lo, hi, number, step=1):
             by_word = bank(number, [P, hi - lo, 2, P], "by_word")
-            for half in range(lo, hi):
+            for half in range(lo, hi)[::step]:
                 pairs = da[half][:].bitcast(F32)
                 for u in range(2):
-                    nc.tensor.transpose(by_word[:, half - lo, u, :], pairs[:, u : H // 2 : 2], ident[:])
+                    nc.tensor.transpose(by_word[:, half - lo, u, :], pairs[:, u * P : (u + 1) * P], ident[:])
             columns = woven[g][:, K + lo * P : K + hi * P, :].rearrange("p s t -> p (s t)").bitcast(F32)
             nc.scalar.copy(
                 columns.rearrange("p (b s u) -> p b s u", b=hi - lo, u=2), by_word[:].rearrange("p b u s -> p b s u")
@@ -329,24 +331,26 @@ def tile_moe_hib_silu_kernel(
         sigmoid1 = make_sigmoid(1, a_turned1, INNER2_AT)
         z_on_scalar(0, 1, z_low1[:, 0], W11_AT)
         z_on_scalar(1, 1, z_low1[:, 1], W21_AT)
-        low2, high2 = bank(2, [P, 2, C1], "low2"), bank(3, [P, 2, C1], "high2")
-        first_product(2, words[2], scales2, [low2[:, 0], low2[:, 1], high2[:, 0], high2[:, 1]], [0, 1, 2, 3])
-        z_low2 = empty_gated(2, low2, "z_low2", None, -1.0)
+        sums12, high2, sums02 = bank(2, [P, 1, C1], "sums12"), bank(3, [P, 2, C1], "high2"), bank(7, [P, 1, C1], "sums02")
+        first_product(2, words[2], scales2, [sums02[:, 0], sums12[:, 0], high2[:, 0], high2[:, 1]], [1, 2, 3, 0])
+        z12 = empty_gated(2, sums12, "z12", None, -1.0)
         inner1 = make_inner(1, a_turned1, sigmoid1)
         weave_wgt(1, "inner0")
         rest1, d1 = turned_tile("rest1"), turned_tile("d1")
         make_rest(flat(rest1[:]), flat(inner1[:]))
         make_d(flat(d1[:]), flat(rest1[:]), flat(sigmoid1[:]))
-        z_turned0 = turn_z(0, [0, 2], [(c, half) for half in range(HALVES) for c in range(I_TILES)])
+        z_turned0 = turn_z(0, [0, 2], [(c, half) for half in (1, 0) for c in range(I_TILES)])
         a_turned2 = turn_a(2, [4, 5])
         z_high2 = empty_gated(2, high2, "z_high2", "wet_w1", -1.0)
-        z_on_scalar(0, 2, z_low2[:, 0])
-        da0 = [make_da(0, 0, z_turned0, d0[0][:]), make_da(0, 1, z_turned0, d0[1][:], DA01_AT)]
-        regroup(0, da0, 0, HALVES, 6)
+        da01 = make_da(0, 1, z_turned0, d0[1][:])
+        da0 = [make_da(0, 0, z_turned0, d0[0][:], DA01_AT), da01]
+        regroup(0, da0, 0, HALVES, 6, -1)
         sigmoid2 = make_sigmoid(2, a_turned2, SIGMOID2_AT)
         z_on_scalar(3, 2, z_high2[:, 1], W12_AT)
-        z_on_vector(1, 2, z_low2[:, 1], "words1")
-        z_on_vector(2, 2, z_high2[:, 0], "d0_1")
+        z_on_vector(1, 2, z12[:, 0], "d0_1")
+        z_on_vector(2, 2, z_high2[:, 0], "words1")
+        z02 = empty_gated(2, sums02, "z02", "z12", -1.0)
+        z_on_scalar(0, 2, z02[:, 0])
         z_turned1 = turn_z(1, [0, 2], [(c, half) for half in range(HALVES) for c in (2, 3, 0, 1)])
         dx_sums0 = bank(7, [P, K_TILES, C1], "dx_sums0")
         second_product(quantize(0, []), [dx_sums0[:, k] for k in range(K_TILES)])
@@ -357,20 +361,20 @@ def tile_moe_hib_silu_kernel(
         dx_on_scalar(0, 0, dx0[:, 0], OUT0_AT)
         inner2 = make_inner(2, a_turned2, sigmoid2, INNER2_AT)
         minus_d2 = [make_minus_d(2, half, inner2, sigmoid2) for half in range(HALVES)]
-        early = [bank(number, [P, I_TILES - 1, P], "z_early") for number in (4, 6)]
+        early = [bank(number, [P, H - P], "z_early") for number in (4, 6)]
         late = bank(2, [P, HALVES, P], "z_late")
         for half in (1, 0):
-            for c in range(I_TILES - 1):
-                turn_block(early[half][:, c], c, 2, half)
+            for c in (1, 2, 3):
+                turn_block(block_of(early[half][:], c - 1, I_TILES - 1), c, 2, half)
         for half in range(HALVES):
-            turn_block(late[:, half], I_TILES - 1, 2, half)
+            turn_block(block_of(late[:, half], 0, 1), 0, 2, half)
         dx_sums1 = [bank(number, [P, C1], "dx_sums1") for number in (0, 5)]
         da2 = [keep([P, H], BF16, "da2_%d" % half) for half in range(HALVES)]
         for half in range(HALVES):
-            cut = H - P
-            turned = early[half][:].rearrange("s c i -> s (c i)")
-            nc.vector.tensor_tensor(da2[half][:, 0:cut], turned, minus_d2[half][:, 0:cut], ALU.mult)
-            nc.vector.tensor_tensor(da2[half][:, cut:], late[:, half], minus_d2[half][:, cut:], ALU.mult)
+            product, factor = [tile[:].rearrange("s (u i) -> s u i", u=2) for tile in (da2[half], minus_d2[half])]
+            cut = P // 2
+            nc.vector.tensor_tensor(product[:, :, cut:], early[half][:].rearrange("s (u i) -> s u i", u=2), factor[:, :, cut:], ALU.mult)
+            nc.vector.tensor_tensor(product[:, :, 0:cut], late[:, half].rearrange("s (u i) -> s u i", u=2), factor[:, :, 0:cut], ALU.mult)
         quantized1 = quantize(1, [], "minus_d2_0")
         for half, number in enumerate([1, 3]):
             regroup(2, da2, half, half + 1, number)

@@ -29,6 +29,8 @@ WOVEN0_AT = OUT0_AT + 2816
 DA1_AT = (WOVEN0_AT + 512, WOVEN0_AT - 512)
 WOVEN2_AT = WOVEN0_AT + 2048
 EARLY = 96
+DX_KEPT = 224
+Z_KEPT = 192
 
 F32 = mybir.dt.float32
 BF16 = mybir.dt.bfloat16
@@ -127,11 +129,6 @@ def tile_moe_hib_silu_kernel(
         def empty_plain(sums, name, on=None):
             rows = keep(list(sums.shape), F32, name, on)
             nc.scalar.copy(rows[:], sums[:])
-            return rows
-
-        def empty_on_vector(sums, name, on=None):
-            rows = keep(list(sums.shape), F32, name, on)
-            nc.vector.tensor_copy(rows[:], sums[:])
             return rows
 
         z_back = {}
@@ -325,7 +322,8 @@ def tile_moe_hib_silu_kernel(
         z_low1 = empty_gated(1, low1, "z_low1")
         z30_late = empty_gated(0, sums0[3], "z30_late", "wet_w1", 1.0, EARLY, C1)
         z_on_scalar(2, 1, z_high1[:, 0])
-        z_on_vector(3, 1, z_high1[:, 1])
+        z_on_vector(3, 1, z_high1[:, 1], None, 0, Z_KEPT, 2 * C1)
+        z_on_scalar(3, 1, z_high1[:, 1], None, Z_KEPT, C1)
         z_on_vector(3, 0, z30_late[:, 0], None, EARLY, C1)
         a_turned1 = turn_a(1, [0, 1])
         sigmoid1 = make_sigmoid(1, a_turned1, INNER2_AT)
@@ -379,16 +377,17 @@ def tile_moe_hib_silu_kernel(
         for half, number in enumerate([1, 3]):
             regroup(2, da2, half, half + 1, number)
         second_product(quantized1, [dx_sums1[k][:] for k in range(K_TILES)])
-        dx1 = keep([P, K_TILES, C1], F32, "dx1", "da2_1")
+        dx1 = keep([P, 3 * C1], F32, "dx1", "da2_1")
         for k in range(K_TILES):
-            nc.scalar.copy(dx1[:, k], dx_sums1[k][:])
+            nc.scalar.copy(dx1[:, k * C1 : (k + 1) * C1], dx_sums1[k][:])
         dx_on_vector(0, 1, dx0[:, 1], "minus_d2_1")
         dx_sums2 = [bank(number, [P, C1], "dx_sums2") for number in (7, 4)]
         second_product(quantize(2, [K + P]), [dx_sums2[k][:] for k in range(K_TILES)])
-        dx_on_scalar(1, 0, dx1[:, 0])
-        dx_on_vector(1, 1, dx1[:, 1])
-        dx2 = [empty_plain(dx_sums2[k], "dx2_%d" % k) for k in range(K_TILES)]
-        dx_on_vector(2, 0, dx2[0])
-        dx_on_scalar(2, 1, dx2[1])
+        dx_on_scalar(1, 0, dx1)
+        dx_on_vector(1, 1, dx1[:, C1:], None, 0, DX_KEPT)
+        dx2 = empty_plain(dx_sums2[0], "dx2")
+        nc.scalar.copy(dx1[:, 2 * C1 :], dx_sums2[1][:])
+        dx_on_vector(2, 0, dx2)
+        dx_on_scalar(1, 1, dx1[:, C1:], None, DX_KEPT, 2 * C1)
         for k, queue in enumerate([nc.sync, nc.scalar]):
             queue.dma_start(out[k * P : (k + 1) * P, :], out_rows[k][:])

from contextlib import ExitStack

import concourse.mybir as mybir
from concourse.masks import make_identity

K, T, H, N = 256, 768, 512, 512
G, C1 = 3, 256
E, C2 = 6, 128
FLOPS = 2 * T * N * H + 2 * T * H * K

P = 128
PACK = 4
QUAD = 32
SCALE_ROWS = 4
PER_COL = 16
K_TILES = K // P
I_TILES = H // P
HALVES = C1 // P

A1_AT = 2560
W11_AT = 3072
W21_AT = 6144
SIGMOID2_AT = 9216
DA01_AT = SIGMOID2_AT + 3584
W12_AT = SIGMOID2_AT + 4096
INNER2_AT = W12_AT + 3072
OUT0_AT = INNER2_AT + 4096
WOVEN0_AT = OUT0_AT + 2816
DA1_AT = (WOVEN0_AT + 512, WOVEN0_AT - 512)
WOVEN2_AT = WOVEN0_AT + 2048
EARLY = 96
DX_KEPT = 224
Z_KEPT = 192

F32 = mybir.dt.float32
BF16 = mybir.dt.bfloat16
I32 = mybir.dt.int32
U32 = mybir.dt.uint32
U16 = mybir.dt.uint16
U8 = mybir.dt.uint8
FP8X4 = mybir.dt.float8_e4m3fn_x4
FP4X4 = mybir.dt.float4_e2m1fn_x4
ACT = mybir.ActivationFunctionType
ALU = mybir.AluOpType


def tile_moe_hib_silu_kernel(
    tc, dy_words, dy_scales, wet_words, wet_scales, wgt, a, gate, offs, offs2, dst, out
):
    nc = tc.nc
    with ExitStack() as ctx:
        held = ctx.enter_context(tc.tile_pool(name="held", bufs=1))
        placed = ctx.enter_context(tc.tile_pool(name="placed", bufs=1))
        psum = ctx.enter_context(tc.psum_pool(name="psum", bufs=1))

        def keep(shape, dtype, name, on=None):
            if isinstance(on, int):
                return placed.tile(shape, dtype, name=name, offset=on, align_bytes=64)
            return held.tile(shape, dtype, name=name, tag=on or name, align_bytes=64)

        def bank(number, shape, name):
            return psum.tile(shape, F32, name=name, tag="bank%d" % number)

        dst_list = held.tile([P, T // PER_COL], U16, name="dst_list")
        offs2_list = held.tile([P, T // PER_COL], U16, name="offs2_list")
        offs_list = held.tile([P, T // PER_COL], U16, name="offs_list")
        dy_w = keep([P, T], I32, "dy_w")
        dy_s = keep([P, T], U8, "dy_s")
        wet_w = [keep([P, HALVES, 2 * H], U8, "wet_w%d" % g) for g in range(G)]
        wet_s = keep([P, E, H], U8, "wet_s")
        gate_rows = keep([P, T], F32, "gate_rows")
        a_rows = [keep([P, I_TILES, C1], F32, "a_rows%d" % g, A1_AT if g == 1 else None) for g in range(G)]
        wgt_planes = [keep([P, PACK, K], F32, "wgt_planes%d" % g) for g in range(G)]
        ident = keep([P, P], F32, "ident")

        nc.vector.memset(wet_s[:].rearrange("p e h -> p (e h)").bitcast(I32), 0)
        unit = held.tile([P, 2], F32, name="unit")
        nc.vector.memset(unit[:, 0:1], 64.0)
        one = unit[:, 1:2]
        make_identity(nc, ident[:])

        def load_wet_words(g):
            source = wet_words[g * HALVES : (g + 1) * HALVES, 0].rearrange("e p b -> p e b")
            nc.sync.dma_start(wet_w[g][:].bitcast(I32), source.bitcast(I32))

        def load_a(g):
            columns = a[:, g * C1 : (g + 1) * C1]
            nc.sync.dma_start(a_rows[g][:], columns.rearrange("(c p) j -> p c j", p=P))

        def load_gate(lo, hi):
            nc.sync.dma_start(gate_rows[:, lo:hi], gate[:, lo:hi])

        def load_wgt(g):
            nc.sync.dma_start(wgt_planes[g][:], wgt[g].rearrange("(p t) k -> p t k", t=PACK))

        def entries(list_tile, lo, hi):
            return list_tile[:, lo // PER_COL : hi // PER_COL]

        def gather_scales(lo, hi, on=None):
            gathered = keep([P, hi - lo], U8, "scale_bytes%d" % lo, on)
            nc.vector.tensor_copy(gathered[:], dy_s[:].indirect(entries(dst_list, lo, hi)))
            return gathered

        def gather_words(g, on=None):
            gathered = keep([P, C1], U32, "words%d" % g, on)
            nc.vector.tensor_copy(gathered[:], dy_w[:].bitcast(U32).indirect(entries(dst_list, g * C1, (g + 1) * C1)))
            return gathered

        def first_product(g, words, scale_bytes, places, tiles):
            for c in tiles:
                for half in range(HALVES):
                    e = g * HALVES + half
                    nc.tensor.matmul_mx(
                        out=places[c][:, half * C2 : (half + 1) * C2],
                        lhsT=wet_w[g][:, half, 2 * P * c : 2 * P * (c + 1)].bitcast(FP4X4),
                        lhsT_scale=wet_s[:, e, P * c : P * (c + 1)],
                        rhs=words[:, half * C2 : (half + 1) * C2].bitcast(FP8X4),
                        rhs_scale=scale_bytes[:, half * C2 : (half + 1) * C2],
                        start=True,
                        stop=True,
                    )

        def empty_gated(g, sums, name, on=None, sign=1.0, lo=0, hi=C1):
            rows = keep(list(sums.shape), F32, name, on)
            gates = gate_rows[:, g * C1 + lo : g * C1 + hi].unsqueeze(1).to_broadcast([P, sums.shape[1], hi - lo])
            nc.vector.scalar_tensor_tensor(rows[:, :, lo:hi], sums[:, :, lo:hi], sign, gates, ALU.mult, ALU.mult)
            return rows

        def empty_plain(sums, name, on=None):
            rows = keep(list(sums.shape), F32, name, on)
            nc.scalar.copy(rows[:], sums[:])
            return rows

        z_back = {}

        def z_window(c, g, lo, hi, on, columns=T):
            if (c, g) not in z_back:
                z_back.setdefault((c, g), keep([P, columns], F32, "z_back%d_%d" % (c, g), on))
            return z_back[c, g][:].indirect(entries(offs2_list, g * C1 + lo, g * C1 + hi))

        def z_on_scalar(c, g, gated, on=None, lo=0, hi=C1):
            nc.scalar.activation(z_window(c, g, lo, hi, on), gated[:, lo:hi], ACT.Copy)

        def z_on_vector(c, g, gated, on=None, lo=0, hi=C1, columns=T):
            nc.vector.tensor_copy(z_window(c, g, lo, hi, on, columns), gated[:, lo:hi])

        def z_gating_on_vector(c, g, sums, on=None, lo=0, hi=C1):
            gates = gate_rows[:, g * C1 + lo : g * C1 + hi]
            nc.vector.tensor_tensor(z_window(c, g, lo, hi, on), sums[:, lo:hi], gates, ALU.mult)

        def block_of(turned, place, blocks=I_TILES):
            return turned.rearrange("s (u b w e) -> s b w u e", u=2, b=blocks, e=2)[:, place]

        def turn_a(g, numbers):
            turned = [bank(number, [P, H], "a_turned") for number in numbers]
            for half in range(HALVES):
                for c in range(I_TILES):
                    block = a_rows[g][:, c, half * P : (half + 1) * P]
                    nc.tensor.transpose(block_of(turned[half][:], c), block, ident[:])
            return turned

        def turn_block(place, c, g, half):
            block = z_back[c, g][:, g * C1 + half * P : g * C1 + (half + 1) * P]
            nc.tensor.transpose(place, block, ident[:])

        def turn_z(g, numbers, blocks):
            turned = [bank(number, [P, H], "z_turned") for number in numbers]
            for c, half in blocks:
                turn_block(block_of(turned[half][:], c), c, g, half)
            return turned

        def make_sigmoid(g, a_turned, on=None):
            sigmoid = keep([P, HALVES, H], F32, "sigmoid%d" % g, on)
            for half in range(HALVES):
                nc.scalar.activation(sigmoid[:, half], a_turned[half][:], ACT.Sigmoid, scale=one)
            return sigmoid

        def make_inner(g, a_turned, sigmoid, on=None):
            inner = keep([P, HALVES, H], F32, "inner%d" % g, on)
            for half in range(HALVES):
                nc.vector.scalar_tensor_tensor(
                    inner[:, half], sigmoid[:, half], 1.0, a_turned[half][:], ALU.subtract, ALU.mult
                )
            return inner

        def flat(tile):
            return tile.rearrange("p b i -> p (b i)")

        def make_rest(rest, inner):
            nc.gpsimd.tensor_scalar(rest, inner, -1.0, 1.0, ALU.mult, ALU.add)

        def make_d(d, rest, sigmoid):
            nc.gpsimd.tensor_tensor(d, rest, sigmoid, ALU.mult)

        def turned_tile(name, on=None):
            return keep([P, HALVES, H], F32, name, on)

        def make_da(g, half, z_turned, d, on=None):
            da = keep([P, H], BF16, "da%d_%d" % (g, half), on)
            nc.vector.tensor_tensor(da[:], z_turned[half][:], d, ALU.mult)
            return da

        def make_minus_d(g, half, inner, sigmoid):
            minus_d = keep([P, H], F32, "minus_d%d_%d" % (g, half))
            nc.vector.scalar_tensor_tensor(minus_d[:], inner[:, half], 1.0, sigmoid[:, half], ALU.subtract, ALU.mult)
            return minus_d


        woven = {}

        def weave_wgt(g, on=None):
            woven.setdefault(g, keep([P, K + C1, PACK], BF16, "woven%d" % g, on))
            planes = wgt_planes[g][:].rearrange("p t k -> p k t")
            nc.gpsimd.tensor_scalar(woven[g][:, 0:K, :], planes, 1.0, 0.0, ALU.mult, ALU.add)

        def regroup(g, da, lo, hi, number, step=1):
            by_word = bank(number, [P, hi - lo, 2, P], "by_word")
            for half in range(lo, hi)[::step]:
                pairs = da[half][:].bitcast(F32)
                for u in range(2):
                    nc.tensor.transpose(by_word[:, half - lo, u, :], pairs[:, u * P : (u + 1) * P], ident[:])
            columns = woven[g][:, K + lo * P : K + hi * P, :].rearrange("p s t -> p (s t)").bitcast(F32)
            nc.scalar.copy(
                columns.rearrange("p (b s u) -> p b s u", b=hi - lo, u=2), by_word[:].rearrange("p b u s -> p b s u")
            )

        def quantize(g, cuts, on=None):
            codes = keep([P, K + C1], U32, "codes%d" % g, on)
            scales = keep([P, K + C1], U8, "scales%d" % g)
            for lo, hi in zip([0] + cuts, cuts + [K + C1]):
                nc.vector.quantize_mx(
                    out=codes[:, lo:hi].bitcast(FP8X4),
                    scales=scales[:, lo:hi],
                    in_=woven[g][:, lo:hi, :].rearrange("p c t -> p (c t)"),
                )
            return codes, scales

        def second_product(quantized, places):
            codes, scales = quantized
            for k in range(K_TILES):
                nc.tensor.matmul_mx(
                    out=places[k],
                    lhsT=codes[:, k * P : (k + 1) * P].bitcast(FP8X4),
                    lhsT_scale=scales[:, k * P : (k + 1) * P],
                    rhs=codes[:, K:].bitcast(FP8X4),
                    rhs_scale=scales[:, K:],
                    start=True,
                    stop=True,
                )

        out_rows = {}

        def dx_window(g, k, lo, hi, on):
            if k not in out_rows:
                out_rows.setdefault(k, keep([P, T], F32, "out_rows%d" % k, on))
            return out_rows[k][:].indirect(entries(offs_list, g * C1 + lo, g * C1 + hi))

        def dx_on_scalar(g, k, rows, on=None, lo=0, hi=C1):
            nc.scalar.activation(dx_window(g, k, lo, hi, on), rows[:, lo:hi], ACT.Copy)

        def dx_on_vector(g, k, rows, on=None, lo=0, hi=C1):
            nc.vector.tensor_copy(dx_window(g, k, lo, hi, on), rows[:, lo:hi])

        def load_dy():
            nc.sync.dma_start(dst_list[:], dst)
            for q in range(P // QUAD):
                rows = dy_scales[0, SCALE_ROWS * q : SCALE_ROWS * (q + 1), :].bitcast(I32)
                repeated = rows.unsqueeze(0).to_broadcast([QUAD // SCALE_ROWS, SCALE_ROWS, T // 4])
                queue = nc.scalar if q % 2 else nc.sync
                queue.dma_start(dy_s[QUAD * q : QUAD * (q + 1), :].bitcast(I32), repeated)
            nc.sync.dma_start(offs2_list[:], offs2)
            nc.sync.dma_start(dy_w[:], dy_words[0].rearrange("p t d -> p (t d)").bitcast(I32))

        def load_wet_scales(lo, hi):
            for r in range(SCALE_ROWS):
                rows = wet_scales[lo:hi, 0, r : N // 32 : SCALE_ROWS, :].rearrange("e q h -> q e h")
                nc.sync.dma_start(wet_s[r:P:QUAD, lo:hi, :].bitcast(I32), rows.bitcast(I32))

        load_dy()
        nc.scalar.activation(unit[:, 1:2], unit[:, 0:1], ACT.Sigmoid)
        load_wet_words(0)
        load_wet_scales(0, HALVES)
        load_gate(0, C1)
        load_a(0)
        load_wgt(0)
        load_wet_words(1)
        load_wet_scales(HALVES, E)
        load_gate(C1, T)
        load_a(1)
        load_wet_words(2)
        load_wgt(1)
        load_a(2)
        load_wgt(2)
        nc.sync.dma_start(offs_list[:], offs)

        scales01 = gather_scales(0, 2 * C1)
        words = [gather_words(g) for g in range(G)]
        sums0 = [bank(number, [P, 1, C1], "sums0") for number in range(4)]
        first_product(0, words[0], scales01, [sums0[c][:, 0] for c in range(I_TILES)], [0, 1, 2, 3])
        z00 = empty_gated(0, sums0[0], "z00")
        z20 = empty_plain(sums0[2], "z20", WOVEN2_AT)
        z_on_scalar(0, 0, z00[:, 0])
        z10 = empty_gated(0, sums0[1], "z10")
        z30 = empty_gated(0, sums0[3], "z30", None, 1.0, 0, EARLY)
        scales2 = gather_scales(2 * C1, T, "words0")
        z_gating_on_vector(2, 0, z20[:, 0])
        z_on_vector(3, 0, z30[:, 0], None, 0, EARLY, 2 * C1)
        a_turned0 = turn_a(0, [4, 5])
        weave_wgt(0, WOVEN0_AT)
        sigmoid0 = make_sigmoid(0, a_turned0)
        z_on_scalar(1, 0, z10[:, 0], "a_rows0")
        inner0 = make_inner(0, a_turned0, sigmoid0)
        rest0 = turned_tile("rest0")
        low1, high1 = bank(6, [P, 2, C1], "low1"), bank(7, [P, 2, C1], "high1")
        first_product(1, words[1], scales01[:, C1:], [low1[:, 0], low1[:, 1], high1[:, 0], high1[:, 1]], [2, 3, 0, 1])
        d0 = [keep([P, H], F32, "d0_0", "words1"), keep([P, H], F32, "d0_1")]
        for half in range(HALVES):
            make_rest(rest0[:, half], inner0[:, half])
        for half in range(HALVES):
            make_d(d0[half][:], rest0[:, half], sigmoid0[:, half])
        z_high1 = empty_gated(1, high1, "z_high1")
        z_low1 = empty_gated(1, low1, "z_low1")
        z30_late = empty_gated(0, sums0[3], "z30_late", "wet_w1", 1.0, EARLY, C1)
        z_on_scalar(2, 1, z_high1[:, 0])
        z_on_vector(3, 1, z_high1[:, 1], None, 0, Z_KEPT, 2 * C1)
        z_on_scalar(3, 1, z_high1[:, 1], None, Z_KEPT, C1)
        z_on_vector(3, 0, z30_late[:, 0], None, EARLY, C1)
        a_turned1 = turn_a(1, [0, 1])
        sigmoid1 = make_sigmoid(1, a_turned1, INNER2_AT)
        z_on_scalar(0, 1, z_low1[:, 0], W11_AT)
        z_on_scalar(1, 1, z_low1[:, 1], W21_AT)
        sums12, high2, sums02 = bank(2, [P, 1, C1], "sums12"), bank(3, [P, 2, C1], "high2"), bank(7, [P, 1, C1], "sums02")
        first_product(2, words[2], scales2, [sums02[:, 0], sums12[:, 0], high2[:, 0], high2[:, 1]], [1, 2, 3, 0])
        z12 = empty_gated(2, sums12, "z12", None, -1.0)
        inner1 = make_inner(1, a_turned1, sigmoid1)
        weave_wgt(1, "inner0")
        rest1, d1 = turned_tile("rest1"), turned_tile("d1")
        make_rest(flat(rest1[:]), flat(inner1[:]))
        make_d(flat(d1[:]), flat(rest1[:]), flat(sigmoid1[:]))
        z_turned0 = turn_z(0, [0, 2], [(c, half) for half in (1, 0) for c in range(I_TILES)])
        a_turned2 = turn_a(2, [4, 5])
        z_high2 = empty_gated(2, high2, "z_high2", "wet_w1", -1.0)
        da01 = make_da(0, 1, z_turned0, d0[1][:])
        da0 = [make_da(0, 0, z_turned0, d0[0][:], DA01_AT), da01]
        regroup(0, da0, 0, HALVES, 6, -1)
        sigmoid2 = make_sigmoid(2, a_turned2, SIGMOID2_AT)
        z_on_scalar(3, 2, z_high2[:, 1], W12_AT)
        z_on_vector(1, 2, z12[:, 0], "d0_1")
        z_on_vector(2, 2, z_high2[:, 0], "words1")
        z02 = empty_gated(2, sums02, "z02", "z12", -1.0)
        z_on_scalar(0, 2, z02[:, 0])
        z_turned1 = turn_z(1, [0, 2], [(c, half) for half in range(HALVES) for c in (2, 3, 0, 1)])
        dx_sums0 = bank(7, [P, K_TILES, C1], "dx_sums0")
        second_product(quantize(0, []), [dx_sums0[:, k] for k in range(K_TILES)])
        weave_wgt(2, WOVEN2_AT)
        da1 = [make_da(1, half, z_turned1, d1[:, half], DA1_AT[half]) for half in range(HALVES)]
        dx0 = empty_plain(dx_sums0, "dx0")
        regroup(1, da1, 0, HALVES, 3)
        dx_on_scalar(0, 0, dx0[:, 0], OUT0_AT)
        inner2 = make_inner(2, a_turned2, sigmoid2, INNER2_AT)
        minus_d2 = [make_minus_d(2, half, inner2, sigmoid2) for half in range(HALVES)]
        early = [bank(number, [P, H - P], "z_early") for number in (4, 6)]
        late = bank(2, [P, HALVES, P], "z_late")
        for half in (1, 0):
            for c in (1, 2, 3):
                turn_block(block_of(early[half][:], c - 1, I_TILES - 1), c, 2, half)
        for half in range(HALVES):
            turn_block(block_of(late[:, half], 0, 1), 0, 2, half)
        dx_sums1 = [bank(number, [P, C1], "dx_sums1") for number in (0, 5)]
        da2 = [keep([P, H], BF16, "da2_%d" % half) for half in range(HALVES)]
        for half in range(HALVES):
            product, factor = [tile[:].rearrange("s (u i) -> s u i", u=2) for tile in (da2[half], minus_d2[half])]
            cut = P // 2
            nc.vector.tensor_tensor(product[:, :, cut:], early[half][:].rearrange("s (u i) -> s u i", u=2), factor[:, :, cut:], ALU.mult)
            nc.vector.tensor_tensor(product[:, :, 0:cut], late[:, half].rearrange("s (u i) -> s u i", u=2), factor[:, :, 0:cut], ALU.mult)
        quantized1 = quantize(1, [], "minus_d2_0")
        for half, number in enumerate([1, 3]):
            regroup(2, da2, half, half + 1, number)
        second_product(quantized1, [dx_sums1[k][:] for k in range(K_TILES)])
        dx1 = keep([P, 3 * C1], F32, "dx1", "da2_1")
        for k in range(K_TILES):
            nc.scalar.copy(dx1[:, k * C1 : (k + 1) * C1], dx_sums1[k][:])
        dx_on_vector(0, 1, dx0[:, 1], "minus_d2_1")
        dx_sums2 = [bank(number, [P, C1], "dx_sums2") for number in (7, 4)]
        second_product(quantize(2, [K + P]), [dx_sums2[k][:] for k in range(K_TILES)])
        dx_on_scalar(1, 0, dx1)
        dx_on_vector(1, 1, dx1[:, C1:], None, 0, DX_KEPT)
        dx2 = empty_plain(dx_sums2[0], "dx2")
        nc.scalar.copy(dx1[:, 2 * C1 :], dx_sums2[1][:])
        dx_on_vector(2, 0, dx2)
        dx_on_scalar(1, 1, dx1[:, C1:], None, DX_KEPT, 2 * C1)
        for k, queue in enumerate([nc.sync, nc.scalar]):
            queue.dma_start(out[k * P : (k + 1) * P, :], out_rows[k][:])
